import numpy as np, ml_dtypes
CORES = [1,5,17,21,33,37,49,53]
N = 8
BF = ml_dtypes.bfloat16
def gentries(a):
    return np.ascontiguousarray(a.reshape(8, 16, -1).transpose(0, 2, 1)).reshape(8, -1)
def gtable(e):
    e = np.asarray(e); return np.ascontiguousarray(e.reshape(8, -1, 16).transpose(0, 2, 1)).reshape(128, -1).astype(np.int32)
P, S, F, SW = 512, 4, 2, 3
V, RO = S * P, S - F
def node(rng, shape):
    return rng.integers(0, 2, shape) * V + rng.integers(0, F * P, shape)
def parts(rng):
    r = rng.integers(-1024, 1025, (N, 8, 16, F, P)); o = rng.integers(-256, 257, (N, 8, 16, S, P)); v = 0.5 + rng.random((N, 8, 16, S, P))
    m = rng.integers(0, 3, (N, 8, 16, 2 * (S - 1))); a = node(rng, (N, 8, F * P))
    return r, o, v, m, a
def lonely(rng, a):
    for q in range(N):
        for g in range(8):
            p = rng.permutation(P)[:7]
            for s in range(F):
                a[q, g, s * P + p[0]] = s * P + p[0]; a[q, g, s * P + p[1]] = s * P + p[2]; a[q, g, s * P + p[2]] = s * P + p[1]
                a[q, g, s * P + p[3]] = s * P + (p[4] if s else p[3]); a[q, g, s * P + p[4]] = s * P + p[3]
                a[q, g, s * P + p[5]] = s * P + (p[5] if s else p[6])
            a[q, g, p[6]] = p[5]
    return a
def pack(r, o, v, m, a):
    return {"r0": np.ascontiguousarray(r.reshape(N, 128, F * P)).astype(np.int32), "oc": o.reshape(N, 128, V).astype(np.float32).astype(BF), "stake": v.reshape(N, 128, V).astype(np.float32).astype(BF),
            "mu": m.reshape(N, 128, 2 * (S - 1)).astype(np.float32).astype(BF), "opp": np.stack([gtable(b) for b in a])}
def setup_inputs(rng):
    r, o, v, m, a = parts(rng)
    return pack(r, o, v, m, lonely(rng, a))
def setup_inputs_spread(rng):
    r, o, v, m, a = parts(rng)
    r = (np.exp2(4 + 6 * rng.random((N, 8, 1, F, P))) * (2 * rng.random(r.shape) - 1)).astype(np.int64)
    o = (np.exp2(8 * rng.random((N, 8, 1, S, P))) * (2 * rng.random(o.shape) - 1)).astype(np.int64)
    v = v * np.exp2(rng.integers(-1, 2, (N, 8, 1, S, P))); m = (3 * rng.random(m.shape) ** 2).astype(np.int64)
    a = rng.integers(0, 2, a.shape) * V + np.minimum((F * P * rng.random(a.shape) ** 2).astype(np.int64), F * P - 1)
    return pack(r, o, v, m, lonely(rng, a))
def setup_inputs_ends(rng):
    r, o, v, m, a = parts(rng); lo, hi = 0, V + F * P - 1
    r = np.where(rng.random(r.shape) < 0.5, -1024, 1024); o = np.where(rng.random(o.shape) < 0.5, -256, 256)
    v = np.where(rng.random(v.shape) < 0.5, 0.25, 4.0); m = 2 * rng.integers(0, 2, m.shape)
    a = np.where(rng.random(a.shape) < 0.7, np.where(rng.random(a.shape) < 0.5, lo, hi), a)
    b = np.where(rng.random((N, 8, P)) < 0.5, -1, 1); b[:, :, 0] = 1; b[:, :, P - 1] = -1
    for g in (0, 3, 5, 7):
        r[:, g] = 1024 * b[:, g, None, None, :]; o[:, g] = -256 * b[:, g, None, None, :]
        m[:, g, ::2] = 2; m[:, g, 15] = 2
        a[:, g] = np.where(rng.random((N, F * P)) < 0.8, np.tile(np.where(b[:, g] > 0, hi, lo), (1, F)), a[:, g])
    return pack(r, o, v, m, a)
def setup_inputs_corners(rng):
    r, o, v, m, a = parts(rng); own = np.arange(F * P)
    o = np.where(rng.random((N, 8, 1, S, P)) < 0.6, 256 * rng.integers(-1, 2, (N, 8, 1, S, P)), o)
    r[:, ::2] = rng.choice(np.array([-1024, -1, 0, 1, 1024]), (N, 4, 16, F, P))
    for i in range(16): m[:, 1::2, i] = i % 3
    far = np.array([0, F * P - 1, V, V + F * P - 1])
    for q in range(N):
        for g in range(8):
            k = (g + q) & 7
            if k == 0: a[q, g] = own
            if k == 1: a[q, g] = own ^ 1
            if k == 2: a[q, g] = (own + 1) % (F * P)
            if k == 3: a[q, g] = V + own
            if k == 4: a[q, g] = rng.choice(far, F * P)
            if k == 5: a[q, g, :P] = own[:P]
            if k == 6: a[q, g, :(F - 1) * P] = own[:(F - 1) * P]
            if k == 7:
                t = rng.integers(0, 5, F * P)
                a[q, g] = np.where(t == 0, own, np.where(t == 1, own ^ 1, np.where(t == 2, V + own, np.where(t == 3, rng.choice(far, F * P), a[q, g]))))
    x = int(rng.integers(0, N)); w = (x - 1) % N; mine = own.reshape(F, P)
    b = 2 * (rng.permutation(P) & 1) - 1; climb = rng.permutation(P) < P // 2
    odd = 2 * rng.permutation(P // 2)[:4] + 1; evn = 2 * rng.permutation(P // 2)[:8]; t = np.array([1, -1])
    d1, d2, low, mid, up, led = odd[:2], odd[2:], evn[:2], evn[2:4], evn[4:6], evn[6:]
    for z in (d1, d2, up, led): b[z] = t
    for z in (low, mid): b[z] = -t
    lead = np.where(climb & (np.arange(F)[:, None] > 0), -b, b); to = np.where(climb, np.arange(P), mine)
    for z in (low, mid, up): lead[:, z] = -t
    lead[:, led] = t
    to[:, up] = led; to[:, led] = mine[:, led]; to[:, mid] = d1
    to[:, low] = d2; to[0, low] = mid; to[F - 1, low] = mine[F - 1, low]
    for z in (d1, d2): to[:, z] = z; to[F - 1, z] = mine[F - 1, low]
    inner = (np.arange(F) > 0) & (np.arange(F) < F - 1)
    run = np.where(inner, -1020, 1024)[None, :, None] - 3 * (np.arange(16) & 1)[:, None, None]
    to = to.reshape(-1)
    for q in (x, w):
        r[q] = lead * (1024 - rng.integers(0, 4, r[q].shape)); o[q] = 256 * b; m[q] = 2
        r[q][..., d1] = t * run; r[q][..., d2] = t * (run - 1)
        a[q] = to if q == x else V + to
    return pack(r, o, v, m, a)
def setup_inputs_crowd(rng):
    r, o, v, m, a = parts(rng); two = rng.permutation(P)[:2]; x, y = int(two[0]), int(two[1])
    for q in range(N):
        for g in range(7):
            w = int(rng.integers(0, F * P)); one = int(rng.integers(0, F * P))
            if g == 6: w = F * P - 1
            if g in (0, 1, 6): a[q, g] = w
            if g == 2: a[q, g] = w; a[q, g, one] = V + one
            if g == 3: a[q, g] = V + w
            if g == 4: a[q, g] = V + w; a[q, g, one] = one
        a[q, 5] = np.where(rng.random(F * P) < 0.5, x, V + y); a[q, 5, x] = x
        r[q, 5, :, F - 1] = rng.integers(-50, 51, (16, P)); r[q, 5, :, 0, x] = 900; r[q, 5, :, 0, y] = 100
        if q % 2: r[q, 5, 3, 0, y] = 1020
    return pack(r, o, v, m, a)
def setup_inputs_ties(rng):
    r, o, v, m, a = parts(rng)
    b = (rng.integers(500, 1001, 16) * (2 * rng.integers(0, 2, 16) - 1))[None, None, :, None, None]
    k = rng.choice(np.array([0, 7, 8, 9, 10, 16]), (N, 8, 1, F, P)); place = np.argsort(np.argsort(rng.random(r.shape), axis=2), axis=2)
    dist = np.where(place < k, 4, 5 + rng.integers(0, 2, (N, 8, 1, F, P)))
    r = b + dist * (2 * rng.integers(0, 2, r.shape) - 1); r[:, :, :, F - 1] = b[:, :, :, 0]
    o = rng.integers(-1, 2, o.shape); m[:, :4] = 0
    a = rng.integers(0, 2, a.shape) * V + rng.integers(0, (F - 1) * P, a.shape)
    return pack(r, o, v, m, a)
def check_ranges(d):
    bad = []
    for k, lo, hi in (("r0", -1024, 1024), ("oc", -256, 256), ("mu", 0, 2), ("opp", 0, V + F * P - 1), ("stake", 0.25, 4)):
        w = np.asarray(d[k]).astype(np.float64)
        if not (np.min(w) >= lo and np.max(w) <= hi): bad.append("range of " + k)
        if k in ("oc", "mu") and np.any(w != np.floor(w)): bad.append("whole numbers of " + k)
    w = np.asarray(d["opp"]).astype(np.int64)
    if np.any((w >= F * P) & (w < V)): bad.append("opp names an empty slot")
    return bad
def both(R):
    w = R.reshape(N, 8, 16, V)
    return np.concatenate([w, np.roll(w, -1, axis=0)], axis=3)
def met(R, a):
    return np.take_along_axis(both(R), a[:, :, None, :], 3).reshape(N, 8, 16, -1, P)
def reference(r0, oc, stake, mu, opp):
    R = np.zeros((N, 8, 16, S, P), np.int64); R[:, :, :, :F] = r0.astype(np.int64).reshape(N, 8, 16, F, P)
    o = oc.astype(np.float64).reshape(N, 8, 16, S, P); v = stake.astype(np.float64).reshape(N, 8, 16, S, P)
    m = mu.astype(np.float64).reshape(N, 8, 16, 2 * (S - 1)); al, ga = m[..., :S - 1], m[..., S - 1:]
    L = np.zeros((N, 8, V), np.int64); L[:, :, :F * P] = np.stack([gentries(b) for b in opp])
    for rnd in range(RO):
        n = F + rnd
        a = L[:, :, :n * P].copy(); home = a < V
        c = np.where(home, np.take_along_axis(L, np.where(home, a, 0), 2), a)
        oneself = ((c < V) & ((c & (P - 1)) == np.tile(np.arange(P), n))).reshape(N, 8, n, P)
        me = R[:, :, :, n - 1].copy()
        dist = np.abs(met(R, c) - me[:, :, :, None, :])
        best = np.full((N, 8, 16, P), 2 ** 17, np.int64); pick = a[:, :, :P].copy(); c = c.reshape(N, 8, n, P)
        for k in range(n):
            nearer = np.add.reduce((dist[:, :, :, k] < best).astype(np.int64), axis=2)
            win = (nearer >= 9) & ~oneself[:, :, k]
            best = np.where(win[:, :, None, :], dist[:, :, :, k], best); pick = np.where(win, c[:, :, k], pick)
        L[:, :, n * P:(n + 1) * P] = np.where(pick >= V, V, 0) + (n - 1) * P + (pick & (P - 1))
        R[:, :, :, n] = (me + np.roll(me, -1, axis=1)) >> 1
        n = n + 1
        for sweep in range(SW):
            e = o[:, :, :, :n] - np.clip(R[:, :, :, :n] - met(R, L[:, :, :n * P]), -256, 256)
            d = e.copy()
            for s in range(1, n): d[:, :, :, s] += 0.5 * al[..., s - 1, None] * d[:, :, :, s - 1]
            x = np.floor(d)
            for s in range(n - 2, -1, -1): x[:, :, :, s] += 0.5 * ga[..., s, None] * x[:, :, :, s + 1]
            R[:, :, :, :n] += np.floor(0.0625 * x).astype(np.int64)
    z = (R - met(R, L)) * 2.0 ** -8
    y = np.add.reduce(v * (0.5 + 0.5 * np.tanh(0.5 * z)), axis=3)
    return {"y": y.reshape(N, 128, P).astype(np.float32), "yr": R.reshape(N, 128, V).astype(np.float32), "yo": np.stack([gtable(b) for b in L[:, :, F * P:]]).astype(np.float32)}

def check_inputs(d):
    bad = list(check_ranges(d))
    if not bad:
        for name, y in reference(**d).items():
            for q in range(N):
                v = np.abs(np.asarray(y[q], np.float64)); s = np.sqrt(np.mean(v * v))
                if v.max() > 11 * s or s < 2.0 ** 0: bad.append('%s of rank %d is uneven or too small' % (name, q))
    return bad

@@ -1,0 +1,684 @@
+import numpy as np
+from concourse.mybir import AluOpType, ActivationFunctionType
+
+CH = [(0, 128, 0), (128, 128, 1), (256, 128, 2), (384, 128, 3)]
+NCH = len(CH)
+MW = float(2 ** 23 + 4096)
+B_PRE = -(2.0 ** 23 - 4096 + 0.5)
+B_FIN = float(2 ** 23 - 4096)
+S_FIN = 1.0 + 2.0 ** -21
+M2 = float(3 * 2 ** 22)
+DELTA = -127.0 / 256.0
+
+F32, BF, I32, F16, U16 = "float32", "bfloat16", "int32", "float16", "uint16"
+SCRATCH = {
+    "W0": ("sbuf", [128, 2048], I32),
+    "W1": ("sbuf", [128, 2048], F32), "W2": ("sbuf", [128, 2048], F32),
+    "W3": ("sbuf", [128, 3072], F32), "W4": ("sbuf", [128, 3072], F32),
+    "W5": ("sbuf", [128, 3072], F32), "W6": ("sbuf", [128, 3072], F32),
+    "mf": ("sbuf", [128, 512], F32), "me": ("sbuf", [128, 512], F32),
+    "Rc": ("sbuf", [128, NCH, 512], F32),
+    "tb": ("sbuf", [128, 2048], F16), "Db": ("sbuf", [128, 1536], F16), "KF": ("sbuf", [128, 1536], F32),
+    "ocb": ("sbuf", [128, 2048], BF), "stk": ("sbuf", [128, 4, 512], BF), "mub": ("sbuf", [128, 8], BF),
+    "Lrow": ("sbuf", [128, 1024], I32), "crow": ("sbuf", [128, 1024], F16),
+    "tc": ("sbuf", [128, 2048], F32), "ds": ("sbuf", [128, 1024], F32), "lt": ("sbuf", [128, 1536], BF),
+    "prod": ("sbuf", [128, 2048], F32), "ysb": ("sbuf", [128, 512], F32), "yrb": ("sbuf", [128, 4, 512], F32),
+    "yob": ("sbuf", [128, 64], F32),
+    "Y": ("sbuf", [128, 144], I32), "Y2": ("sbuf", [128, 128], I32),
+    "Ib": ("sbuf", [128, 128], BF), "I16": ("sbuf", [128, 128], BF), "If": ("sbuf", [128, 128], F32),
+    "Sh": ("sbuf", [128, 128], F32), "Z": ("sbuf", [128, 144], BF), "DG": ("sbuf", [128, 1536], BF),
+    "dl": ("sbuf", [128, 512], BF), "CB": ("sbuf", [128, 8], F32), "pmi": ("sbuf", [128, 1], I32),
+    "zc": ("sbuf", [128, 1], F32), "AC": ("sbuf", [128, 16], F32),
+    "pw0": ("sbuf", [128, 96], I32), "pw": ("sbuf", [128, 96], I32),
+    "LV": ("sbuf", [128, 6, 32], I32), "c3": ("sbuf", [128, 6, 32], I32),
+    "x1": ("sbuf", [128, 6, 32], I32), "x2": ("sbuf", [128, 6, 32], I32), "x3": ("sbuf", [128, 6, 32], I32),
+    "x4": ("sbuf", [128, 6, 32], I32), "x5": ("sbuf", [128, 6, 32], I32), "x6": ("sbuf", [128, 6, 32], I32),
+    "x7": ("sbuf", [128, 6, 32], I32),
+    "hm": ("sbuf", [128, 96], I32), "aw": ("sbuf", [128, 64], I32), "aw2": ("sbuf", [128, 64], I32),
+    "qq": ("sbuf", [128, 128], I32), "vv": ("sbuf", [128, 96], I32), "EE": ("sbuf", [128, 96], I32),
+    "TH": ("sbuf", [128, 96], F32), "x9": ("sbuf", [128, 64], F32), "uu": ("sbuf", [128, 96], I32),
+    "BB": ("sbuf", [128, 64], I32), "DD": ("sbuf", [128, 64], I32), "s1": ("sbuf", [128, 64], I32),
+    "s2": ("sbuf", [128, 64], I32), "s3": ("sbuf", [128, 64], I32), "s4": ("sbuf", [128, 64], I32),
+    "oG": ("sbuf", [128, 64], U16), "oL0": ("sbuf", [128, 64], U16), "oC": ("sbuf", [128, 96], U16),
+    "oU0": ("sbuf", [128, 32], U16), "oN2": ("sbuf", [128, 96], U16),
+    "oN3": ("sbuf", [128, 128], U16), "oU3": ("sbuf", [128, 32], U16),
+}
+for _j in range(4):
+    SCRATCH["PR%d" % _j] = ("psum", [128, 512], F32)
+    SCRATCH["PF%d" % _j] = ("psum", [128, 512], F32)
+
+ENG = {"v": "sv", "a": "sa", "p": "sp", "g": "sg"}
+DSEM = ["d_r0a", "d_r0b", "d_opp", "d_mu", "d_lrow", "d_oc", "d_stk", "d_yr", "d_yo", "d_y0", "d_y1"]
+DSEM += ["d_c%d%d" % (_k, _j) for _k in range(1, 7) for _j in range(NCH)]
+SEMAPHORES = list(ENG.values()) + DSEM + ["arr%d" % k for k in range(7)] + ["sent"]
+RELAY = [(_k, _j) for _k in range(2, 7) for _j in ()]
+SEMAPHORES += ["h%d%d" % _p for _p in RELAY]
+
+AL = AluOpType
+AF = ActivationFunctionType
+
+
+def _cols(name, idx):
+    shape = SCRATCH[name][1][1:]
+    n = int(np.prod(shape))
+    return np.arange(n).reshape(shape)[idx[1:]].reshape(-1)
+
+
+def _emit(g, T, ops, totals):
+    queue = {"v": g.vector, "a": g.scalar, "p": g.tensor, "g": g, "s": g.sync}
+    wr, rd, bank = {}, {}, {}
+    order, know, clock, waits, need = {}, {q: {} for q in queue}, [], [], set()
+    for i, o in enumerate(ops):
+        q, key = o["q"], o["sem"] or o["q"]
+        deps = set()
+        touched = [(a, False) for a in o["r"]] + [(a, True) for a in o["w"]]
+        for (name, idx), write in touched:
+            if name not in wr:
+                n = int(np.prod(SCRATCH[name][1][1:]))
+                wr[name], rd[name], bank[name] = np.full(n, -1), {}, {}
+            cols = _cols(name, idx)
+            deps.update(int(d) for d in np.unique(wr[name][cols]))
+            if write:
+                for a in rd[name].values():
+                    deps.update(int(d) for d in np.unique(a[cols]))
+            if SCRATCH[name][0] == "psum":
+                deps.update(d for e, d in bank[name].items() if e != q)
+        for (name, idx), write in touched:
+            cols = _cols(name, idx)
+            if write:
+                wr[name][cols] = i
+                for a in rd[name].values():
+                    a[cols] = -1
+            else:
+                rd[name].setdefault(key, np.full(len(wr[name]), -1))[cols] = i
+            bank[name][q] = i
+        deps.discard(-1)
+        deps.discard(i)
+        mine = []
+        for s in o["ext"]:
+            if know[q].get(s, 0) < 1:
+                mine.append(("x", s))
+                know[q][s] = 1
+        best = {}
+        for d in deps:
+            dk = ops[d]["sem"] or ops[d]["q"]
+            if ops[d]["sem"] == "sent" or (dk == key and (q == "p" or o["sem"])):
+                continue
+            if dk not in best or d > best[dk]:
+                best[dk] = d
+        for dk, d in sorted(best.items(), key=lambda e: -e[1]):
+            if know[q].get(dk, 0) >= clock[d][dk]:
+                continue
+            mine.append(("o", d))
+            need.add(d)
+            for k2, v2 in clock[d].items():
+                if know[q].get(k2, 0) < v2:
+                    know[q][k2] = v2
+        order[key] = order.get(key, 0) + 1
+        ck = dict(know[q])
+        ck[key] = 1 if o["sem"] else order[key]
+        clock.append(ck)
+        waits.append(mine)
+    count, at = {}, {}
+    for i, o in enumerate(ops):
+        if o["sem"] in DSEM:
+            count[o["sem"]] = count.get(o["sem"], 0) + 16
+        elif not o["sem"] and i in need:
+            s = ENG[o["q"]]
+            count[s] = count.get(s, 0) + 1
+            at[i] = count[s]
+    for i, o in enumerate(ops):
+        e = queue[o["q"]]
+        for kind, d in waits[i]:
+            if kind == "x":
+                e.wait_ge(T.sem[d], totals[d])
+            elif ops[d]["sem"]:
+                e.wait_ge(T.sem[ops[d]["sem"]], count[ops[d]["sem"]])
+            else:
+                e.wait_ge(T.sem[ENG[ops[d]["q"]]], at[d])
+        ins = o["fn"](e)
+        if o["sem"] in DSEM:
+            ins.then_inc(T.sem[o["sem"]], 16)
+        elif i in at:
+            ins.then_inc(T.sem[ENG[o["q"]]], 1)
+    for s, n in list(totals.items()) + list(count.items()):
+        g.wait_ge(T.sem[s], n)
+
+
+def _helper(T, topo, rank):
+    core, dst = T.cores[rank], T.cores[(rank - 1) % len(T.cores)]
+    if topo.chip(core) == topo.chip(dst):
+        return None
+    return [c for c in topo.cores_of(core)
+            if topo.die(c) != topo.die(core) and c not in T.cores and topo.may_write(c, dst)][0]
+
+
+def _piece(T, k, j):
+    no = 2 if k < 3 else 3
+    a, n, w = CH[j][0] * no, CH[j][1] * no, T["W%d" % k]
+    return w[:, a:a + n], w[:, no * 512 + a:no * 512 + a + n]
+
+
+def _hand_on(g, core, T, topo, src, dst):
+    rid, pid, _ = topo.addr(dst)
+    n_in = len(topo.engines(src, core)) - len(topo.engines(src, dst))
+    for k, j in RELAY:
+        away = _piece(T, k, j)[1]
+        g.wait_ge(T.sem["h%d%d" % (k, j)], n_in)
+        g.remote_dma(away, away, T.sem["arr%d" % k], T.sem.sent, pid, rid, topo.mask(core, dst))
+    g.wait_ge(T.sem.sent, len(RELAY) * len(topo.engines(core, dst)))
+
+
+def rank_program(g, core, T, topo):
+    rank = T.rank_of(core)
+    nr = len(T.cores)
+    if rank is None:
+        for r in range(nr):
+            if _helper(T, topo, r) == core:
+                _hand_on(g, core, T, topo, T.cores[r], T.cores[(r - 1) % nr])
+        return
+    dst, src = T.cores[(rank - 1) % nr], T.cores[(rank + 1) % nr]
+    helper = _helper(T, topo, rank)
+    rid, pid, _ = topo.addr(dst)
+    mask_out = topo.mask(core, dst)
+    n_out, n_in = len(topo.engines(core, dst)), len(topo.engines(src, core))
+    totals = {"arr0": n_in, "sent": 0}
+    for k in range(1, 7):
+        totals["arr%d" % k] = NCH * n_in
+    ops, last = [], {}
+    ALL = slice(None)
+
+    def A(name, *idx):
+        return (name, (ALL,) + (idx if idx else (ALL,) * (len(SCRATCH[name][1]) - 1)))
+
+    def R(name, a, n, step=None):
+        return (name, (ALL, slice(a, a + n, step)))
+
+    def ap(a):
+        if isinstance(a, tuple):
+            return T[a[0]][a[1]] if len(a) == 2 else T[a[0]][a[1]].indirect(T[a[2]][a[3]])
+        return a
+
+    def rds(*xs):
+        out = []
+        for a in xs:
+            if isinstance(a, tuple):
+                out.append(a[:2])
+                if len(a) == 4:
+                    out.append(a[2:])
+        return out
+
+    def op(q, fn, r, w, sem=None, ext=()):
+        ops.append({"q": q, "fn": fn, "r": rds(*r), "w": rds(*w), "sem": sem, "ext": ext})
+        for a in rds(*r):
+            last.pop(a[0], None)
+
+    def G(win, off):
+        return A(win) + off
+
+    def ts(out, a, s1, s2, o0, o1=None):
+        if o1 is None:
+            op("v", lambda e: e.tensor_scalar(ap(out), ap(a), ap(s1), None, o0), [a, s1], [out])
+        else:
+            op("v", lambda e: e.tensor_scalar(ap(out), ap(a), ap(s1), ap(s2), o0, o1), [a, s1, s2], [out])
+
+    def tt(out, a, b, o, ext=()):
+        op("v", lambda e: e.tensor_tensor(ap(out), ap(a), ap(b), o), [a, b], [out], ext=ext)
+
+    def cp(out, a):
+        op("v", lambda e: e.tensor_copy(ap(out), ap(a)), [a], [out])
+
+    def ms(out, c):
+        op("v", lambda e: e.memset(ap(out), c), [], [out])
+
+    def act(out, a, f=AF.Identity, bias=0.0, scale=1.0):
+        op("a", lambda e: e.activation(ap(out), ap(a), f, bias=ap(bias), scale=ap(scale)), [a, bias, scale], [out])
+
+    def mm(out, l, r, start=False):
+        if start:
+            last.pop(out[0], None)
+        if out[0] in last:
+            last[out[0]][0] = False
+        flag = [True]
+        last[out[0]] = flag
+        op("p", lambda e: e.matmul(ap(out), ap(l), ap(r), start, flag[0]), [l, r], [out])
+
+    def opened(b, n):
+        mm(R(b, 0, n), A("Ib"), R("dl", 0, n), True)
+
+    def dma(q, out, a, sem, ext=()):
+        op(q, lambda e: e.dma_start(ap(out), ap(a)), [a], [out], sem=sem, ext=ext)
+
+    def send(win, a, n, half, k, j=None):
+        if helper is not None and (k, j) in RELAY:
+            hr, hp, _ = topo.addr(helper)
+            spare = topo.mask(core, helper) & ~mask_out
+            totals["sent"] += len(topo.engines(core, helper)) - n_out
+            op("g", lambda e: e.remote_dma(T[win][:, half + a:half + a + n], T[win][:, a:a + n], T.sem["h%d%d" % (k, j)],
+                                           T.sem.sent, hp, hr, spare), [R(win, a, n)], [], sem="sent")
+            return
+        totals["sent"] += n_out
+        op("g", lambda e: e.remote_dma(T[win][:, half + a:half + a + n], T[win][:, a:a + n], T.sem["arr%d" % k],
+                                       T.sem.sent, pid, rid, mask_out), [R(win, a, n)], [], sem="sent")
+
+    def dg(d):
+        return R("DG", d * 128, 128)
+
+    def own(j, a, n):
+        c = CH[j][1]
+        return A("Rc", j, slice(a * c, (a + n) * c))
+
+    def slot(s):
+        return [(A("Rc", ALL, slice(s * 128, s * 128 + 128)), 0, 512)]
+
+    def rows(name, a, b):
+        return A(name, slice(a, b), ALL)
+
+    def at(name, j, width, s, n):
+        return R(name, CH[j][0] * width + s * CH[j][1], n * CH[j][1])
+
+    def pf(j, s, n):
+        return R("PF%d" % CH[j][2], s * CH[j][1], n * CH[j][1])
+
+    def pr(j, s, n):
+        return R("PR%d" % CH[j][2], s * CH[j][1], n * CH[j][1])
+
+    def offs(name, j, width, s, n):
+        return R(name, (CH[j][0] * width + s * CH[j][1]) // 16, n * CH[j][1] // 16)
+
+    def players(j):
+        return slice(CH[j][0], CH[j][0] + CH[j][1])
+
+    def run(steps):
+        for f in steps:
+            f()
+
+    bpre, bfin, bneg, bpos, braw = [R("CB", i, 1) for i in range(5)]
+    ADG = {(1, 0): 0, (2, 1): 1, (3, 2): 2, (2, 0): 3, (3, 1): 4, (3, 0): 5}
+    CDG = {(0, 1): 6, (1, 2): 7, (2, 3): 8, (0, 2): 9, (1, 3): 10, (0, 3): 11}
+    SCALE = [0, 1, 2, 6, 7, 8, 9, 10, 11, 12, 13, 14]
+
+    dma("s", R("W0", 0, 512), T.r0[:, 0:512], "d_r0a")
+    dma("a", R("W0", 512, 512), T.r0[:, 512:1024], "d_r0b")
+    dma("s", rows("LV", 0, 2), T.opp[:], "d_opp")
+    dma("a", R("mub", 0, 6), T.mu[:], "d_mu")
+    for i in range(16):
+        dma("sa"[i % 2], ("Lrow", (slice(i, 128, 16), ALL)), T.opp[:], "d_lrow")
+    dma("s", A("ocb"), T.oc[:], "d_oc")
+    op("g", lambda e: e.iota(T.Y[:], [[-1, 144]], 128, 1), [], [A("Y")])
+    op("g", lambda e: e.iota(T.pw0[:], [[0, 3], [16, 32]], 0, 0), [], [A("pw0")])
+    send("W0", 0, 1024, 1024, 0)
+    dma("s", A("stk"), T.stake[:], "d_stk", ext=("arr0",))
+
+    ms(A("dl"), DELTA)
+    for col, c in ((bpre, B_PRE), (bfin, B_FIN), (bneg, -MW), (bpos, MW), (braw, 8191.5)):
+        ms(col, c)
+    ts(A("Ib"), R("Y", 0, 128), 128.0, None, AL.is_equal)
+    ts(A("pmi"), R("Y", 0, 1), 15, None, AL.bitwise_and)
+    ts(A("Y2"), R("Y", 0, 128), 111, None, AL.bitwise_and)
+    ts(A("I16"), R("Y", 0, 128), 128.0, 0.0625, AL.is_equal, AL.mult)
+    ts(A("zc"), A("pmi"), 113.0, None, AL.add)
+    ts(A("Sh"), A("Y2"), 0.0, 0.5, AL.is_equal, AL.mult)
+    ts(A("Z"), A("Y"), A("zc"), None, AL.is_equal)
+    ts(A("pw"), A("pw0"), A("zc"), -113.0, AL.add, AL.add)
+    kbank = ["PF0", "PF1", "PF2", "PF3", "PR2"]
+    for j in range(NCH):
+        opened(kbank[j], 3 * CH[j][1])
+    opened("PR0", 512)
+
+    def by_chunk(o, n, m, j):
+        cp(offs(o, j, n, 0, m), A("c3", slice(0, m), slice(CH[j][0] // 16, (CH[j][0] + CH[j][1]) // 16)))
+
+    def lrow_steps(a, b):
+        n = (b - a) * 32
+        return [lambda: ts(R("s1", 0, n), rows("LV", a, b), 15, None, AL.bitwise_and),
+                lambda: ts(R("s2", 0, n), rows("LV", a, b), 4, 63, AL.logical_shift_right, AL.bitwise_and),
+                lambda: ts(R("s3", 0, n), R("s1", 0, n), 64.0, None, AL.mult),
+                lambda: ts(R("hm", a * 32, n), rows("LV", a, b), 2048.0, None, AL.is_lt),
+                lambda: tt(R("s4", 0, n), R("s3", 0, n), R("s2", 0, n), AL.add),
+                lambda: cp(R("oG", 0, n), R("s4", 0, n))]
+
+    def candidates(a, b, bk, between=(), mix=()):
+        n = (b - a) * 32
+        ts(R("crow", 0, 16 * n), G("Lrow", R("oG", 0, n)), -1536.0, None, AL.add)
+        for i in range(16):
+            mm(R(bk, 0, n), R("Z", 15 - i, 128), R("crow", i, 16 * n - i, 16), i == 0)
+        run(between)
+        mix = list(mix) + [lambda: None] * 4
+        ts(R("s1", 0, n), R(bk, 0, n), 0.0625, 1536.0, AL.mult, AL.add)
+        mix[0]()
+        tt(R("s2", 0, n), R("s1", 0, n), rows("LV", a, b), AL.subtract)
+        mix[1]()
+        tt(R("s3", 0, n), R("s2", 0, n), R("hm", a * 32, n), AL.mult)
+        mix[2]()
+        tt(rows("LV", 3 + a, 3 + b), R("s3", 0, n), rows("LV", a, b), AL.add)
+        mix[3]()
+
+    def diag(d):
+        act(dg(d), A("Ib"), scale=R("AC", SCALE[d], 1))
+
+    def outcomes(j):
+        p, c, _ = CH[j]
+        for s in (1, 2, 3):
+            for t in range(s + 1):
+                mm(R(kbank[j], (s - 1) * c, c), A("Ib") if t == s else dg(ADG[(s, t)]), R("ocb", t * 512 + p, c))
+        act(at("KF", j, 3, 0, 3), R(kbank[j], 0, 3 * c))
+
+    st = lrow_steps(0, 2)
+    run(st[:3])
+    ts(R("AC", 0, 6), R("mub", 0, 6), 0.5, None, AL.mult)
+    st[4]()
+    tt(R("AC", 6, 2), R("AC", 0, 2), R("AC", 1, 2), AL.mult)
+    st[5]()
+    tt(R("AC", 8, 1), R("AC", 6, 1), R("AC", 2, 1), AL.mult)
+    for d in (0, 1, 2, 3, 4, 5):
+        diag(d)
+    cp(A("me"), R("W0", 512, 512))
+    for a, p, n in slot(1):
+        act(a, R("me", p, n))
+    outcomes(0)
+    outcomes(1)
+    candidates(0, 2, "PR3", between=[
+        st[3],
+        lambda: ts(A("aw"), rows("LV", 0, 2), 2048.0, -1024.0, AL.is_ge, AL.mult),
+        lambda: cp(slot(0)[0][0], R("W0", 0, 512)),
+        lambda: tt(rows("c3", 0, 2), A("aw"), rows("LV", 0, 2), AL.add)],
+        mix=[lambda j=j: by_chunk("oL0", 2, 2, j) for j in range(NCH)])
+    mm(A("PR0"), A("Sh"), A("me"))
+    outcomes(2)
+    act(A("mf"), A("PR0"), bias=bpos)
+    outcomes(3)
+    for a, p, n in slot(2):
+        act(a, R("mf", p, n), bias=bneg)
+    ts(A("aw2"), rows("LV", 3, 5), 2048.0, -1024.0, AL.is_ge, AL.mult)
+    ts(R("qq", 0, 64), rows("LV", 3, 5), 2559, None, AL.bitwise_and)
+    tt(R("s4", 0, 64), A("aw2"), rows("LV", 3, 5), AL.add)
+    tt(R("vv", 0, 64), R("qq", 0, 64), R("pw", 0, 64), AL.not_equal)
+    cp(R("oC", 0, 64), R("s4", 0, 64))
+    ts(R("AC", 9, 3), R("mub", 3, 3), 1.0 / 32, None, AL.mult)
+    ts(R("qq", 96, 32), rows("LV", 0, 1), 2559, None, AL.bitwise_and)
+    tt(R("AC", 12, 2), R("AC", 9, 2), R("AC", 4, 2), AL.mult)
+    tt(R("EE", 64, 32), R("qq", 96, 32), R("aw", 0, 32), AL.add)
+    tt(R("AC", 14, 1), R("AC", 12, 1), R("AC", 5, 1), AL.mult)
+
+    def named(k):
+        return 2 if k <= 3 else 3
+
+    def pre_f(k, j):
+        nn = named(k)
+        opened("PF%d" % CH[j][2], nn * CH[j][1])
+        act(pf(j, 0, nn), at("KF", j, 3, 0, nn))
+
+    def pre_r(k, j):
+        n = named(k) + 1
+        opened("PR%d" % CH[j][2], n * CH[j][1])
+        act(pr(j, 0, n), own(j, 0, n), bias=braw if k == 1 else bpre)
+
+    def oc0(j):
+        mm(pr(j, 0, 1), A("I16"), R("ocb", CH[j][0], CH[j][1]))
+
+    def c0(j):
+        mm(pr(j, 0, 1), A("I16"), at("tb", j, 4, 0, 1))
+
+    def gather(out, k, off, j, a, n):
+        tt(at(out, j, 4, a, n), G("W%d" % (k - 1), off), own(j, a, n), AL.subtract, ("arr%d" % (k - 1),))
+
+    def g_all(k, j, out="tb"):
+        n = named(k) + 1
+        gather(out, k, offs("oN2" if k <= 3 else "oN3", j, n, 0, n), j, 0, n)
+
+    def g_named(k, j):
+        gather("tb", k, offs("oL0", j, 2, 0, 2) if k == 1 else offs("oN3", j, 4, 0, 3), j, 0, named(k))
+
+    def g_new(k, j):
+        gather("tb", k, offs("oU0" if k == 1 else "oU3", j, 1, 0, 1), j, named(k), 1)
+
+    def clip(j, a, n):
+        ts(at("tb", j, 4, a, n), at("tb", j, 4, a, n), 256.0, -256.0, AL.min, AL.max)
+
+    def fwd(k, j, part="all"):
+        nn = named(k)
+        if part != "new":
+            for s in range(1, nn + 1):
+                for t in range(s):
+                    mm(pf(j, s - 1, 1), dg(ADG[(s, t)]), at("tb", j, 4, t, 1))
+        lo, hi = (nn if part == "new" else 1), (nn if part == "old" else nn + 1)
+        mm(pf(j, lo - 1, hi - lo), A("Ib"), at("tb", j, 4, lo, hi - lo))
+        if part == "old":
+            oc0(j)
+            c0(j)
+
+    def floor_d(k, j):
+        ts(at("Db", j, 3, 0, named(k)), pf(j, 0, named(k)), M2, -M2, AL.add, AL.add)
+
+    def bwd(k, j):
+        nn = named(k)
+        for s in range(nn):
+            for t in range(s + 1, nn + 1):
+                mm(pr(j, s, 1), dg(CDG[(s, t)]), at("Db", j, 3, t - 1, 1))
+        mm(pr(j, 1, nn), A("I16"), at("Db", j, 3, 0, nn))
+
+    def fin(k, j):
+        nn = named(k)
+        no = 2 if k < 3 else 3
+        w = "W%d" % k
+        act(at(w, j, no, 0, no), pr(j, 0, no), bias=bfin, scale=S_FIN)
+        send(w, CH[j][0] * no, CH[j][1] * no, no * 512, k, j)
+        dma("s", own(j, 0, nn), at(w, j, no, 0, nn), "d_c%d%d" % (k, j))
+        act(own(j, nn, 1), pr(j, nn, 1), bias=bfin, scale=S_FIN)
+
+    def prepare(k, plan):
+        for x in plan.split():
+            (pre_f if x[0] == "F" else pre_r)(k, int(x[1]))
+
+    def early(k, j):
+        if k < 6:
+            pre_f(k + 1, j)
+
+    NEXT = "R0 R1 F2 R2 F3 R3"
+
+    def sweep(k, fill=()):
+        n, fill = named(k) + 1, list(fill)
+
+        def some(m=1):
+            for _ in range(min(m, len(fill))):
+                fill.pop(0)()
+        oc0(0); oc0(1)
+        g_all(k, 0); g_all(k, 1); clip(0, 0, n); fwd(k, 0); c0(0); clip(1, 0, n); fwd(k, 1); c0(1)
+        g_all(k, 2); floor_d(k, 0); bwd(k, 0); fin(k, 0); oc0(2); oc0(3); early(k, 0)
+        clip(2, 0, n); fwd(k, 2); c0(2); floor_d(k, 1); bwd(k, 1); fin(k, 1); early(k, 1)
+        g_all(k, 3); some(); clip(3, 0, n); fwd(k, 3)
+        floor_d(k, 2); c0(3); bwd(k, 2); fin(k, 2)
+        some(2)
+        floor_d(k, 3); bwd(k, 3); fin(k, 3)
+        some(len(fill))
+
+    def sweep_end(k, fill=()):
+        nn, fill = named(k), list(fill)
+
+        def some(m=1):
+            for _ in range(min(m, len(fill))):
+                fill.pop(0)()
+        g_new(k, 0); g_new(k, 1); clip(0, nn, 1); fwd(k, 0, "new")
+        clip(1, nn, 1); fwd(k, 1, "new"); floor_d(k, 0); bwd(k, 0); fin(k, 0)
+        g_new(k, 2); floor_d(k, 1); clip(2, nn, 1); fwd(k, 2, "new"); bwd(k, 1); fin(k, 1)
+        g_new(k, 3); floor_d(k, 2); clip(3, nn, 1); fwd(k, 3, "new"); bwd(k, 2); fin(k, 2)
+        some(1); floor_d(k, 3); bwd(k, 3); fin(k, 3)
+        some(len(fill))
+
+    def counts(m):
+        for i in range(16):
+            mm(R("PR3", 0, 32 * m), R("Z", 15 - i, 128), R("lt", i, 512 * m - i, 16), i == 0)
+
+    ts(R("x9", 0, 32), R("vv", 0, 32), 9.0, None, AL.mult)
+    ts(R("x9", 32, 32), R("vv", 32, 32), -99.0, 99.0, AL.mult, AL.add)
+    tt(R("EE", 0, 64), R("qq", 0, 64), A("aw2"), AL.add)
+    for kk in range(2):
+        tt(R("tc", kk * 512, 512), G("W0", R("oC", kk * 32, 32)), A("me"), AL.subtract, ("arr0",))
+    act(A("PR1"), R("tc", 0, 512), AF.Abs)
+    act(R("ds", 0, 512), R("tc", 512, 512), AF.Abs)
+    prepare(1, "F0 R0 F1")
+    tt(R("s1", 0, 32), R("EE", 0, 32), R("EE", 64, 32), AL.subtract)
+    tt(R("TH", 0, 32), R("x9", 0, 32), R("x9", 32, 32), AL.add)
+    tt(R("s2", 0, 32), R("s1", 0, 32), R("vv", 0, 32), AL.mult)
+    g_named(1, 0)
+    tt(R("lt", 0, 512), R("ds", 0, 512), A("PR1"), AL.is_lt)
+    counts(1)
+    prepare(1, "R1 F2 R2 F3")
+    tt(R("BB", 0, 32), R("s2", 0, 32), R("EE", 64, 32), AL.add)
+    g_named(1, 1)
+    tt(R("DD", 0, 32), R("EE", 32, 32), R("BB", 0, 32), AL.subtract)
+    clip(0, 0, 2)
+    tt(R("uu", 0, 32), R("PR3", 0, 32), R("TH", 0, 32), AL.is_ge)
+    fwd(1, 0, "old")
+    pre_r(1, 3)
+    for d in (6, 7, 9):
+        diag(d)
+    clip(1, 0, 2); fwd(1, 1, "old")
+    tt(R("s1", 0, 32), R("uu", 0, 32), R("DD", 0, 32), AL.mult)
+    g_named(1, 2)
+    tt(R("s2", 0, 32), R("s1", 0, 32), R("BB", 0, 32), AL.add)
+    g_named(1, 3)
+    ts(A("oU0"), R("s2", 0, 32), 512.0, None, AL.add)
+    clip(2, 0, 2); fwd(1, 2, "old")
+    clip(3, 0, 2); fwd(1, 3, "old")
+
+    def col_steps(a, m):
+        v = rows("LV", a, m)
+        x1, x2, x3, x4 = [rows("x%d" % i, a, m) for i in range(1, 5)]
+        return [lambda: ts(x2, v, 384, None, AL.bitwise_and),
+                lambda: ts(x1, v, 511, None, AL.bitwise_and),
+                lambda: ts(x3, v, 2, 384, AL.logical_shift_right, AL.bitwise_and),
+                lambda: ts(x4, v, 1, 1024, AL.logical_shift_right, AL.bitwise_and),
+                lambda: tt(x1, x1, x2, AL.add),
+                lambda: tt(x4, x4, x3, AL.add),
+                lambda: tt(rows("c3", a, m), x1, x4, AL.add)]
+
+    sweep_end(1, [lambda: ts(R("s3", 0, 32), R("s2", 0, 32), 1024.0, 1024.0, AL.is_ge, AL.mult),
+                  lambda: ts(R("s4", 0, 32), R("s2", 0, 32), 512.0, None, AL.add),
+                  lambda: tt(rows("LV", 2, 3), R("s3", 0, 32), R("s4", 0, 32), AL.add)])
+    prepare(2, "F0 R0 F1 R1 F2 R2 F3 R3")
+    run(col_steps(0, 3))
+    for j in range(NCH):
+        by_chunk("oN2", 3, 3, j)
+    for d in (8, 10, 11):
+        diag(d)
+    st = lrow_steps(2, 3)
+    run(st[:3])
+    sweep(2, st[3:])
+    candidates(2, 3, "PF3", between=[lambda: prepare(3, "R0 R1 F2 R2"),
+                                     lambda: cp(R("yob", 0, 32), rows("LV", 2, 3))])
+    prepare(3, "F3 R3")
+    ts(R("qq", 64, 32), rows("LV", 5, 6), 2559, None, AL.bitwise_and)
+    cs = col_steps(3, 6)
+    run(cs[:3])
+    tt(R("vv", 64, 32), R("qq", 64, 32), R("pw", 64, 32), AL.not_equal)
+    run(cs[3:4])
+    sweep(3, cs[4:])
+
+    for a, p, n in slot(2):
+        act(R("me", p, n), a)
+    act(A("mf"), A("me"), bias=bpre)
+    mm(A("PR0"), A("Sh"), A("mf"), True)
+    prepare(4, "F2 F3")
+    ts(A("x5"), A("LV"), 2, 512, AL.logical_shift_right, AL.bitwise_and)
+    ts(R("x9", 32, 32), R("vv", 64, 32), -99.0, 99.0, AL.mult, AL.add)
+    tt(A("x5"), A("x5"), A("x2"), AL.add)
+    tt(A("c3"), A("c3"), A("x5"), AL.add)
+    cp(A("oC"), rows("c3", 3, 6))
+    for j in range(NCH):
+        by_chunk("oN3", 4, 3, j)
+    tt(A("x1"), A("c3"), A("x3"), AL.subtract)
+    tt(R("TH", 32, 32), R("x9", 0, 32), R("x9", 32, 32), AL.add)
+    ts(R("TH", 64, 32), R("x9", 32, 32), 9.0, None, AL.add)
+
+    def table_steps(ta, t0, t1, t2):
+        return [lambda: tt(R("s1", 0, 32), t0, ta, AL.subtract),
+                lambda: cp(R("BB", 32, 32), t1),
+                lambda: tt(R("s2", 0, 32), R("s1", 0, 32), R("vv", 0, 32), AL.mult),
+                lambda: tt(R("DD", 32, 32), t2, t1, AL.subtract),
+                lambda: tt(R("BB", 0, 32), R("s2", 0, 32), ta, AL.add),
+                lambda: tt(R("DD", 0, 32), t2, R("BB", 0, 32), AL.subtract)]
+
+    pick = [lambda: tt(A("s1"), R("uu", 32, 64), A("DD"), AL.mult),
+            lambda: tt(A("s2"), A("s1"), A("BB"), AL.add),
+            lambda: tt(R("s3", 0, 32), R("s2", 32, 32), R("s2", 0, 32), AL.subtract),
+            lambda: tt(R("s4", 0, 32), R("s3", 0, 32), R("uu", 0, 32), AL.mult),
+            lambda: tt(R("s3", 32, 32), R("s4", 0, 32), R("s2", 0, 32), AL.add)]
+    run(table_steps(rows("x1", 0, 1), rows("x1", 3, 4), rows("x1", 4, 5), rows("x1", 5, 6)))
+    for kk in range(3):
+        tt(R("tc", kk * 512, 512), G("W3", R("oC", kk * 32, 32)), A("me"), AL.subtract, ("arr3",))
+    act(A("PR1"), R("tc", 0, 512), AF.Abs)
+    act(R("ds", 0, 512), R("tc", 512, 512), AF.Abs)
+    act(R("ds", 512, 512), R("tc", 1024, 512), AF.Abs)
+    act(A("PR2"), R("tc", 512, 512), AF.Abs)
+    for a, p, n in slot(3):
+        act(a, R("PR0", p, n), bias=bfin, scale=S_FIN)
+    prepare(4, "R0")
+    tt(R("lt", 0, 512), R("ds", 0, 512), A("PR1"), AL.is_lt)
+    tt(R("lt", 512, 512), R("ds", 512, 512), A("PR1"), AL.is_lt)
+    tt(R("lt", 1024, 512), R("ds", 512, 512), A("PR2"), AL.is_lt)
+    counts(3)
+    prepare(4, "R1 R2")
+    g_named(4, 0); g_named(4, 1)
+    tt(A("uu"), R("PR3", 0, 96), A("TH"), AL.is_ge)
+    pre_r(4, 3)
+    clip(0, 0, 3); fwd(4, 0, "old")
+    pick[0]()
+    clip(1, 0, 3); fwd(4, 1, "old")
+    pick[1]()
+    g_named(4, 2)
+    pick[2]()
+    clip(2, 0, 3); fwd(4, 2, "old")
+    pick[3]()
+    g_named(4, 3)
+    pick[4]()
+    ts(A("oU3"), R("s3", 32, 32), 256.0, None, AL.add)
+    clip(3, 0, 3); fwd(4, 3, "old")
+    sweep_end(4)
+    prepare(5, "F0 R0 F1 R1 F2 R2 F3 R3")
+    for j in range(NCH):
+        cp(offs("oN3", j, 4, 3, 1), offs("oU3", j, 1, 0, 1))
+    run(table_steps(R("qq", 96, 32), R("qq", 0, 32), R("qq", 32, 32), R("qq", 64, 32)))
+    sweep(5)
+    prepare(6, NEXT)
+    run(pick)
+    ts(R("yob", 32, 32), R("s3", 32, 32), 1024.0, None, AL.add)
+    ts(A("If"), R("Y", 0, 128), 128.0, None, AL.is_equal)
+    dma("s", T.yo[:], A("yob"), "d_yo")
+    sweep(6)
+
+    for j in range(NCH):
+        if j < 3:
+            ts(A("yrb", slice(0, 3), players(j)), at("W6", j, 3, 0, 3), -MW, None, AL.add)
+        else:
+            act(A("yrb", slice(0, 3), players(j)), at("W6", j, 3, 0, 3), bias=bneg)
+    for a, p, n in slot(3):
+        act(A("yrb", 3, slice(p, p + n)), a, bias=bneg)
+    dma("s", T.yr[:], A("yrb"), "d_yr", ext=("arr6",))
+    zb = ["PR0", "PR1", "PR2", "PR3", "PF3"]
+
+    def z_of(j):
+        g_all(7, j, "tc")
+        act(R(zb[j], 0, 4 * CH[j][1]), at("tc", j, 4, 0, 4), AF.Sigmoid, scale=-1.0 / 256)
+
+    def weigh(j):
+        p, c, _ = CH[j]
+        tt(at("prod", j, 4, 0, 4), R(zb[j], 0, 4 * c), A("stk", ALL, players(j)), AL.mult)
+        if j < 3:
+            for s in range(4):
+                mm(R("PF%d" % j, 0, c), A("If"), at("prod", j, 4, s, 1), s == 0)
+            act(R("ysb", p, c), R("PF%d" % j, 0, c))
+
+    for a, n in ((0, 1), (1, 3)):
+        gather("tc", 7, offs("oN3", 0, 4, a, n), 0, a, n)
+        act(pr(0, a, n), at("tc", 0, 4, a, n), AF.Sigmoid, scale=-1.0 / 256)
+    z_of(1); z_of(2); weigh(0); z_of(3); weigh(1)
+    dma("s", T.y[:, 0:256], R("ysb", 0, 256), "d_y0")
+    weigh(2)
+    tt(pr(3, 2, 2), pr(3, 2, 2), A("stk", slice(2, 4), players(3)), AL.mult)
+    tt(at("prod", 3, 4, 0, 2), pr(3, 0, 2), A("stk", slice(0, 2), players(3)), AL.mult)
+    tt(R("ds", 0, 256), pr(3, 2, 2), at("prod", 3, 4, 0, 2), AL.add)
+    tt(R("ysb", 384, 128), R("ds", 0, 128), R("ds", 128, 128), AL.add)
+    dma("s", T.y[:, 256:512], R("ysb", 256, 256), "d_y1")
+    _emit(g, T, ops, totals)

@@ -1,58 +1,59 @@
 import numpy as np
 from concourse.mybir import AluOpType, ActivationFunctionType
 
-CH = [(0, 128, 0), (128, 128, 1), (256, 128, 2), (384, 128, 3)]
-NCH = len(CH)
-MW = float(2 ** 23 + 4096)
-B_PRE = -(2.0 ** 23 - 4096 + 0.5)
-B_FIN = float(2 ** 23 - 4096)
-S_FIN = 1.0 + 2.0 ** -21
-M2 = float(3 * 2 ** 22)
+NCH, C = 4, 128
+CW = [C] * NCH
+CP = [C * _j for _j in range(NCH)]
+H = 256
+NEW = [(0, H, "PF2"), (H, H, "PF3")]
+WRITES = {_k: [(0, 2), (2, 4)] if _k in (1, 4) else [(0, 1), (1, 2), (2, 3), (3, 4)] for _k in range(1, 7)}
+M = float(3 * 2 ** 22)
 DELTA = -127.0 / 256.0
+AWAY = 2048
+OPT = {}
 
 F32, BF, I32, F16, U16 = "float32", "bfloat16", "int32", "float16", "uint16"
 SCRATCH = {
-    "W0": ("sbuf", [128, 2048], I32),
-    "W1": ("sbuf", [128, 2048], F32), "W2": ("sbuf", [128, 2048], F32),
-    "W3": ("sbuf", [128, 3072], F32), "W4": ("sbuf", [128, 3072], F32),
-    "W5": ("sbuf", [128, 3072], F32), "W6": ("sbuf", [128, 3072], F32),
-    "mf": ("sbuf", [128, 512], F32), "me": ("sbuf", [128, 512], F32),
-    "Rc": ("sbuf", [128, NCH, 512], F32),
-    "tb": ("sbuf", [128, 2048], F16), "Db": ("sbuf", [128, 1536], F16), "KF": ("sbuf", [128, 1536], F32),
+    "W0": ("sbuf", [128, 3072], I32), "W": ("sbuf", [128, 3584], F32),
+    "me": ("sbuf", [128, 512], F16), "N": ("sbuf", [128, 6, 512], F16), "cq": ("sbuf", [128, 1024], F16),
+    "tb": ("sbuf", [128, 2048], F16), "tn": ("sbuf", [128, 4, 512], F16), "Db": ("sbuf", [128, 3, 512], F16),
+    "KF": ("sbuf", [128, 3, 512], F32),
     "ocb": ("sbuf", [128, 2048], BF), "stk": ("sbuf", [128, 4, 512], BF), "mub": ("sbuf", [128, 8], BF),
-    "Lrow": ("sbuf", [128, 1024], I32), "crow": ("sbuf", [128, 1024], F16),
+    "LQ": ("sbuf", [128, 512], I32), "LH": ("sbuf", [128, 512], F16),
+    "Lrow": ("sbuf", [128, 1024], F32), "crow": ("sbuf", [128, 1024], F16),
     "tc": ("sbuf", [128, 2048], F32), "ds": ("sbuf", [128, 1024], F32), "lt": ("sbuf", [128, 1536], BF),
     "prod": ("sbuf", [128, 2048], F32), "ysb": ("sbuf", [128, 512], F32), "yrb": ("sbuf", [128, 4, 512], F32),
     "yob": ("sbuf", [128, 64], F32),
-    "Y": ("sbuf", [128, 144], I32), "Y2": ("sbuf", [128, 128], I32),
+    "Y": ("sbuf", [128, 144], I32), "Y2": ("sbuf", [128, 128], I32), "YE": ("sbuf", [128, 256], I32),
     "Ib": ("sbuf", [128, 128], BF), "I16": ("sbuf", [128, 128], BF), "If": ("sbuf", [128, 128], F32),
-    "Sh": ("sbuf", [128, 128], F32), "Z": ("sbuf", [128, 144], BF), "DG": ("sbuf", [128, 1536], BF),
-    "dl": ("sbuf", [128, 512], BF), "CB": ("sbuf", [128, 8], F32), "pmi": ("sbuf", [128, 1], I32),
-    "zc": ("sbuf", [128, 1], F32), "AC": ("sbuf", [128, 16], F32),
-    "pw0": ("sbuf", [128, 96], I32), "pw": ("sbuf", [128, 96], I32),
-    "LV": ("sbuf", [128, 6, 32], I32), "c3": ("sbuf", [128, 6, 32], I32),
-    "x1": ("sbuf", [128, 6, 32], I32), "x2": ("sbuf", [128, 6, 32], I32), "x3": ("sbuf", [128, 6, 32], I32),
-    "x4": ("sbuf", [128, 6, 32], I32), "x5": ("sbuf", [128, 6, 32], I32), "x6": ("sbuf", [128, 6, 32], I32),
-    "x7": ("sbuf", [128, 6, 32], I32),
-    "hm": ("sbuf", [128, 96], I32), "aw": ("sbuf", [128, 64], I32), "aw2": ("sbuf", [128, 64], I32),
-    "qq": ("sbuf", [128, 128], I32), "vv": ("sbuf", [128, 96], I32), "EE": ("sbuf", [128, 96], I32),
-    "TH": ("sbuf", [128, 96], F32), "x9": ("sbuf", [128, 64], F32), "uu": ("sbuf", [128, 96], I32),
-    "BB": ("sbuf", [128, 64], I32), "DD": ("sbuf", [128, 64], I32), "s1": ("sbuf", [128, 64], I32),
-    "s2": ("sbuf", [128, 64], I32), "s3": ("sbuf", [128, 64], I32), "s4": ("sbuf", [128, 64], I32),
-    "oG": ("sbuf", [128, 64], U16), "oL0": ("sbuf", [128, 64], U16), "oC": ("sbuf", [128, 96], U16),
-    "oU0": ("sbuf", [128, 32], U16), "oN2": ("sbuf", [128, 96], U16),
-    "oN3": ("sbuf", [128, 128], U16), "oU3": ("sbuf", [128, 32], U16),
+    "Sh": ("sbuf", [128, 128], BF), "Z": ("sbuf", [128, 144], BF), "DG": ("sbuf", [128, 1536], BF),
+    "E": ("sbuf", [128, 256], BF),
+    "dl": ("sbuf", [128, 512], BF), "Mc": ("sbuf", [128, 512], BF), "CB": ("sbuf", [128, 8], F32),
+    "pmi": ("sbuf", [128, 1], I32), "zc": ("sbuf", [128, 1], F32), "AC": ("sbuf", [128, 16], F32),
+    "pw0": ("sbuf", [128, 64], I32), "pw": ("sbuf", [128, 64], I32),
+    "LV": ("sbuf", [128, 4, 32], I32), "CV": ("sbuf", [128, 3, 32], I32),
+    "hm": ("sbuf", [128, 96], F32), "base": ("sbuf", [128, 96], I32),
+    "qq": ("sbuf", [128, 128], I32), "vv": ("sbuf", [128, 96], I32),
+    "TH": ("sbuf", [128, 96], F32), "x9": ("sbuf", [128, 96], F32), "uu": ("sbuf", [128, 96], I32),
+    "BB": ("sbuf", [128, 64], I32), "DD": ("sbuf", [128, 96], I32),
+    "s1": ("sbuf", [128, 64], I32), "s2": ("sbuf", [128, 64], I32), "s3": ("sbuf", [128, 64], I32),
+    "s4": ("sbuf", [128, 64], I32), "s5": ("sbuf", [128, 64], F32),
+    "oG": ("sbuf", [128, 96], U16), "oC": ("sbuf", [128, 96], U16),
+    "oA2": ("sbuf", [128, 64], U16), "oA3": ("sbuf", [128, 96], U16),
+    "oU2": ("sbuf", [128, 32], U16), "oU3": ("sbuf", [128, 32], U16), "oY": ("sbuf", [128, 128], U16),
 }
-for _j in range(4):
+for _k in range(7):
+    SCRATCH["Q%d" % _k] = ("sbuf", [128, NCH, (2 if _k < 3 else 3) * C], F16)
+    if _k:
+        SCRATCH["L%d" % _k] = SCRATCH["Q%d" % _k]
+for _j in range(NCH):
     SCRATCH["PR%d" % _j] = ("psum", [128, 512], F32)
     SCRATCH["PF%d" % _j] = ("psum", [128, 512], F32)
 
 ENG = {"v": "sv", "a": "sa", "p": "sp", "g": "sg"}
-DSEM = ["d_r0a", "d_r0b", "d_opp", "d_mu", "d_lrow", "d_oc", "d_stk", "d_yr", "d_yo", "d_y0", "d_y1"]
-DSEM += ["d_c%d%d" % (_k, _j) for _k in range(1, 7) for _j in range(NCH)]
-SEMAPHORES = list(ENG.values()) + DSEM + ["arr%d" % k for k in range(7)] + ["sent"]
-RELAY = [(_k, _j) for _k in range(2, 7) for _j in ()]
-SEMAPHORES += ["h%d%d" % _p for _p in RELAY]
+DSEM = ["d_r0a", "d_r0b", "d_opp", "d_lq", "d_mu", "d_oc", "d_stk", "d_yr", "d_yo", "d_y0", "d_y1"]
+ARR = ["arr0"] + ["arr%d%d" % (_k, _j) for _k in range(1, 7) for _j, _ in WRITES[_k]]
+SEMAPHORES = list(ENG.values()) + DSEM + ARR + ["sent"]
 
 AL = AluOpType
 AF = ActivationFunctionType
@@ -145,46 +146,19 @@ def _emit(g, T, ops, totals):
         g.wait_ge(T.sem[s], n)
 
 
-def _helper(T, topo, rank):
-    core, dst = T.cores[rank], T.cores[(rank - 1) % len(T.cores)]
-    if topo.chip(core) == topo.chip(dst):
-        return None
-    return [c for c in topo.cores_of(core)
-            if topo.die(c) != topo.die(core) and c not in T.cores and topo.may_write(c, dst)][0]
-
-
-def _piece(T, k, j):
-    no = 2 if k < 3 else 3
-    a, n, w = CH[j][0] * no, CH[j][1] * no, T["W%d" % k]
-    return w[:, a:a + n], w[:, no * 512 + a:no * 512 + a + n]
-
-
-def _hand_on(g, core, T, topo, src, dst):
-    rid, pid, _ = topo.addr(dst)
-    n_in = len(topo.engines(src, core)) - len(topo.engines(src, dst))
-    for k, j in RELAY:
-        away = _piece(T, k, j)[1]
-        g.wait_ge(T.sem["h%d%d" % (k, j)], n_in)
-        g.remote_dma(away, away, T.sem["arr%d" % k], T.sem.sent, pid, rid, topo.mask(core, dst))
-    g.wait_ge(T.sem.sent, len(RELAY) * len(topo.engines(core, dst)))
-
-
 def rank_program(g, core, T, topo):
     rank = T.rank_of(core)
-    nr = len(T.cores)
     if rank is None:
-        for r in range(nr):
-            if _helper(T, topo, r) == core:
-                _hand_on(g, core, T, topo, T.cores[r], T.cores[(r - 1) % nr])
         return
+    nr = len(T.cores)
     dst, src = T.cores[(rank - 1) % nr], T.cores[(rank + 1) % nr]
-    helper = _helper(T, topo, rank)
     rid, pid, _ = topo.addr(dst)
     mask_out = topo.mask(core, dst)
     n_out, n_in = len(topo.engines(core, dst)), len(topo.engines(src, core))
-    totals = {"arr0": n_in, "sent": 0}
+    totals = {"arr0": 2 * n_in, "sent": 0}
     for k in range(1, 7):
-        totals["arr%d" % k] = NCH * n_in
+        for j, _ in WRITES[k]:
+            totals["arr%d%d" % (k, j)] = n_in
     ops, last = [], {}
     ALL = slice(None)
 
@@ -193,6 +167,9 @@ def rank_program(g, core, T, topo):
 
     def R(name, a, n, step=None):
         return (name, (ALL, slice(a, a + n, step)))
+
+    def R16(name, a, n):
+        return (name, (slice(0, 16), slice(a, a + n)))
 
     def ap(a):
         if isinstance(a, tuple):
@@ -213,9 +190,6 @@ def rank_program(g, core, T, topo):
         for a in rds(*r):
             last.pop(a[0], None)
 
-    def G(win, off):
-        return A(win) + off
-
     def ts(out, a, s1, s2, o0, o1=None):
         if o1 is None:
             op("v", lambda e: e.tensor_scalar(ap(out), ap(a), ap(s1), None, o0), [a, s1], [out])
@@ -225,460 +199,552 @@ def rank_program(g, core, T, topo):
     def tt(out, a, b, o, ext=()):
         op("v", lambda e: e.tensor_tensor(ap(out), ap(a), ap(b), o), [a, b], [out], ext=ext)
 
-    def cp(out, a):
-        op("v", lambda e: e.tensor_copy(ap(out), ap(a)), [a], [out])
+    def cp(out, a, ext=()):
+        op("v", lambda e: e.tensor_copy(ap(out), ap(a)), [a], [out], ext=ext)
 
     def ms(out, c):
         op("v", lambda e: e.memset(ap(out), c), [], [out])
 
-    def act(out, a, f=AF.Identity, bias=0.0, scale=1.0):
-        op("a", lambda e: e.activation(ap(out), ap(a), f, bias=ap(bias), scale=ap(scale)), [a, bias, scale], [out])
+    def act(out, a, f=AF.Identity, bias=0.0, scale=1.0, ext=()):
+        op("a", lambda e: e.activation(ap(out), ap(a), f, bias=ap(bias), scale=ap(scale)), [a, bias, scale], [out],
+           ext=ext)
 
-    def mm(out, l, r, start=False):
+    def mm(out, l, r, start=False, ext=()):
         if start:
             last.pop(out[0], None)
         if out[0] in last:
             last[out[0]][0] = False
         flag = [True]
         last[out[0]] = flag
-        op("p", lambda e: e.matmul(ap(out), ap(l), ap(r), start, flag[0]), [l, r], [out])
+        op("p", lambda e: e.matmul(ap(out), ap(l), ap(r), start, flag[0]), [l, r], [out], ext=ext)
 
     def opened(b, n):
         mm(R(b, 0, n), A("Ib"), R("dl", 0, n), True)
 
+    def rounded(b, n):
+        mm(R(b, 0, n), A("Ib"), R("Mc", 0, n))
+
     def dma(q, out, a, sem, ext=()):
         op(q, lambda e: e.dma_start(ap(out), ap(a)), [a], [out], sem=sem, ext=ext)
 
-    def send(win, a, n, half, k, j=None):
-        if helper is not None and (k, j) in RELAY:
-            hr, hp, _ = topo.addr(helper)
-            spare = topo.mask(core, helper) & ~mask_out
-            totals["sent"] += len(topo.engines(core, helper)) - n_out
-            op("g", lambda e: e.remote_dma(T[win][:, half + a:half + a + n], T[win][:, a:a + n], T.sem["h%d%d" % (k, j)],
-                                           T.sem.sent, hp, hr, spare), [R(win, a, n)], [], sem="sent")
-            return
+    def send(out, a, sem):
         totals["sent"] += n_out
-        op("g", lambda e: e.remote_dma(T[win][:, half + a:half + a + n], T[win][:, a:a + n], T.sem["arr%d" % k],
-                                       T.sem.sent, pid, rid, mask_out), [R(win, a, n)], [], sem="sent")
+        op("g", lambda e: e.remote_dma(ap(out), ap(a), T.sem[sem], T.sem.sent, pid, rid, mask_out), [a], [], sem="sent")
+
+    def iota(out, pattern, base, step, flag=False):
+        if flag:
+            op("g", lambda e: e.iota(ap(out), pattern, base, step, allow_small_or_imprecise_dtypes=True), [], [out])
+        else:
+            op("g", lambda e: e.iota(ap(out), pattern, base, step), [], [out])
 
     def dg(d):
         return R("DG", d * 128, 128)
 
-    def own(j, a, n):
-        c = CH[j][1]
-        return A("Rc", j, slice(a * c, (a + n) * c))
+    def chunk(fam, k, j, s, n):
+        return A("%s%d" % (fam, k), j, slice(s * C, (s + n) * C))
 
-    def slot(s):
-        return [(A("Rc", ALL, slice(s * 128, s * 128 + 128)), 0, 512)]
+    def part(fam, k, s, a=0, b=NCH):
+        return A("%s%d" % (fam, k), slice(a, b), slice(s * C, (s + 1) * C))
+
+    def nat(name, s, n, j):
+        return A(name, s if n == 1 else slice(s, s + n), slice(CP[j], CP[j] + CW[j]))
 
     def rows(name, a, b):
         return A(name, slice(a, b), ALL)
 
-    def at(name, j, width, s, n):
-        return R(name, CH[j][0] * width + s * CH[j][1], n * CH[j][1])
-
     def pf(j, s, n):
-        return R("PF%d" % CH[j][2], s * CH[j][1], n * CH[j][1])
+        return R("PF%d" % j, s * CW[j], n * CW[j])
 
     def pr(j, s, n):
-        return R("PR%d" % CH[j][2], s * CH[j][1], n * CH[j][1])
-
-    def offs(name, j, width, s, n):
-        return R(name, (CH[j][0] * width + s * CH[j][1]) // 16, n * CH[j][1] // 16)
-
-    def players(j):
-        return slice(CH[j][0], CH[j][0] + CH[j][1])
+        return R("PR%d" % j, s * CW[j], n * CW[j])
 
     def run(steps):
         for f in steps:
             f()
 
-    bpre, bfin, bneg, bpos, braw = [R("CB", i, 1) for i in range(5)]
+    bneg, bdel, bpos = R("CB", 0, 1), R("CB", 1, 1), R("CB", 2, 1)
     ADG = {(1, 0): 0, (2, 1): 1, (3, 2): 2, (2, 0): 3, (3, 1): 4, (3, 0): 5}
     CDG = {(0, 1): 6, (1, 2): 7, (2, 3): 8, (0, 2): 9, (1, 3): 10, (0, 3): 11}
     SCALE = [0, 1, 2, 6, 7, 8, 9, 10, 11, 12, 13, 14]
 
+    dma("s", R("W0", 512, 512), T.r0[:, 512:1024], "d_r0b")
+    dma("a", R16("LQ", 0, 512), T.opp[:], "d_lq")
+    dma("a", rows("LV", 0, 2), T.opp[:], "d_opp")
     dma("s", R("W0", 0, 512), T.r0[:, 0:512], "d_r0a")
-    dma("a", R("W0", 512, 512), T.r0[:, 512:1024], "d_r0b")
-    dma("s", rows("LV", 0, 2), T.opp[:], "d_opp")
     dma("a", R("mub", 0, 6), T.mu[:], "d_mu")
-    for i in range(16):
-        dma("sa"[i % 2], ("Lrow", (slice(i, 128, 16), ALL)), T.opp[:], "d_lrow")
     dma("s", A("ocb"), T.oc[:], "d_oc")
-    op("g", lambda e: e.iota(T.Y[:], [[-1, 144]], 128, 1), [], [A("Y")])
-    op("g", lambda e: e.iota(T.pw0[:], [[0, 3], [16, 32]], 0, 0), [], [A("pw0")])
-    send("W0", 0, 1024, 1024, 0)
+    iota(A("Y"), [[-1, 144]], 128, 1)
+    iota(R16("YE", 0, 256), [[1, 2], [2, 8], [0, 16]], 0, -1)
+    iota(A("pw0"), [[0, 2], [16, 32]], 0, 0)
+    send(R("W0", AWAY + 512, 512), R("W0", 512, 512), "arr0")
+    send(R("W0", AWAY, 512), R("W0", 0, 512), "arr0")
+    iota(R("W0", 1024, 1024), [[0, 1024]], 0, 0)
+    iota(R("W", 1024, 1024), [[0, 1024]], 0, 0, True)
     dma("s", A("stk"), T.stake[:], "d_stk", ext=("arr0",))
 
     ms(A("dl"), DELTA)
-    for col, c in ((bpre, B_PRE), (bfin, B_FIN), (bneg, -MW), (bpos, MW), (braw, 8191.5)):
-        ms(col, c)
+    ms(A("Mc"), M)
     ts(A("Ib"), R("Y", 0, 128), 128.0, None, AL.is_equal)
     ts(A("pmi"), R("Y", 0, 1), 15, None, AL.bitwise_and)
     ts(A("Y2"), R("Y", 0, 128), 111, None, AL.bitwise_and)
-    ts(A("I16"), R("Y", 0, 128), 128.0, 0.0625, AL.is_equal, AL.mult)
+    ms(bneg, -M)
+    ms(bdel, DELTA)
+    ms(bpos, M)
+    ts(R16("E", 0, 256), R16("YE", 0, 256), 0.0, None, AL.is_equal)
     ts(A("zc"), A("pmi"), 113.0, None, AL.add)
     ts(A("Sh"), A("Y2"), 0.0, 0.5, AL.is_equal, AL.mult)
     ts(A("Z"), A("Y"), A("zc"), None, AL.is_equal)
-    ts(A("pw"), A("pw0"), A("zc"), -113.0, AL.add, AL.add)
-    kbank = ["PF0", "PF1", "PF2", "PF3", "PR2"]
-    for j in range(NCH):
-        opened(kbank[j], 3 * CH[j][1])
-    opened("PR0", 512)
+    ts(A("I16"), R("Y", 0, 128), 128.0, 0.0625, AL.is_equal, AL.mult)
 
-    def by_chunk(o, n, m, j):
-        cp(offs(o, j, n, 0, m), A("c3", slice(0, m), slice(CH[j][0] // 16, (CH[j][0] + CH[j][1]) // 16)))
+    def by_chunk(m, j):
+        cp(R("oA%d" % m, m * CP[j] // 16, m * CW[j] // 16), A("LV", slice(0, m), slice(CP[j] // 16, (CP[j] + CW[j]) // 16)))
 
     def lrow_steps(a, b):
-        n = (b - a) * 32
-        return [lambda: ts(R("s1", 0, n), rows("LV", a, b), 15, None, AL.bitwise_and),
-                lambda: ts(R("s2", 0, n), rows("LV", a, b), 4, 63, AL.logical_shift_right, AL.bitwise_and),
+        n, v = (b - a) * 32, rows("LV", a, b)
+        return [lambda: ts(R("s1", 0, n), v, 15, None, AL.bitwise_and),
+                lambda: ts(R("s2", 0, n), v, 4, 63, AL.logical_shift_right, AL.bitwise_and),
                 lambda: ts(R("s3", 0, n), R("s1", 0, n), 64.0, None, AL.mult),
-                lambda: ts(R("hm", a * 32, n), rows("LV", a, b), 2048.0, None, AL.is_lt),
+                lambda: ts(R("hm", a * 32, n), v, float(AWAY), 0.0625, AL.is_lt, AL.mult),
                 lambda: tt(R("s4", 0, n), R("s3", 0, n), R("s2", 0, n), AL.add),
-                lambda: cp(R("oG", 0, n), R("s4", 0, n))]
+                lambda: ts(R("base", a * 32, n), v, 1536.0, None, AL.max),
+                lambda: cp(R("oG", a * 32, n), R("s4", 0, n))]
 
-    def candidates(a, b, bk, between=(), mix=()):
+    def to_list(a, b, bk):
         n = (b - a) * 32
-        ts(R("crow", 0, 16 * n), G("Lrow", R("oG", 0, n)), -1536.0, None, AL.add)
         for i in range(16):
             mm(R(bk, 0, n), R("Z", 15 - i, 128), R("crow", i, 16 * n - i, 16), i == 0)
-        run(between)
-        mix = list(mix) + [lambda: None] * 4
-        ts(R("s1", 0, n), R(bk, 0, n), 0.0625, 1536.0, AL.mult, AL.add)
-        mix[0]()
-        tt(R("s2", 0, n), R("s1", 0, n), rows("LV", a, b), AL.subtract)
-        mix[1]()
-        tt(R("s3", 0, n), R("s2", 0, n), R("hm", a * 32, n), AL.mult)
-        mix[2]()
-        tt(rows("LV", 3 + a, 3 + b), R("s3", 0, n), rows("LV", a, b), AL.add)
-        mix[3]()
+
+    def cand_steps(a, b, bk):
+        n = (b - a) * 32
+        return [lambda: tt(R("s5", 0, n), R(bk, 0, n), R("hm", a * 32, n), AL.mult),
+                lambda: tt(rows("CV", a, b), R("s5", 0, n), R("base", a * 32, n), AL.add),
+                lambda: cp(R("oC", a * 32, n), rows("CV", a, b)),
+                lambda: ts(R("qq", a * 32, n), rows("CV", a, b), AWAY + 511, None, AL.bitwise_and),
+                lambda: tt(R("vv", a * 32, n), R("qq", a * 32, n), R("pw", 0, n), AL.not_equal)]
 
     def diag(d):
         act(dg(d), A("Ib"), scale=R("AC", SCALE[d], 1))
 
-    def outcomes(j):
-        p, c, _ = CH[j]
-        for s in (1, 2, 3):
-            for t in range(s + 1):
-                mm(R(kbank[j], (s - 1) * c, c), A("Ib") if t == s else dg(ADG[(s, t)]), R("ocb", t * 512 + p, c))
-        act(at("KF", j, 3, 0, 3), R(kbank[j], 0, 3 * c))
+    def outcomes(s, bk):
+        for t in range(s + 1):
+            mm(A(bk), A("Ib") if t == s else dg(ADG[(s, t)]), R("ocb", t * 512, 512), t == 0)
+        return lambda: act(A("KF", s - 1, ALL), A(bk), bias=bdel)
 
-    st = lrow_steps(0, 2)
-    run(st[:3])
-    ts(R("AC", 0, 6), R("mub", 0, 6), 0.5, None, AL.mult)
-    st[4]()
-    tt(R("AC", 6, 2), R("AC", 0, 2), R("AC", 1, 2), AL.mult)
-    st[5]()
-    tt(R("AC", 8, 1), R("AC", 6, 1), R("AC", 2, 1), AL.mult)
-    for d in (0, 1, 2, 3, 4, 5):
-        diag(d)
-    cp(A("me"), R("W0", 512, 512))
-    for a, p, n in slot(1):
-        act(a, R("me", p, n))
-    outcomes(0)
-    outcomes(1)
-    candidates(0, 2, "PR3", between=[
-        st[3],
-        lambda: ts(A("aw"), rows("LV", 0, 2), 2048.0, -1024.0, AL.is_ge, AL.mult),
-        lambda: cp(slot(0)[0][0], R("W0", 0, 512)),
-        lambda: tt(rows("c3", 0, 2), A("aw"), rows("LV", 0, 2), AL.add)],
-        mix=[lambda j=j: by_chunk("oL0", 2, 2, j) for j in range(NCH)])
-    mm(A("PR0"), A("Sh"), A("me"))
-    outcomes(2)
-    act(A("mf"), A("PR0"), bias=bpos)
-    outcomes(3)
-    for a, p, n in slot(2):
-        act(a, R("mf", p, n), bias=bneg)
-    ts(A("aw2"), rows("LV", 3, 5), 2048.0, -1024.0, AL.is_ge, AL.mult)
-    ts(R("qq", 0, 64), rows("LV", 3, 5), 2559, None, AL.bitwise_and)
-    tt(R("s4", 0, 64), A("aw2"), rows("LV", 3, 5), AL.add)
-    tt(R("vv", 0, 64), R("qq", 0, 64), R("pw", 0, 64), AL.not_equal)
-    cp(R("oC", 0, 64), R("s4", 0, 64))
-    ts(R("AC", 9, 3), R("mub", 3, 3), 1.0 / 32, None, AL.mult)
-    ts(R("qq", 96, 32), rows("LV", 0, 1), 2559, None, AL.bitwise_and)
-    tt(R("AC", 12, 2), R("AC", 9, 2), R("AC", 4, 2), AL.mult)
-    tt(R("EE", 64, 32), R("qq", 96, 32), R("aw", 0, 32), AL.add)
-    tt(R("AC", 14, 1), R("AC", 12, 1), R("AC", 5, 1), AL.mult)
+    def new_rating(k, bk):
+        opened(bk, 512)
+        mm(A(bk), A("Sh"), A("me"))
+        rounded(bk, 512)
+        act(A("N", k, ALL), A(bk), bias=bneg)
 
     def named(k):
         return 2 if k <= 3 else 3
 
-    def pre_f(k, j):
-        nn = named(k)
-        opened("PF%d" % CH[j][2], nn * CH[j][1])
-        act(pf(j, 0, nn), at("KF", j, 3, 0, nn))
+    def sent(k):
+        return 2 if k < 3 else 3
 
-    def pre_r(k, j):
-        n = named(k) + 1
-        opened("PR%d" % CH[j][2], n * CH[j][1])
-        act(pr(j, 0, n), own(j, 0, n), bias=braw if k == 1 else bpre)
+    def window(k):
+        return A("W0") if k == 1 else R("W", 0, AWAY + sent(k - 1) * 512)
 
-    def oc0(j):
-        mm(pr(j, 0, 1), A("I16"), R("ocb", CH[j][0], CH[j][1]))
+    def arrived(k):
+        return ("arr0",) if k == 1 else ()
 
-    def c0(j):
-        mm(pr(j, 0, 1), A("I16"), at("tb", j, 4, 0, 1))
+    def open_f(k, j):
+        opened("PF%d" % j, named(k) * CW[j])
 
-    def gather(out, k, off, j, a, n):
-        tt(at(out, j, 4, a, n), G("W%d" % (k - 1), off), own(j, a, n), AL.subtract, ("arr%d" % (k - 1),))
+    def open_r(k, j):
+        opened("PR%d" % j, sent(k) * CW[j])
 
-    def g_all(k, j, out="tb"):
-        n = named(k) + 1
-        gather(out, k, offs("oN2" if k <= 3 else "oN3", j, n, 0, n), j, 0, n)
+    def fill_f(k, j):
+        act(pf(j, 0, named(k)), nat("KF", 0, named(k), j))
 
-    def g_named(k, j):
-        gather("tb", k, offs("oL0", j, 2, 0, 2) if k == 1 else offs("oN3", j, 4, 0, 3), j, 0, named(k))
+    def fill_r(k, j):
+        if k < 6:
+            act(pr(j, 0, named(k)), chunk("Q", k - 1, j, 0, named(k)), bias=bdel)
+        if sent(k) > named(k):
+            act(pr(j, named(k), 1), nat("N", k - 1, 1, j), bias=bdel)
 
-    def g_new(k, j):
-        gather("tb", k, offs("oU0" if k == 1 else "oU3", j, 1, 0, 1), j, named(k), 1)
+    def oc0(k, j):
+        mm(pr(j, 0, 1), A("I16"), R("ocb", CP[j], CW[j]))
 
-    def clip(j, a, n):
-        ts(at("tb", j, 4, a, n), at("tb", j, 4, a, n), 256.0, -256.0, AL.min, AL.max)
-
-    def fwd(k, j, part="all"):
-        nn = named(k)
-        if part != "new":
-            for s in range(1, nn + 1):
-                for t in range(s):
-                    mm(pf(j, s - 1, 1), dg(ADG[(s, t)]), at("tb", j, 4, t, 1))
-        lo, hi = (nn if part == "new" else 1), (nn if part == "old" else nn + 1)
-        mm(pf(j, lo - 1, hi - lo), A("Ib"), at("tb", j, 4, lo, hi - lo))
-        if part == "old":
-            oc0(j)
-            c0(j)
-
-    def floor_d(k, j):
-        ts(at("Db", j, 3, 0, named(k)), pf(j, 0, named(k)), M2, -M2, AL.add, AL.add)
-
-    def bwd(k, j):
-        nn = named(k)
-        for s in range(nn):
-            for t in range(s + 1, nn + 1):
-                mm(pr(j, s, 1), dg(CDG[(s, t)]), at("Db", j, 3, t - 1, 1))
-        mm(pr(j, 1, nn), A("I16"), at("Db", j, 3, 0, nn))
-
-    def fin(k, j):
-        nn = named(k)
-        no = 2 if k < 3 else 3
-        w = "W%d" % k
-        act(at(w, j, no, 0, no), pr(j, 0, no), bias=bfin, scale=S_FIN)
-        send(w, CH[j][0] * no, CH[j][1] * no, no * 512, k, j)
-        dma("s", own(j, 0, nn), at(w, j, no, 0, nn), "d_c%d%d" % (k, j))
-        act(own(j, nn, 1), pr(j, nn, 1), bias=bfin, scale=S_FIN)
+    def load_r(k, j):
+        open_r(k, j)
+        mm(pr(j, 0, named(k)), A("Ib"), chunk("Q", k - 1, j, 0, named(k)))
+        if sent(k) > named(k):
+            mm(pr(j, named(k), 1), A("Ib"), nat("N", k - 1, 1, j))
+        oc0(k, j)
 
     def prepare(k, plan):
         for x in plan.split():
-            (pre_f if x[0] == "F" else pre_r)(k, int(x[1]))
+            {"f": fill_f, "r": fill_r, "F": open_f, "R": open_r, "O": oc0, "L": load_r}[x[0]](k, int(x[1]))
 
-    def early(k, j):
-        if k < 6:
-            pre_f(k + 1, j)
+    def c0(j):
+        mm(pr(j, 0, 1), A("I16"), nat("tn", 0, 1, j))
 
-    NEXT = "R0 R1 F2 R2 F3 R3"
+    def tbat(j, s, n):
+        return R("tb", 4 * CP[j] + s * CW[j], n * CW[j])
 
-    def sweep(k, fill=()):
-        n, fill = named(k) + 1, list(fill)
+    def g_named(k, j, a=0, n=None):
+        nn = named(k)
+        n = nn - a if n is None else n
+        off = R("oA%d" % nn, (nn * CP[j] + a * CW[j]) // 16, n * CW[j] // 16)
+        tt(tbat(j, a, n), window(k) + off, chunk("Q", k - 1, j, a, n), AL.subtract, arrived(k))
 
-        def some(m=1):
-            for _ in range(min(m, len(fill))):
-                fill.pop(0)()
-        oc0(0); oc0(1)
-        g_all(k, 0); g_all(k, 1); clip(0, 0, n); fwd(k, 0); c0(0); clip(1, 0, n); fwd(k, 1); c0(1)
-        g_all(k, 2); floor_d(k, 0); bwd(k, 0); fin(k, 0); oc0(2); oc0(3); early(k, 0)
-        clip(2, 0, n); fwd(k, 2); c0(2); floor_d(k, 1); bwd(k, 1); fin(k, 1); early(k, 1)
-        g_all(k, 3); some(); clip(3, 0, n); fwd(k, 3)
-        floor_d(k, 2); c0(3); bwd(k, 2); fin(k, 2)
-        some(2)
-        floor_d(k, 3); bwd(k, 3); fin(k, 3)
-        some(len(fill))
+    def g_last(k, j):
+        nn = named(k)
+        tt(tbat(j, nn, 1), window(k) + R("oU%d" % nn, CP[j] // 16, CW[j] // 16), nat("N", k - 1, 1, j), AL.subtract)
 
-    def sweep_end(k, fill=()):
-        nn, fill = named(k), list(fill)
+    def clip(j, a, n):
+        ts(nat("tn", a, n, j), tbat(j, a, n), 256.0, -256.0, AL.min, AL.max)
 
-        def some(m=1):
-            for _ in range(min(m, len(fill))):
-                fill.pop(0)()
-        g_new(k, 0); g_new(k, 1); clip(0, nn, 1); fwd(k, 0, "new")
-        clip(1, nn, 1); fwd(k, 1, "new"); floor_d(k, 0); bwd(k, 0); fin(k, 0)
-        g_new(k, 2); floor_d(k, 1); clip(2, nn, 1); fwd(k, 2, "new"); bwd(k, 1); fin(k, 1)
-        g_new(k, 3); floor_d(k, 2); clip(3, nn, 1); fwd(k, 3, "new"); bwd(k, 2); fin(k, 2)
-        some(1); floor_d(k, 3); bwd(k, 3); fin(k, 3)
-        some(len(fill))
+    def fwd(k, j, lo=0, hi=None):
+        nn = named(k)
+        hi = nn + 1 if hi is None else hi
+        for t in range(lo, hi):
+            for s in range(t + 1, nn + 1):
+                mm(pf(j, s - 1, 1), dg(ADG[(s, t)]), nat("tn", t, 1, j))
+        a = max(lo, 1)
+        if hi > a:
+            mm(pf(j, a - 1, hi - a), A("Ib"), nat("tn", a, hi - a, j))
+
+    def floor_d(k, j, on="v"):
+        if on == "a":
+            rounded("PF%d" % j, named(k) * CW[j])
+            act(nat("Db", 0, named(k), j), pf(j, 0, named(k)), bias=bneg)
+        elif on == "b":
+            act(pf(j, 0, named(k)), pf(j, 0, named(k)), bias=bpos)
+            act(nat("Db", 0, named(k), j), pf(j, 0, named(k)), bias=bneg)
+        else:
+            ts(nat("Db", 0, named(k), j), pf(j, 0, named(k)), M, -M, AL.add, AL.add)
+
+    def bwd(k, j, lo=1, hi=None):
+        nn, no = named(k), sent(k)
+        hi = nn + 1 if hi is None else hi
+        for t in range(lo, hi):
+            for s in range(t):
+                mm(pr(j, s, 1), dg(CDG[(s, t)]), nat("Db", t - 1, 1, j))
+        b = min(hi, no)
+        if b > lo:
+            mm(pr(j, lo, b - lo), A("I16"), nat("Db", lo - 1, b - lo, j))
+
+    def fin(k, j, on="a"):
+        no = sent(k)
+        if on == "a":
+            rounded("PR%d" % j, no * CW[j])
+            act(chunk("Q", k, j, 0, no), pr(j, 0, no), bias=bneg)
+        else:
+            ts(chunk("Q", k, j, 0, no), pr(j, 0, no), M, -M, AL.add, AL.add)
+        for a, b in WRITES[k]:
+            if b == j + 1:
+                send(rows("L%d" % k, a, b), rows("Q%d" % k, a, b), "arr%d%d" % (k, a))
+
+    def newest(k, bk):
+        opened(bk, 512)
+        mm(A(bk), A("Ib"), A("N", k - 1, ALL))
+        mm(A(bk), A("I16"), A("Db", named(k) - 1, ALL))
+        rounded(bk, 512)
+        act(A("N", k, ALL) if k < 6 else A("yrb", 3, ALL), A(bk), bias=bneg)
+
+    def home(k, a, b, on="vvv"):
+        for s in range(sent(k)):
+            (cp if on[s] == "v" else act)(R("W", s * 512 + a * C, (b - a) * C), part("Q", k, s, a, b))
+
+    def away(k, a, b, on="vvv"):
+        ext = tuple("arr%d%d" % (k, x) for x, y in WRITES[k] if x < b and y > a)
+        for s in range(sent(k)):
+            (cp if on[s] == "v" else act)(R("W", AWAY + s * 512 + a * C, (b - a) * C), part("L", k, s, a, b), ext=ext)
+
+    def sweep(k, ahead=(), mid=(), more=()):
+        nn = named(k)
+        step = {"n": lambda j: g_named(k, j), "l": lambda j: g_last(k, j),
+                "g": lambda j: (g_named(k, j), g_last(k, j)),
+                "c": lambda j: (clip(j, 0, nn + 1), fwd(k, j), c0(j)),
+                "x": lambda j: (clip(j, 0, nn), fwd(k, j, 0, nn), c0(j)),
+                "y": lambda j: (clip(j, nn, 1), fwd(k, j, nn)),
+                "f": lambda j: floor_d(k, j), "F": lambda j: floor_d(k, j, "b"), "M": lambda j: floor_d(k, j, "a"),
+                "b": lambda j: bwd(k, j), "o": lambda j: fin(k, j), "v": lambda j: fin(k, j, "v"),
+                "O": lambda j: oc0(k, j), "m": lambda j: run(mid), "p": lambda j: run(more)}
+        run(ahead)
+        for x in OPT.get("s%d" % k, ORDER[k]).split():
+            step[x[0]](int(x[1]))
+
+    ORDER = {2: "g0 c0 m0 g1 c1 f0 b0 o0 p0 g2 c2 f1 b1 o1 O3 g3 c3 f2 b2 o2 f3 b3 o3",
+             3: "g0 c0 F0 g1 c1 F1 b0 o0 g2 c2 F2 b1 g3 c3 v1 b2 f3 b3 v2 o3",
+             5: "g0 c0 F0 g1 c1 F1 b0 o0 O2 g2 c2 F2 b1 O3 g3 c3 v1 b2 f3 b3 v2 o3"}
+    ORDER[6] = ORDER[5]
+
+    def between(k, first, plan):
+        prepare(k + 1, "F0 f0")
+        newest(k, "PF3")
+        prepare(k + 1, plan)
+        update(k, first)
+
+    def update(k, first, on="vav"):
+        h = OPT.get("h", "vvv vva vvv").split()
+        home(k, 0, 2, h[0])
+        run(first)
+        home(k, 2, 4, h[1])
+        away(k, 0, 2, h[2])
+        for a, b in WRITES[k][-2:]:
+            if a >= 2:
+                away(k, a, b, on)
 
     def counts(m):
         for i in range(16):
             mm(R("PR3", 0, 32 * m), R("Z", 15 - i, 128), R("lt", i, 512 * m - i, 16), i == 0)
 
+    def open_first(k):
+        for s in range(1, named(k)):
+            opened("PF%d" % (s - 1), 512)
+        for a, n, bk in NEW:
+            opened(bk, n)
+
+    def halves(name, h):
+        return A(name, slice(0, 2), slice(h * H, h * H + H))
+
+    def old_fwd(k, j):
+        nn = named(k)
+        a, n, bk = NEW[j // 2]
+        clip(j, 0, nn)
+        for s in range(1, nn):
+            to = R("PF0", j * C, C) if k == 1 else R("PF%d" % (j // 2), (s - 1) * H + j % 2 * C, C)
+            for t in range(s + 1):
+                mm(to, A("Ib") if t == s else dg(ADG[(s, t)]), nat("tn", t, 1, j))
+        for t in range(nn):
+            mm(R(bk, CP[j] - a, CW[j]), dg(ADG[(nn, t)]), nat("tn", t, 1, j))
+
+    def load_first(s, pieces):
+        for a, n, bk in pieces:
+            for t in range(s + 1):
+                mm(R(bk, 0, n), A("Ib") if t == s else dg(ADG[(s, t)]), R("ocb", t * 512 + a, n))
+
+    def old_floor(k, h):
+        rounded("PF%d" % h, 512)
+        act(A("Db", 0, ALL) if k == 1 else halves("Db", h), A("PF%d" % h), bias=bneg)
+
+    def old_bwd(k, j):
+        c0(j)
+        bwd(k, j, 1, named(k))
+
+    def new_gather(k, h):
+        nn, (a, n, bk) = named(k), NEW[h]
+        t = R("tb", 2048 - 512 + a, n)
+        tt(t, window(k) + R("oU%d" % nn, a // 16, n // 16), A("N", k - 1, slice(a, a + n)), AL.subtract)
+
+    def new_fwd(k, h):
+        nn, (a, n, bk) = named(k), NEW[h]
+        ts(A("tn", nn, slice(a, a + n)), R("tb", 2048 - 512 + a, n), 256.0, -256.0, AL.min, AL.max)
+        mm(R(bk, 0, n), A("Ib"), A("tn", nn, slice(a, a + n)))
+
+    def new_floor(k, h):
+        nn, (a, n, bk) = named(k), NEW[h]
+        ts(A("Db", nn - 1, slice(a, a + n)), R(bk, 0, n), M, -M, AL.add, AL.add)
+
+    def first_end(k):
+        on = OPT.get("e%d" % k, "avva")
+        new_gather(k, 0); new_fwd(k, 0)
+        if k == 1:
+            old_bwd(k, 0); old_bwd(k, 1)
+        else:
+            old_bwd(k, 2)
+        new_gather(k, 1); new_floor(k, 0); new_fwd(k, 1)
+        bwd(k, 0, named(k)); fin(k, 0, on[0])
+        new_floor(k, 1)
+        bwd(k, 1, named(k)); fin(k, 1, on[1])
+        if k == 1:
+            old_bwd(k, 2)
+        bwd(k, 2, named(k)); fin(k, 2, on[2])
+        oc0(k, 3); old_bwd(k, 3); bwd(k, 3, named(k)); fin(k, 3, on[3])
+
+    def far(k, c, bk):
+        act(R("cq", c * 512, 512), window(k) + R("oC", c * 32, 32), scale=-1.0, ext=arrived(k))
+        mm(A(bk), A("Ib"), R("cq", c * 512, 512))
+
+    st = lrow_steps(0, 2)
+    ts(R16("LH", 0, 512), R16("LQ", 0, 512), -1536.0, None, AL.add)
+    for h in range(2):
+        mm(A("PF%d" % h), R16("E", h * 128, 128), R16("LH", 0, 512), True)
+    act(R("Lrow", 0, 512), A("PF0"))
+    run(st[:3])
+    ts(A("pw"), A("pw0"), A("zc"), -113.0, AL.add, AL.add)
+    st[4]()
+    cp(R("Lrow", 512, 512), A("PF1"))
+    st[6]()
+    ts(R("AC", 0, 6), R("mub", 0, 6), 0.5, None, AL.mult)
+    act(R("crow", 512, 512), A("Lrow") + R("oG", 32, 32))
+    cp(R("crow", 0, 512), A("Lrow") + R("oG", 0, 32))
+    tt(R("AC", 6, 2), R("AC", 0, 2), R("AC", 1, 2), AL.mult)
+    to_list(0, 2, "PR3")
+    cp(A("me"), R("W0", 512, 512))
+    for d in (0, 1, 3):
+        diag(d)
+    st[3]()
+    st[5]()
+    cs = cand_steps(0, 2, "PR3")
+    cs[0]()
+    ts(R("AC", 9, 3), R("mub", 3, 3), 1.0 / 32, None, AL.mult)
+    cs[1]()
+    ts(R("qq", 96, 32), rows("LV", 0, 1), AWAY + 511, None, AL.bitwise_and)
+    cs[2]()
+    cs[3]()
+    tt(R("AC", 12, 2), R("AC", 9, 2), R("AC", 4, 2), AL.mult)
+    cs[4]()
+    new_rating(0, "PR2")
+    cp(part("Q", 0, 0), R("W0", 0, 512))
+    cp(part("Q", 0, 1), A("me"))
+    outcomes(1, "PR0")()
+    outcomes(2, "PR1")()
+    mm(A("PF1"), A("Ib"), A("me"), True)
+    open_first(1)
+    load_first(1, [(0, 512, "PF0")])
+    load_first(2, NEW)
+    prepare(1, "L2 L0")
+    for j in range(NCH):
+        by_chunk(2, j)
+    tt(R("s1", 0, 32), R("qq", 0, 32), R("qq", 96, 32), AL.subtract)
     ts(R("x9", 0, 32), R("vv", 0, 32), 9.0, None, AL.mult)
-    ts(R("x9", 32, 32), R("vv", 32, 32), -99.0, 99.0, AL.mult, AL.add)
-    tt(R("EE", 0, 64), R("qq", 0, 64), A("aw2"), AL.add)
-    for kk in range(2):
-        tt(R("tc", kk * 512, 512), G("W0", R("oC", kk * 32, 32)), A("me"), AL.subtract, ("arr0",))
-    act(A("PR1"), R("tc", 0, 512), AF.Abs)
-    act(R("ds", 0, 512), R("tc", 512, 512), AF.Abs)
-    prepare(1, "F0 R0 F1")
-    tt(R("s1", 0, 32), R("EE", 0, 32), R("EE", 64, 32), AL.subtract)
-    tt(R("TH", 0, 32), R("x9", 0, 32), R("x9", 32, 32), AL.add)
     tt(R("s2", 0, 32), R("s1", 0, 32), R("vv", 0, 32), AL.mult)
-    g_named(1, 0)
-    tt(R("lt", 0, 512), R("ds", 0, 512), A("PR1"), AL.is_lt)
-    counts(1)
-    prepare(1, "R1 F2 R2 F3")
-    tt(R("BB", 0, 32), R("s2", 0, 32), R("EE", 64, 32), AL.add)
-    g_named(1, 1)
-    tt(R("DD", 0, 32), R("EE", 32, 32), R("BB", 0, 32), AL.subtract)
-    clip(0, 0, 2)
-    tt(R("uu", 0, 32), R("PR3", 0, 32), R("TH", 0, 32), AL.is_ge)
-    fwd(1, 0, "old")
-    pre_r(1, 3)
+    ts(R("x9", 32, 32), R("vv", 32, 32), -99.0, 99.0, AL.mult, AL.add)
+    tt(R("BB", 0, 32), R("s2", 0, 32), R("qq", 96, 32), AL.add)
+    tt(R("TH", 0, 32), R("x9", 0, 32), R("x9", 32, 32), AL.add)
+    tt(R("DD", 64, 32), R("qq", 32, 32), R("BB", 0, 32), AL.subtract)
+    tt(R("AC", 8, 1), R("AC", 6, 1), R("AC", 2, 1), AL.mult)
+    tt(R("AC", 14, 1), R("AC", 12, 1), R("AC", 5, 1), AL.mult)
+
+    far(1, 0, "PF1")
+    tt(R("tc", 512, 512), A("W0") + R("oC", 32, 32), A("me"), AL.subtract, ("arr0",))
+    act(R("ds", 0, 512), R("tc", 512, 512), AF.Abs)
+    act(A("PF1"), A("PF1"), AF.Abs)
+    prepare(1, "L1")
     for d in (6, 7, 9):
         diag(d)
-    clip(1, 0, 2); fwd(1, 1, "old")
-    tt(R("s1", 0, 32), R("uu", 0, 32), R("DD", 0, 32), AL.mult)
-    g_named(1, 2)
+    g_named(1, 0); g_named(1, 1); old_fwd(1, 0); old_fwd(1, 1)
+    tt(R("lt", 0, 512), R("ds", 0, 512), A("PF1"), AL.is_lt)
+    counts(1)
+    g_named(1, 2); g_named(1, 3)
+    tt(R("uu", 0, 32), R("PR3", 0, 32), R("TH", 0, 32), AL.is_ge)
+    old_fwd(1, 2)
+    tt(R("s1", 0, 32), R("uu", 0, 32), R("DD", 64, 32), AL.mult)
+    old_fwd(1, 3)
     tt(R("s2", 0, 32), R("s1", 0, 32), R("BB", 0, 32), AL.add)
-    g_named(1, 3)
-    ts(A("oU0"), R("s2", 0, 32), 512.0, None, AL.add)
-    clip(2, 0, 2); fwd(1, 2, "old")
-    clip(3, 0, 2); fwd(1, 3, "old")
-
-    def col_steps(a, m):
-        v = rows("LV", a, m)
-        x1, x2, x3, x4 = [rows("x%d" % i, a, m) for i in range(1, 5)]
-        return [lambda: ts(x2, v, 384, None, AL.bitwise_and),
-                lambda: ts(x1, v, 511, None, AL.bitwise_and),
-                lambda: ts(x3, v, 2, 384, AL.logical_shift_right, AL.bitwise_and),
-                lambda: ts(x4, v, 1, 1024, AL.logical_shift_right, AL.bitwise_and),
-                lambda: tt(x1, x1, x2, AL.add),
-                lambda: tt(x4, x4, x3, AL.add),
-                lambda: tt(rows("c3", a, m), x1, x4, AL.add)]
-
-    sweep_end(1, [lambda: ts(R("s3", 0, 32), R("s2", 0, 32), 1024.0, 1024.0, AL.is_ge, AL.mult),
-                  lambda: ts(R("s4", 0, 32), R("s2", 0, 32), 512.0, None, AL.add),
-                  lambda: tt(rows("LV", 2, 3), R("s3", 0, 32), R("s4", 0, 32), AL.add)])
-    prepare(2, "F0 R0 F1 R1 F2 R2 F3 R3")
-    run(col_steps(0, 3))
-    for j in range(NCH):
-        by_chunk("oN2", 3, 3, j)
-    for d in (8, 10, 11):
+    old_floor(1, 0)
+    prepare(1, "R3 r3")
+    for d in (2, 4, 5):
         diag(d)
-    st = lrow_steps(2, 3)
-    run(st[:3])
-    sweep(2, st[3:])
-    candidates(2, 3, "PF3", between=[lambda: prepare(3, "R0 R1 F2 R2"),
-                                     lambda: cp(R("yob", 0, 32), rows("LV", 2, 3))])
-    prepare(3, "F3 R3")
-    ts(R("qq", 64, 32), rows("LV", 5, 6), 2559, None, AL.bitwise_and)
-    cs = col_steps(3, 6)
-    run(cs[:3])
-    tt(R("vv", 64, 32), R("qq", 64, 32), R("pw", 64, 32), AL.not_equal)
-    run(cs[3:4])
-    sweep(3, cs[4:])
+    ts(A("oU2"), R("s2", 0, 32), 512.0, None, AL.add)
+    first_end(1)
+    between(1, [lambda: ts(rows("LV", 2, 3), R("s2", 0, 32), 512.0, None, AL.add)] + lrow_steps(2, 3),
+            "R0 r0 F1 f1 L1 F2 L2 O0")
+    cs = cand_steps(2, 3, "PR3")
+    sweep(2, [lambda: act(R("crow", 0, 512), A("Lrow") + R("oG", 64, 32)), lambda: prepare(2, "f2"),
+              lambda: outcomes(3, "PF3")()],
+          [lambda: to_list(2, 3, "PR3"), lambda: prepare(2, "F3 f3")], [cs[0], lambda: prepare(2, "R3 r3")])
+    between(2, cs[1:] + [lambda j=j: by_chunk(3, j) for j in range(NCH)]
+            + [lambda: ts(R("x9", 64, 32), R("vv", 64, 32), -99.0, 99.0, AL.mult, AL.add),
+               lambda: cp(R("BB", 32, 32), R("qq", 32, 32)),
+               lambda: tt(R("DD", 0, 32), R("qq", 64, 32), R("BB", 0, 32), AL.subtract)],
+            "F1 f1 F2 F3 L0 L1 L2 L3")
+    sweep(3, [lambda: prepare(3, "f2 f3")] + [lambda d=d: diag(d) for d in (8, 10, 11)])
 
-    for a, p, n in slot(2):
-        act(R("me", p, n), a)
-    act(A("mf"), A("me"), bias=bpre)
-    mm(A("PR0"), A("Sh"), A("mf"), True)
-    prepare(4, "F2 F3")
-    ts(A("x5"), A("LV"), 2, 512, AL.logical_shift_right, AL.bitwise_and)
-    ts(R("x9", 32, 32), R("vv", 64, 32), -99.0, 99.0, AL.mult, AL.add)
-    tt(A("x5"), A("x5"), A("x2"), AL.add)
-    tt(A("c3"), A("c3"), A("x5"), AL.add)
-    cp(A("oC"), rows("c3", 3, 6))
-    for j in range(NCH):
-        by_chunk("oN3", 4, 3, j)
-    tt(A("x1"), A("c3"), A("x3"), AL.subtract)
-    tt(R("TH", 32, 32), R("x9", 0, 32), R("x9", 32, 32), AL.add)
-    ts(R("TH", 64, 32), R("x9", 32, 32), 9.0, None, AL.add)
-
-    def table_steps(ta, t0, t1, t2):
-        return [lambda: tt(R("s1", 0, 32), t0, ta, AL.subtract),
-                lambda: cp(R("BB", 32, 32), t1),
-                lambda: tt(R("s2", 0, 32), R("s1", 0, 32), R("vv", 0, 32), AL.mult),
-                lambda: tt(R("DD", 32, 32), t2, t1, AL.subtract),
-                lambda: tt(R("BB", 0, 32), R("s2", 0, 32), ta, AL.add),
-                lambda: tt(R("DD", 0, 32), t2, R("BB", 0, 32), AL.subtract)]
-
-    pick = [lambda: tt(A("s1"), R("uu", 32, 64), A("DD"), AL.mult),
+    open_first(4)
+    act(A("me"), part("Q", 3, 2))
+    for h in range(2):
+        act(A("PF%d" % h), halves("KF", h))
+    new_rating(3, "PR2")
+    mm(A("PR0"), A("Ib"), A("me"), True)
+    mm(A("PR1"), A("Ib"), A("me"), True)
+    load_first(3, NEW)
+    prepare(4, "L2")
+    update(3, [lambda: tt(R("TH", 32, 32), R("x9", 0, 32), R("x9", 64, 32), AL.add),
+               lambda: tt(R("DD", 32, 32), R("qq", 64, 32), R("qq", 32, 32), AL.subtract),
+               lambda: ts(R("TH", 64, 32), R("x9", 64, 32), 9.0, None, AL.add)])
+    pick = [lambda: tt(A("s1"), R("uu", 32, 64), R("DD", 0, 64), AL.mult),
             lambda: tt(A("s2"), A("s1"), A("BB"), AL.add),
             lambda: tt(R("s3", 0, 32), R("s2", 32, 32), R("s2", 0, 32), AL.subtract),
             lambda: tt(R("s4", 0, 32), R("s3", 0, 32), R("uu", 0, 32), AL.mult),
             lambda: tt(R("s3", 32, 32), R("s4", 0, 32), R("s2", 0, 32), AL.add)]
-    run(table_steps(rows("x1", 0, 1), rows("x1", 3, 4), rows("x1", 4, 5), rows("x1", 5, 6)))
-    for kk in range(3):
-        tt(R("tc", kk * 512, 512), G("W3", R("oC", kk * 32, 32)), A("me"), AL.subtract, ("arr3",))
-    act(A("PR1"), R("tc", 0, 512), AF.Abs)
-    act(R("ds", 0, 512), R("tc", 512, 512), AF.Abs)
+    far(4, 0, "PR0")
+    far(4, 1, "PR1")
+    tt(R("tc", 1024, 512), window(4) + R("oC", 64, 32), A("me"), AL.subtract)
     act(R("ds", 512, 512), R("tc", 1024, 512), AF.Abs)
-    act(A("PR2"), R("tc", 512, 512), AF.Abs)
-    for a, p, n in slot(3):
-        act(a, R("PR0", p, n), bias=bfin, scale=S_FIN)
-    prepare(4, "R0")
-    tt(R("lt", 0, 512), R("ds", 0, 512), A("PR1"), AL.is_lt)
-    tt(R("lt", 512, 512), R("ds", 512, 512), A("PR1"), AL.is_lt)
-    tt(R("lt", 1024, 512), R("ds", 512, 512), A("PR2"), AL.is_lt)
+    act(A("PR0"), A("PR0"), AF.Abs)
+    act(R("ds", 0, 512), A("PR1"), AF.Abs)
+    act(A("PR1"), R("ds", 0, 512))
+    g_named(4, 0); g_named(4, 1); old_fwd(4, 0); old_fwd(4, 1)
+    old_floor(4, 0)
+    tt(R("lt", 512, 512), R("ds", 512, 512), A("PR0"), AL.is_lt)
+    tt(R("lt", 0, 512), R("ds", 0, 512), A("PR0"), AL.is_lt)
+    prepare(4, "R0 r0")
+    tt(R("lt", 1024, 512), R("ds", 512, 512), A("PR1"), AL.is_lt)
     counts(3)
-    prepare(4, "R1 R2")
-    g_named(4, 0); g_named(4, 1)
+    prepare(4, "R1 r1 O0")
+    old_bwd(4, 0)
+    g_named(4, 2); g_named(4, 3)
     tt(A("uu"), R("PR3", 0, 96), A("TH"), AL.is_ge)
-    pre_r(4, 3)
-    clip(0, 0, 3); fwd(4, 0, "old")
+    old_fwd(4, 2)
     pick[0]()
-    clip(1, 0, 3); fwd(4, 1, "old")
-    pick[1]()
-    g_named(4, 2)
-    pick[2]()
-    clip(2, 0, 3); fwd(4, 2, "old")
-    pick[3]()
-    g_named(4, 3)
-    pick[4]()
-    ts(A("oU3"), R("s3", 32, 32), 256.0, None, AL.add)
-    clip(3, 0, 3); fwd(4, 3, "old")
-    sweep_end(4)
-    prepare(5, "F0 R0 F1 R1 F2 R2 F3 R3")
-    for j in range(NCH):
-        cp(offs("oN3", j, 4, 3, 1), offs("oU3", j, 1, 0, 1))
-    run(table_steps(R("qq", 96, 32), R("qq", 0, 32), R("qq", 32, 32), R("qq", 64, 32)))
-    sweep(5)
-    prepare(6, NEXT)
-    run(pick)
-    ts(R("yob", 32, 32), R("s3", 32, 32), 1024.0, None, AL.add)
-    ts(A("If"), R("Y", 0, 128), 128.0, None, AL.is_equal)
-    dma("s", T.yo[:], A("yob"), "d_yo")
-    sweep(6)
+    old_fwd(4, 3)
+    old_floor(4, 1)
+    prepare(4, "R3 r3 O1")
+    old_bwd(4, 1)
+    run(pick[1:])
+    ts(A("oU3"), R("s3", 32, 32), 1024.0, None, AL.add)
+    first_end(4)
+    plan = "R0 r0 F1 f1 R1 r1 F2 R2 F3 R3 O0 O1"
+    between(4, [lambda: ts(rows("LV", 3, 4), R("s3", 32, 32), 1024.0, None, AL.add)], plan)
+    sweep(5, [lambda: prepare(5, "f2 r2 f3 r3")])
+    between(5, [lambda: cp(A("oY"), A("LV")), lambda: cp(A("yob"), rows("LV", 2, 4)),
+                lambda: dma("s", T.yo[:], A("yob"), "d_yo"),
+                lambda: ts(A("If"), R("Y", 0, 128), 128.0, None, AL.is_equal)], plan)
+    sweep(6, [lambda: prepare(6, "f2 f3")])
 
-    for j in range(NCH):
-        if j < 3:
-            ts(A("yrb", slice(0, 3), players(j)), at("W6", j, 3, 0, 3), -MW, None, AL.add)
+    for s in range(3):
+        mm(A("PF%d" % s), A("Ib"), part("Q", 5, s), True)
+        mm(A("PF%d" % s), A("Ib"), part("Q", 6, s))
+    for s, t in ((0, 1), (2, 0), (1, 2)):
+        act(A("yrb", s, ALL), A("PF%d" % s))
+        cp(R("W", t * 512, 512), A("PF%d" % t))
+
+    def landed(bk, s, a, b, on):
+        n = (b - a) * C
+        mm(R(bk, 0, n), A("Ib"), part("L", 5, s, a, b), True)
+        mm(R(bk, 0, n), A("Ib"), part("L", 6, s, a, b), ext=tuple("arr6%d" % j for j in range(a, b)))
+        on(R("W", AWAY + s * 512 + a * C, n), R(bk, 0, n))
+
+    for s in range(3):
+        landed("PR%d" % s, s, 0, 2, act if s == 1 else cp)
+    for s in range(3):
+        landed("PF%d" % s, s, 2, 3, act)
+    for s in range(3):
+        if s < 2:
+            tt(R("W", AWAY + s * 512 + 3 * C, C), chunk("L", 5, 3, s, 1), chunk("L", 6, 3, s, 1), AL.add, ("arr63",))
         else:
-            act(A("yrb", slice(0, 3), players(j)), at("W6", j, 3, 0, 3), bias=bneg)
-    for a, p, n in slot(3):
-        act(A("yrb", 3, slice(p, p + n)), a, bias=bneg)
-    dma("s", T.yr[:], A("yrb"), "d_yr", ext=("arr6",))
-    zb = ["PR0", "PR1", "PR2", "PR3", "PF3"]
+            landed("PR3", s, 3, 4, act)
+    newest(6, "PF3")
+    dma("s", T.yr[:], A("yrb"), "d_yr", ext=("arr63",))
 
-    def z_of(j):
-        g_all(7, j, "tc")
-        act(R(zb[j], 0, 4 * CH[j][1]), at("tc", j, 4, 0, 4), AF.Sigmoid, scale=-1.0 / 256)
+    def z_of(h, s):
+        a = h * H
+        tt(R("tc", (4 * h + s) * H, H), window(7) + R("oY", s * 32 + a // 16, H // 16), A("yrb", s, slice(a, a + H)),
+           AL.subtract)
+        if s % 2:
+            act(A("PR%d" % (2 * h + s // 2)), R("tc", (4 * h + s - 1) * H, 2 * H), AF.Sigmoid, scale=-1.0 / 256)
 
-    def weigh(j):
-        p, c, _ = CH[j]
-        tt(at("prod", j, 4, 0, 4), R(zb[j], 0, 4 * c), A("stk", ALL, players(j)), AL.mult)
-        if j < 3:
-            for s in range(4):
-                mm(R("PF%d" % j, 0, c), A("If"), at("prod", j, 4, s, 1), s == 0)
-            act(R("ysb", p, c), R("PF%d" % j, 0, c))
+    def weigh(out, h, s):
+        tt(out, A("PR%d" % (2 * h + s // 2)), A("stk", slice(s, s + 2), slice(h * H, h * H + H)), AL.mult)
 
-    for a, n in ((0, 1), (1, 3)):
-        gather("tc", 7, offs("oN3", 0, 4, a, n), 0, a, n)
-        act(pr(0, a, n), at("tc", 0, 4, a, n), AF.Sigmoid, scale=-1.0 / 256)
-    z_of(1); z_of(2); weigh(0); z_of(3); weigh(1)
-    dma("s", T.y[:, 0:256], R("ysb", 0, 256), "d_y0")
-    weigh(2)
-    tt(pr(3, 2, 2), pr(3, 2, 2), A("stk", slice(2, 4), players(3)), AL.mult)
-    tt(at("prod", 3, 4, 0, 2), pr(3, 0, 2), A("stk", slice(0, 2), players(3)), AL.mult)
-    tt(R("ds", 0, 256), pr(3, 2, 2), at("prod", 3, 4, 0, 2), AL.add)
-    tt(R("ysb", 384, 128), R("ds", 0, 128), R("ds", 128, 128), AL.add)
-    dma("s", T.y[:, 256:512], R("ysb", 256, 256), "d_y1")
+    for h in range(2):
+        for s in range(4):
+            z_of(h, s)
+    for s in (0, 2):
+        weigh(R("prod", s * H, 2 * H), 0, s)
+        mm(R("PF0", 0, H), A("If"), R("prod", s * H, H), s == 0)
+        mm(R("PF0", 0, H), A("If"), R("prod", (s + 1) * H, H))
+    act(R("ysb", 0, H), R("PF0", 0, H))
+    dma("a", T.y[:, 0:H], R("ysb", 0, H), "d_y0")
+    weigh(R("prod", 4 * H, 2 * H), 1, 0)
+    weigh(A("PR3"), 1, 2)
+    tt(R("ds", 0, H), R("PR3", 0, H), R("prod", 4 * H, H), AL.add)
+    tt(R("PR3", H, H), R("PR3", H, H), R("prod", 5 * H, H), AL.add)
+    tt(R("ysb", H, H), R("PR3", H, H), R("ds", 0, H), AL.add)
+    dma("s", T.y[:, H:512], R("ysb", H, H), "d_y1")
     _emit(g, T, ops, totals)

@@ -1,21 +1,31 @@
 import numpy as np
 from concourse.mybir import AluOpType, ActivationFunctionType
 
-NCH, C = 4, 128
-CW = [C] * NCH
-CP = [C * _j for _j in range(NCH)]
+CW = [128, 128, 160, 96]
+NCH = len(CW)
+CP = [sum(CW[:_j]) for _j in range(NCH + 1)]
+CT = []
+for _j in range(NCH):
+    CT.append((CT[-1][0], CT[-1][1] + 1) if _j and CW[_j] == CW[_j - 1] else ("abcd"[_j], 0))
 H = 256
-NEW = [(0, H, "PF2"), (H, H, "PF3")]
-WRITES = {_k: [(0, 2), (2, 4)] if _k in (1, 4) else [(0, 1), (1, 2), (2, 3), (3, 4)] for _k in range(1, 7)}
+OLD = {"PF0": [0, 1], "PF1": [2, 3]}
+NEW = {_k: [(0, CP[1], "PF2"), (CP[1], 512 - CP[1], "PF3")] for _k in (1, 4)}
+WRITES = {_k: [(0, 1), (1, 2), (2, 3), (3, 4)] for _k in range(1, 7)}
+BYSLOT = False
+SG = 1
+APART = {}
 M = float(3 * 2 ** 22)
 DELTA = -127.0 / 256.0
 AWAY = 2048
+FIRST = [(768, 256), (256, 512), (0, 256)]
 OPT = {}
 
 F32, BF, I32, F16, U16 = "float32", "bfloat16", "int32", "float16", "uint16"
 SCRATCH = {
-    "W0": ("sbuf", [128, 3072], I32), "W": ("sbuf", [128, 3584], F32),
-    "me": ("sbuf", [128, 512], F16), "N": ("sbuf", [128, 6, 512], F16), "cq": ("sbuf", [128, 1024], F16),
+    "R0": ("sbuf", [128, 1024], I32), "W": ("sbuf", [128, 3584], F32),
+    "X0": ("sbuf", [128, 1024], F16), "L0": ("sbuf", [128, 1024], F16),
+    "me": ("sbuf", [128, 512], F16), "Lme": ("sbuf", [128, 512], F16),
+    "N": ("sbuf", [128, 4, 512], F16), "cq": ("sbuf", [128, 1536], F16),
     "tb": ("sbuf", [128, 2048], F16), "tn": ("sbuf", [128, 4, 512], F16), "Db": ("sbuf", [128, 3, 512], F16),
     "KF": ("sbuf", [128, 3, 512], F32),
     "ocb": ("sbuf", [128, 2048], BF), "stk": ("sbuf", [128, 4, 512], BF), "mub": ("sbuf", [128, 8], BF),
@@ -26,33 +36,38 @@ SCRATCH = {
     "yob": ("sbuf", [128, 64], F32),
     "Y": ("sbuf", [128, 144], I32), "Y2": ("sbuf", [128, 128], I32), "YE": ("sbuf", [128, 256], I32),
     "Ib": ("sbuf", [128, 128], BF), "I16": ("sbuf", [128, 128], BF), "If": ("sbuf", [128, 128], F32),
+    "In": ("sbuf", [128, 128], BF), "I9": ("sbuf", [128, 128], BF), "I99": ("sbuf", [128, 128], BF),
     "Sh": ("sbuf", [128, 128], BF), "Z": ("sbuf", [128, 144], BF), "DG": ("sbuf", [128, 1536], BF),
-    "E": ("sbuf", [128, 256], BF),
-    "dl": ("sbuf", [128, 512], BF), "Mc": ("sbuf", [128, 512], BF), "CB": ("sbuf", [128, 8], F32),
-    "pmi": ("sbuf", [128, 1], I32), "zc": ("sbuf", [128, 1], F32), "AC": ("sbuf", [128, 16], F32),
+    "E": ("sbuf", [128, 256], BF), "dl": ("sbuf", [128, 512], BF), "Mc": ("sbuf", [128, 512], BF),
+    "pmi": ("sbuf", [128, 1], I32), "zc": ("sbuf", [128, 1], F32), "AC": ("sbuf", [128, 8], F32),
     "pw0": ("sbuf", [128, 64], I32), "pw": ("sbuf", [128, 64], I32),
-    "LV": ("sbuf", [128, 4, 32], I32), "CV": ("sbuf", [128, 3, 32], I32),
+    "LV": ("sbuf", [128, 2, 32], I32), "CV": ("sbuf", [128, 3, 32], I32),
     "hm": ("sbuf", [128, 96], F32), "base": ("sbuf", [128, 96], I32),
-    "qq": ("sbuf", [128, 128], I32), "vv": ("sbuf", [128, 96], I32),
-    "TH": ("sbuf", [128, 96], F32), "x9": ("sbuf", [128, 96], F32), "uu": ("sbuf", [128, 96], I32),
-    "BB": ("sbuf", [128, 64], I32), "DD": ("sbuf", [128, 96], I32),
+    "qq": ("sbuf", [128, 128], I32), "vv": ("sbuf", [128, 128], BF), "uu": ("sbuf", [128, 96], I32),
+    "DD": ("sbuf", [128, 96], I32),
     "s1": ("sbuf", [128, 64], I32), "s2": ("sbuf", [128, 64], I32), "s3": ("sbuf", [128, 64], I32),
     "s4": ("sbuf", [128, 64], I32), "s5": ("sbuf", [128, 64], F32),
     "oG": ("sbuf", [128, 96], U16), "oC": ("sbuf", [128, 96], U16),
-    "oA2": ("sbuf", [128, 64], U16), "oA3": ("sbuf", [128, 96], U16),
-    "oU2": ("sbuf", [128, 32], U16), "oU3": ("sbuf", [128, 32], U16), "oY": ("sbuf", [128, 128], U16),
+    "oY": ("sbuf", [128, 128], U16),
 }
-for _k in range(7):
-    SCRATCH["Q%d" % _k] = ("sbuf", [128, NCH, (2 if _k < 3 else 3) * C], F16)
-    if _k:
-        SCRATCH["L%d" % _k] = SCRATCH["Q%d" % _k]
+for _j, (_p, _i) in enumerate(CT):
+    SCRATCH["oA" + _p] = ("sbuf", [128, _i + 1, CW[_j] // 4], U16)
+    for _k in range(7):
+        SCRATCH["Q%d%s" % (_k, _p)] = ("sbuf", [128, _i + 1, (APART.get(_k) or 4) * CW[_j]], F16)
+        if _k:
+            SCRATCH["L%d%s" % (_k, _p)] = ("sbuf", [128, _i + 1, (2 if _k < 4 else 3) * CW[_j]], F16)
+for _k in APART:
+    for _f in "QL":
+        SCRATCH["%s%de" % (_f, _k)] = ("sbuf", [128, APART[_k] * (512 - CP[2])], F16)
+        for _p in {CT[2][0], CT[3][0]}:
+            del SCRATCH["%s%d%s" % (_f, _k, _p)]
 for _j in range(NCH):
     SCRATCH["PR%d" % _j] = ("psum", [128, 512], F32)
     SCRATCH["PF%d" % _j] = ("psum", [128, 512], F32)
 
 ENG = {"v": "sv", "a": "sa", "p": "sp", "g": "sg"}
-DSEM = ["d_r0a", "d_r0b", "d_opp", "d_lq", "d_mu", "d_oc", "d_stk", "d_yr", "d_yo", "d_y0", "d_y1"]
-ARR = ["arr0"] + ["arr%d%d" % (_k, _j) for _k in range(1, 7) for _j, _ in WRITES[_k]]
+DSEM = ["d_r0%d" % _i for _i in range(len(FIRST))] + ["d_opp", "d_lq", "d_mu", "d_oc", "d_stk", "d_yr", "d_yo", "d_y0", "d_y1"]
+ARR = ["arr0%d" % _i for _i in range(len(FIRST))] + ["arrme"] + ["arr%d%d" % (_k, _j) for _k in range(1, 7) for _j, _ in WRITES[_k]]
 SEMAPHORES = list(ENG.values()) + DSEM + ARR + ["sent"]
 
 AL = AluOpType
@@ -155,10 +170,8 @@ def rank_program(g, core, T, topo):
     rid, pid, _ = topo.addr(dst)
     mask_out = topo.mask(core, dst)
     n_out, n_in = len(topo.engines(core, dst)), len(topo.engines(src, core))
-    totals = {"arr0": 2 * n_in, "sent": 0}
-    for k in range(1, 7):
-        for j, _ in WRITES[k]:
-            totals["arr%d%d" % (k, j)] = n_in
+    totals = {s: n_in for s in ARR}
+    totals["sent"] = 0
     ops, last = [], {}
     ALL = slice(None)
 
@@ -241,13 +254,25 @@ def rank_program(g, core, T, topo):
         return R("DG", d * 128, 128)
 
     def chunk(fam, k, j, s, n):
-        return A("%s%d" % (fam, k), j, slice(s * C, (s + n) * C))
+        if k in APART and j >= 2:
+            a = APART[k] * (CP[j] - CP[2]) + s * CW[j]
+            return R("%s%de" % (fam, k), a, n * CW[j])
+        return A("%s%d%s" % (fam, k, CT[j][0]), CT[j][1], slice(s * CW[j], (s + n) * CW[j]))
 
-    def part(fam, k, s, a=0, b=NCH):
-        return A("%s%d" % (fam, k), slice(a, b), slice(s * C, (s + 1) * C))
+    def parts(name, s, a=0, b=NCH, unit=1):
+        out = []
+        for p in sorted({CT[j][0] for j in range(a, b)}):
+            js = [j for j in range(a, b) if CT[j][0] == p]
+            w = CW[js[0]] // unit
+            if name + "e" in SCRATCH and js[0] >= 2:
+                out += [(chunk(name[0], int(name[1]), j, s, 1), CP[j], CW[j]) for j in js]
+                continue
+            out.append((A(name + p, slice(CT[js[0]][1], CT[js[-1]][1] + 1), slice(s * w, (s + 1) * w)),
+                        CP[js[0]], CP[js[-1] + 1] - CP[js[0]]))
+        return out
 
     def nat(name, s, n, j):
-        return A(name, s if n == 1 else slice(s, s + n), slice(CP[j], CP[j] + CW[j]))
+        return A(name, s if n == 1 else slice(s, s + n), slice(CP[j], CP[j + 1]))
 
     def rows(name, a, b):
         return A(name, slice(a, b), ALL)
@@ -262,52 +287,66 @@ def rank_program(g, core, T, topo):
         for f in steps:
             f()
 
-    bneg, bdel, bpos = R("CB", 0, 1), R("CB", 1, 1), R("CB", 2, 1)
+    def on(x):
+        return cp if x == "v" else act
+
     ADG = {(1, 0): 0, (2, 1): 1, (3, 2): 2, (2, 0): 3, (3, 1): 4, (3, 0): 5}
     CDG = {(0, 1): 6, (1, 2): 7, (2, 3): 8, (0, 2): 9, (1, 3): 10, (0, 3): 11}
-    SCALE = [0, 1, 2, 6, 7, 8, 9, 10, 11, 12, 13, 14]
 
-    dma("s", R("W0", 512, 512), T.r0[:, 512:1024], "d_r0b")
+    def diag(d):
+        of, by = {0: ("Ib", 0), 1: ("Ib", 1), 2: ("Ib", 2), 3: (0, 1), 4: (1, 2), 5: (3, 2),
+                  6: ("I16", 3), 7: ("I16", 4), 8: ("I16", 5), 9: (6, 4), 10: (7, 5), 11: (9, 5)}[d]
+        act(dg(d), A(of) if of in ("Ib", "I16") else dg(of), scale=R("AC", by, 1))
+
+    def load(i):
+        a, n = FIRST[i]
+        dma("s", R("R0", a, n), T.r0[:, a:a + n], "d_r0%d" % i)
+
+    def first_write(i, x):
+        if i < len(FIRST):
+            a, n = FIRST[i]
+            on(x)(R("X0", a, n), R("R0", a, n))
+            send(R("L0", a, n), R("X0", a, n), "arr0%d" % i)
+
+    def first_landed(i, x):
+        if i < len(FIRST):
+            a, n = FIRST[i]
+            on(x)(R("W", AWAY + a, n), R("L0", a, n), ext=("arr0%d" % i,))
+
+    load(0)
     dma("a", R16("LQ", 0, 512), T.opp[:], "d_lq")
-    dma("a", rows("LV", 0, 2), T.opp[:], "d_opp")
-    dma("s", R("W0", 0, 512), T.r0[:, 0:512], "d_r0a")
+    dma("a", A("LV"), T.opp[:], "d_opp")
+    load(1)
     dma("a", R("mub", 0, 6), T.mu[:], "d_mu")
+    for i in range(2, len(FIRST)):
+        load(i)
     dma("s", A("ocb"), T.oc[:], "d_oc")
     iota(A("Y"), [[-1, 144]], 128, 1)
     iota(R16("YE", 0, 256), [[1, 2], [2, 8], [0, 16]], 0, -1)
     iota(A("pw0"), [[0, 2], [16, 32]], 0, 0)
-    send(R("W0", AWAY + 512, 512), R("W0", 512, 512), "arr0")
-    send(R("W0", AWAY, 512), R("W0", 0, 512), "arr0")
-    iota(R("W0", 1024, 1024), [[0, 1024]], 0, 0)
-    iota(R("W", 1024, 1024), [[0, 1024]], 0, 0, True)
-    dma("s", A("stk"), T.stake[:], "d_stk", ext=("arr0",))
+    dma("s", A("stk"), T.stake[:], "d_stk", ext=("arr0%d" % (len(FIRST) - 1),))
 
     ms(A("dl"), DELTA)
     ms(A("Mc"), M)
     ts(A("Ib"), R("Y", 0, 128), 128.0, None, AL.is_equal)
     ts(A("pmi"), R("Y", 0, 1), 15, None, AL.bitwise_and)
     ts(A("Y2"), R("Y", 0, 128), 111, None, AL.bitwise_and)
-    ms(bneg, -M)
-    ms(bdel, DELTA)
-    ms(bpos, M)
     ts(R16("E", 0, 256), R16("YE", 0, 256), 0.0, None, AL.is_equal)
     ts(A("zc"), A("pmi"), 113.0, None, AL.add)
     ts(A("Sh"), A("Y2"), 0.0, 0.5, AL.is_equal, AL.mult)
     ts(A("Z"), A("Y"), A("zc"), None, AL.is_equal)
-    ts(A("I16"), R("Y", 0, 128), 128.0, 0.0625, AL.is_equal, AL.mult)
+    ts(A("pw"), A("pw0"), A("zc"), -113.0, AL.add, AL.add)
+    ms(R("vv", 96, 32), 1.0)
+    act(A("I16"), A("Ib"), scale=0.0625)
+    act(A("In"), A("Ib"), scale=-1.0)
+    act(A("I9"), A("Ib"), scale=-9.0)
+    act(A("I99"), A("Ib"), scale=99.0)
 
-    def by_chunk(m, j):
-        cp(R("oA%d" % m, m * CP[j] // 16, m * CW[j] // 16), A("LV", slice(0, m), slice(CP[j] // 16, (CP[j] + CW[j]) // 16)))
-
-    def lrow_steps(a, b):
-        n, v = (b - a) * 32, rows("LV", a, b)
-        return [lambda: ts(R("s1", 0, n), v, 15, None, AL.bitwise_and),
-                lambda: ts(R("s2", 0, n), v, 4, 63, AL.logical_shift_right, AL.bitwise_and),
-                lambda: ts(R("s3", 0, n), R("s1", 0, n), 64.0, None, AL.mult),
+    def lookup_steps(v, a, b):
+        n = (b - a) * 32
+        return [lambda: ts(R("oG", a * 32, n), v, 1023.0, None, AL.min),
                 lambda: ts(R("hm", a * 32, n), v, float(AWAY), 0.0625, AL.is_lt, AL.mult),
-                lambda: tt(R("s4", 0, n), R("s3", 0, n), R("s2", 0, n), AL.add),
-                lambda: ts(R("base", a * 32, n), v, 1536.0, None, AL.max),
-                lambda: cp(R("oG", a * 32, n), R("s4", 0, n))]
+                lambda: ts(R("base", a * 32, n), v, 1536.0, None, AL.max)]
 
     def to_list(a, b, bk):
         n = (b - a) * 32
@@ -322,191 +361,239 @@ def rank_program(g, core, T, topo):
                 lambda: ts(R("qq", a * 32, n), rows("CV", a, b), AWAY + 511, None, AL.bitwise_and),
                 lambda: tt(R("vv", a * 32, n), R("qq", a * 32, n), R("pw", 0, n), AL.not_equal)]
 
-    def diag(d):
-        act(dg(d), A("Ib"), scale=R("AC", SCALE[d], 1))
+    def by_chunk(s):
+        for x, a, n in parts("oA", s, unit=16):
+            cp(x, R("oY", s * 32 + a // 16, n // 16))
 
     def outcomes(s, bk):
         for t in range(s + 1):
             mm(A(bk), A("Ib") if t == s else dg(ADG[(s, t)]), R("ocb", t * 512, 512), t == 0)
-        return lambda: act(A("KF", s - 1, ALL), A(bk), bias=bdel)
+        return lambda: act(A("KF", s - 1, ALL), A(bk), bias=DELTA)
 
     def new_rating(k, bk):
         opened(bk, 512)
-        mm(A(bk), A("Sh"), A("me"))
+        mm(A(bk), A("Sh"), me(k))
         rounded(bk, 512)
-        act(A("N", k, ALL), A(bk), bias=bneg)
+        return lambda: act(A("N", k // 3, ALL), A(bk), bias=-M)
 
     def named(k):
         return 2 if k <= 3 else 3
 
-    def sent(k):
-        return 2 if k < 3 else 3
+    def window(k, whole=False):
+        return R("W", 0, AWAY + (3 if whole else named(k - 1)) * 512)
 
-    def window(k):
-        return A("W0") if k == 1 else R("W", 0, AWAY + sent(k - 1) * 512)
-
-    def arrived(k):
-        return ("arr0",) if k == 1 else ()
+    def me(k):
+        return R("X0", 512, 512) if k == 0 else A("me")
 
     def open_f(k, j):
         opened("PF%d" % j, named(k) * CW[j])
 
     def open_r(k, j):
-        opened("PR%d" % j, sent(k) * CW[j])
+        opened("PR%d" % j, named(k) * CW[j])
 
     def fill_f(k, j):
         act(pf(j, 0, named(k)), nat("KF", 0, named(k), j))
 
     def fill_r(k, j):
-        if k < 6:
-            act(pr(j, 0, named(k)), chunk("Q", k - 1, j, 0, named(k)), bias=bdel)
-        if sent(k) > named(k):
-            act(pr(j, named(k), 1), nat("N", k - 1, 1, j), bias=bdel)
+        act(pr(j, 0, named(k)), chunk("Q", k - 1, j, 0, named(k)), bias=DELTA)
 
     def oc0(k, j):
         mm(pr(j, 0, 1), A("I16"), R("ocb", CP[j], CW[j]))
 
     def load_r(k, j):
         open_r(k, j)
-        mm(pr(j, 0, named(k)), A("Ib"), chunk("Q", k - 1, j, 0, named(k)))
-        if sent(k) > named(k):
-            mm(pr(j, named(k), 1), A("Ib"), nat("N", k - 1, 1, j))
+        if k < 6:
+            mm(pr(j, 0, named(k)), A("Ib"), chunk("Q", k - 1, j, 0, named(k)))
         oc0(k, j)
 
     def prepare(k, plan):
         for x in plan.split():
-            {"f": fill_f, "r": fill_r, "F": open_f, "R": open_r, "O": oc0, "L": load_r}[x[0]](k, int(x[1]))
+            {"f": fill_f, "r": fill_r, "F": open_f, "R": open_r, "O": oc0, "L": load_r, "T": less}[x[0]](k, int(x[1]))
 
     def c0(j):
         mm(pr(j, 0, 1), A("I16"), nat("tn", 0, 1, j))
 
-    def tbat(j, s, n):
-        return R("tb", 4 * CP[j] + s * CW[j], n * CW[j])
+    def tbat(j, n):
+        return R("tb", 4 * CP[j], n * CW[j])
 
-    def g_named(k, j, a=0, n=None):
+    def gather(k, j, n):
+        m, w = n - 1 if k - 1 in APART else n, CW[j]
+        off = lambda a, b: A("oA" + CT[j][0], CT[j][1], slice(a * w // 16, b * w // 16))
+        tt(tbat(j, m), window(k) + off(0, m), chunk("Q", k - 1, j, 0, m), AL.subtract)
+        if m < n:
+            tt(R("tb", 4 * CP[j] + m * w, w), window(k) + off(m, n), nat("N", 2 + k // 3, 1, j), AL.subtract)
+
+    def spare(k, j):
+        return "PR3" if k == 3 else "PF3"
+
+    def less(k, j, n=None, bk=None):
+        n, bk = n or named(k) + 1, bk or spare(k, j)
+        m = n - 1 if k - 1 in APART else n
+        mm(R(bk, 0, m * CW[j]), A("In"), chunk("Q", k - 1, j, 0, m), True)
+        if m < n:
+            mm(R(bk, m * CW[j], CW[j]), A("In"), nat("N", 2 + k // 3, 1, j))
+
+    def gather_a(k, j, n=None):
+        n, w = n or named(k) + 1, CW[j]
+        act(R("cq", j % 3 * 512, n * w), window(k) + A("oA" + CT[j][0], CT[j][1], slice(0, n * w // 16)))
+
+    def clip_a(k, j, n=None, bk=None):
+        n, bk = n or named(k) + 1, bk or spare(k, j)
+        mm(R(bk, 0, n * CW[j]), A("Ib"), R("cq", j % 3 * 512, n * CW[j]))
+        ts(nat("tn", 0, n, j), R(bk, 0, n * CW[j]), 256.0, -256.0, AL.min, AL.max)
+
+    def clip(j, n):
+        ts(nat("tn", 0, n, j), tbat(j, n), 256.0, -256.0, AL.min, AL.max)
+
+    def fwd(k, j):
         nn = named(k)
-        n = nn - a if n is None else n
-        off = R("oA%d" % nn, (nn * CP[j] + a * CW[j]) // 16, n * CW[j] // 16)
-        tt(tbat(j, a, n), window(k) + off, chunk("Q", k - 1, j, a, n), AL.subtract, arrived(k))
-
-    def g_last(k, j):
-        nn = named(k)
-        tt(tbat(j, nn, 1), window(k) + R("oU%d" % nn, CP[j] // 16, CW[j] // 16), nat("N", k - 1, 1, j), AL.subtract)
-
-    def clip(j, a, n):
-        ts(nat("tn", a, n, j), tbat(j, a, n), 256.0, -256.0, AL.min, AL.max)
-
-    def fwd(k, j, lo=0, hi=None):
-        nn = named(k)
-        hi = nn + 1 if hi is None else hi
-        for t in range(lo, hi):
+        for t in range(nn):
             for s in range(t + 1, nn + 1):
                 mm(pf(j, s - 1, 1), dg(ADG[(s, t)]), nat("tn", t, 1, j))
-        a = max(lo, 1)
-        if hi > a:
-            mm(pf(j, a - 1, hi - a), A("Ib"), nat("tn", a, hi - a, j))
+        mm(pf(j, 0, nn), A("Ib"), nat("tn", 1, nn, j))
 
-    def floor_d(k, j, on="v"):
-        if on == "a":
-            rounded("PF%d" % j, named(k) * CW[j])
-            act(nat("Db", 0, named(k), j), pf(j, 0, named(k)), bias=bneg)
-        elif on == "b":
-            act(pf(j, 0, named(k)), pf(j, 0, named(k)), bias=bpos)
-            act(nat("Db", 0, named(k), j), pf(j, 0, named(k)), bias=bneg)
+    def whole(out, a, n, x):
+        if x == "v":
+            ts(out, R(a, 0, n), M, -M, AL.add, AL.add)
+            return
+        if x == "t":
+            rounded(a, n)
         else:
-            ts(nat("Db", 0, named(k), j), pf(j, 0, named(k)), M, -M, AL.add, AL.add)
+            act(R(a, 0, n), R(a, 0, n), bias=M)
+        act(out, R(a, 0, n), bias=-M)
+
+    def floor_d(k, j, x):
+        whole(nat("Db", 0, named(k), j), "PF%d" % j, named(k) * CW[j], x)
 
     def bwd(k, j, lo=1, hi=None):
-        nn, no = named(k), sent(k)
+        nn = named(k)
         hi = nn + 1 if hi is None else hi
         for t in range(lo, hi):
             for s in range(t):
                 mm(pr(j, s, 1), dg(CDG[(s, t)]), nat("Db", t - 1, 1, j))
-        b = min(hi, no)
+        b = min(hi, nn)
         if b > lo:
             mm(pr(j, lo, b - lo), A("I16"), nat("Db", lo - 1, b - lo, j))
 
-    def fin(k, j, on="a"):
-        no = sent(k)
-        if on == "a":
-            rounded("PR%d" % j, no * CW[j])
-            act(chunk("Q", k, j, 0, no), pr(j, 0, no), bias=bneg)
-        else:
-            ts(chunk("Q", k, j, 0, no), pr(j, 0, no), M, -M, AL.add, AL.add)
+    def fin(k, j, x):
+        nn = named(k)
+        whole(chunk("Q", k, j, 0, nn), "PR%d" % j, nn * CW[j], x)
         for a, b in WRITES[k]:
-            if b == j + 1:
-                send(rows("L%d" % k, a, b), rows("Q%d" % k, a, b), "arr%d%d" % (k, a))
+            if b == j + 1 and k in APART and a >= 2:
+                x, n = nn * (CP[a] - CP[2]), nn * (CP[b] - CP[a])
+                send(R("L%de" % k, x, n), R("Q%de" % k, x, n), "arr%d%d" % (k, a))
+            elif b == j + 1:
+                (p, i), at = CT[j], slice(CT[a][1], CT[j][1] + 1)
+                send(A("L%d%s" % (k, p), at, ALL), A("Q%d%s" % (k, p), at, slice(0, nn * CW[j])), "arr%d%d" % (k, a))
 
     def newest(k, bk):
+        nn = named(k)
         opened(bk, 512)
-        mm(A(bk), A("Ib"), A("N", k - 1, ALL))
-        mm(A(bk), A("I16"), A("Db", named(k) - 1, ALL))
+        was = {1: A("N", 0, ALL), 4: A("N", 1, ALL)}
+        now = {3: A("me"), 6: A("yrb", 3, ALL)}
+        for x in APART:
+            now[x] = was[x + 1] = A("N", 2 + x // 3, ALL)
+        for x, a, n in [(was[k], 0, 512)] if k in was else parts("Q%d" % (k - 1), nn):
+            mm(R(bk, a, n), A("Ib"), x)
+        mm(A(bk), A("I16"), A("Db", nn - 1, ALL))
         rounded(bk, 512)
-        act(A("N", k, ALL) if k < 6 else A("yrb", 3, ALL), A(bk), bias=bneg)
+        if k == 6:
+            return lambda: act(now[k], A(bk), bias=-M)
+        if k in now:
+            act(now[k], A(bk), bias=-M)
+            return None
+        (x, a, n), rest = parts("Q%d" % k, nn)[0], parts("Q%d" % k, nn)[1:]
+        act(x, R(bk, a, n), bias=-M)
+        if OPT.get("nw", "a") == "a":
+            for x, a, n in rest:
+                act(x, R(bk, a, n), bias=-M)
+            return None
+        return lambda: [ts(x, R(bk, a, n), -M, None, AL.add) for x, a, n in rest]
 
-    def home(k, a, b, on="vvv"):
-        for s in range(sent(k)):
-            (cp if on[s] == "v" else act)(R("W", s * 512 + a * C, (b - a) * C), part("Q", k, s, a, b))
+    def home(k, a, b, by):
+        for s in range(named(k)):
+            if by[s] != "-":
+                for x, p, n in parts("Q%d" % k, s, a, b):
+                    on(by[s])(R("W", s * 512 + p, n), x)
 
-    def away(k, a, b, on="vvv"):
-        ext = tuple("arr%d%d" % (k, x) for x, y in WRITES[k] if x < b and y > a)
-        for s in range(sent(k)):
-            (cp if on[s] == "v" else act)(R("W", AWAY + s * 512 + a * C, (b - a) * C), part("L", k, s, a, b), ext=ext)
+    def away(k, a, b, by):
+        for s in range(named(k)):
+            for x, p, n in parts("L%d" % k, s, a, b):
+                on(by[s])(R("W", AWAY + s * 512 + p, n), x,
+                          ext=tuple("arr%d%d" % (k, u) for u, v in WRITES[k] if u < b and v > a))
 
     def sweep(k, ahead=(), mid=(), more=()):
         nn = named(k)
-        step = {"n": lambda j: g_named(k, j), "l": lambda j: g_last(k, j),
-                "g": lambda j: (g_named(k, j), g_last(k, j)),
-                "c": lambda j: (clip(j, 0, nn + 1), fwd(k, j), c0(j)),
-                "x": lambda j: (clip(j, 0, nn), fwd(k, j, 0, nn), c0(j)),
-                "y": lambda j: (clip(j, nn, 1), fwd(k, j, nn)),
-                "f": lambda j: floor_d(k, j), "F": lambda j: floor_d(k, j, "b"), "M": lambda j: floor_d(k, j, "a"),
-                "b": lambda j: bwd(k, j), "o": lambda j: fin(k, j), "v": lambda j: fin(k, j, "v"),
-                "O": lambda j: oc0(k, j), "m": lambda j: run(mid), "p": lambda j: run(more)}
+        step = {"g": lambda j: gather(k, j, nn + 1), "c": lambda j: (clip(j, nn + 1), fwd(k, j), c0(j)),
+                "f": lambda j: floor_d(k, j, "v"), "F": lambda j: floor_d(k, j, "s"), "M": lambda j: floor_d(k, j, "t"),
+                "b": lambda j: bwd(k, j), "o": lambda j: fin(k, j, "t"), "v": lambda j: fin(k, j, "v"),
+                "G": lambda j: gather_a(k, j), "C": lambda j: clip_a(k, j), "w": lambda j: (fwd(k, j), c0(j)),
+                "d": lambda j: clip(j, nn + 1), "T": lambda j: less(k, j), "L": lambda j: load_r(k, j),
+                "X": lambda j: prepare(k, "F%d f%d" % (j, j)), "x": lambda j: fill_f(k, j),
+                "s": lambda j: fin(k, j, "s"), "m": lambda j: run(mid), "p": lambda j: run(more),
+                "q": lambda s: [tt(A("yrb", s, slice(a, a + n)), x, y, AL.add)
+                                for (x, a, n), (y, _, _) in zip(parts("Q5", s, 0, 2), parts("Q6", s, 0, 2))]}
         run(ahead)
         for x in OPT.get("s%d" % k, ORDER[k]).split():
             step[x[0]](int(x[1]))
 
-    ORDER = {2: "g0 c0 m0 g1 c1 f0 b0 o0 p0 g2 c2 f1 b1 o1 O3 g3 c3 f2 b2 o2 f3 b3 o3",
-             3: "g0 c0 F0 g1 c1 F1 b0 o0 g2 c2 F2 b1 g3 c3 v1 b2 f3 b3 v2 o3",
-             5: "g0 c0 F0 g1 c1 F1 b0 o0 O2 g2 c2 F2 b1 O3 g3 c3 v1 b2 f3 b3 v2 o3"}
-    ORDER[6] = ORDER[5]
+    ORDER = {2: "G1 x2 g0 m0 d0 C1 w0 M0 w1 X3 M1 b0 o0 p0 g2 c2 b1 o1 g3 c3 f2 f3 b2 v2 b3 v3",
+             3: "G1 m0 x2 g0 d0 C1 w0 M0 w1 X3 M1 b0 o0 L3 g2 c2 b1 o1 p0 g3 c3 f2 f3 b2 v2 b3 v3",
+             5: "G1 x2 g0 d0 C1 w0 M0 w1 M1 b0 o0 X3 g2 c2 b1 g3 c3 f2 v1 b2 f3 b3 v2 v3"}
+    ORDER[6] = ORDER[5].replace("g0", "m0 g0") + " q0 q1 q2"
 
-    def between(k, first, plan):
+    def between(k, first, plan, second=()):
         prepare(k + 1, "F0 f0")
-        newest(k, "PF3")
-        prepare(k + 1, plan)
-        update(k, first)
+        rest = newest(k, "PF3")
+        early, late = plan.split("|")
+        prepare(k + 1, early)
+        update(k, list(first) + [rest or (lambda: None), lambda: prepare(k + 1, late)], second)
 
-    def update(k, first, on="vav"):
-        h = OPT.get("h", "vvv vva vvv").split()
-        home(k, 0, 2, h[0])
-        run(first)
-        home(k, 2, 4, h[1])
-        away(k, 0, 2, h[2])
-        for a, b in WRITES[k][-2:]:
-            if a >= 2:
-                away(k, a, b, on)
+    UPDATE = {k: "h02vv- * h24vvv h02--a a02vvv a23vav a34vav" for k in range(1, 6)}
+    for k in APART:
+        UPDATE[k] = "h02vv- * h24vv- h04--a a02vvv a24vav"
+    UPDATE[3] = "h04vv- a02vvv * a23vvv a34vav"
 
-    def counts(m):
+    UPDATE[1] = "h02vv- * h24vvv a02vvv + a23vav a34vav"
+
+    def update(k, first, second=()):
+        for x in OPT.get("h%d" % k, UPDATE[k]).split():
+            if x in "*+":
+                run(first if x == "*" else second)
+            else:
+                (home if x[0] == "h" else away)(k, int(x[1]), int(x[2]), x[3:])
+
+    def counts(m, bk):
+        for i, (best, later) in enumerate([(0, 1), (0, 2), (3, 2)][:m]):
+            mm(R(bk, 32 * i, 32), A("I9"), R("vv", 32 * best, 32), i == 0)
+            mm(R(bk, 32 * i, 32), A("I99"), R("vv", 32 * later, 32))
         for i in range(16):
-            mm(R("PR3", 0, 32 * m), R("Z", 15 - i, 128), R("lt", i, 512 * m - i, 16), i == 0)
+            mm(R(bk, 0, 32 * m), R("Z", 15 - i, 128), R("lt", i, 512 * m - i, 16))
 
-    def open_first(k):
-        for s in range(1, named(k)):
-            opened("PF%d" % (s - 1), 512)
-        for a, n, bk in NEW:
-            opened(bk, n)
+    def old_at(j, s):
+        if BYSLOT:
+            return R("PF%d" % s, CP[j], CW[j])
+        bk = [b for b in OLD if j in OLD[b]][0]
+        return R(bk, s * old_n(bk) + CP[j] - CP[OLD[bk][0]], CW[j])
 
-    def halves(name, h):
-        return A(name, slice(0, 2), slice(h * H, h * H + H))
+    def old_n(bk):
+        return H if BYSLOT else sum(CW[j] for j in OLD[bk])
+
+    def old_of(name, bk):
+        if BYSLOT:
+            return A(name, int(bk[2]), ALL)
+        return A(name, slice(0, 2), slice(CP[OLD[bk][0]], CP[OLD[bk][-1] + 1]))
+
+    def old_fill(bk):
+        opened(bk, 2 * old_n(bk))
+        act(R(bk, 0, 2 * old_n(bk)), old_of("KF", bk))
 
     def old_fwd(k, j):
         nn = named(k)
-        a, n, bk = NEW[j // 2]
-        clip(j, 0, nn)
+        a, n, bk = [x for x in NEW[k] if x[0] <= CP[j] < x[0] + x[1]][0]
+        clip(j, nn)
         for s in range(1, nn):
-            to = R("PF0", j * C, C) if k == 1 else R("PF%d" % (j // 2), (s - 1) * H + j % 2 * C, C)
+            to = R("PF0", CP[j], CW[j]) if k == 1 else old_at(j, s - 1)
             for t in range(s + 1):
                 mm(to, A("Ib") if t == s else dg(ADG[(s, t)]), nat("tn", t, 1, j))
         for t in range(nn):
@@ -514,219 +601,222 @@ def rank_program(g, core, T, topo):
 
     def load_first(s, pieces):
         for a, n, bk in pieces:
+            opened(bk, n)
             for t in range(s + 1):
                 mm(R(bk, 0, n), A("Ib") if t == s else dg(ADG[(s, t)]), R("ocb", t * 512 + a, n))
 
-    def old_floor(k, h):
-        rounded("PF%d" % h, 512)
-        act(A("Db", 0, ALL) if k == 1 else halves("Db", h), A("PF%d" % h), bias=bneg)
+    def old_floor(bk):
+        whole(old_of("Db", bk), bk, 2 * old_n(bk), "t")
 
     def old_bwd(k, j):
         c0(j)
         bwd(k, j, 1, named(k))
 
     def new_gather(k, h):
-        nn, (a, n, bk) = named(k), NEW[h]
-        t = R("tb", 2048 - 512 + a, n)
-        tt(t, window(k) + R("oU%d" % nn, a // 16, n // 16), A("N", k - 1, slice(a, a + n)), AL.subtract)
+        nn, (a, n, bk) = named(k), NEW[k][h]
+        tt(R("tb", 1536 + a, n), window(k, k == 4) + R("oY", nn * 32 + a // 16, n // 16),
+           A("N", k // 3, slice(a, a + n)), AL.subtract)
 
     def new_fwd(k, h):
-        nn, (a, n, bk) = named(k), NEW[h]
-        ts(A("tn", nn, slice(a, a + n)), R("tb", 2048 - 512 + a, n), 256.0, -256.0, AL.min, AL.max)
+        nn, (a, n, bk) = named(k), NEW[k][h]
+        ts(A("tn", nn, slice(a, a + n)), R("tb", 1536 + a, n), 256.0, -256.0, AL.min, AL.max)
         mm(R(bk, 0, n), A("Ib"), A("tn", nn, slice(a, a + n)))
 
-    def new_floor(k, h):
-        nn, (a, n, bk) = named(k), NEW[h]
-        ts(A("Db", nn - 1, slice(a, a + n)), R(bk, 0, n), M, -M, AL.add, AL.add)
+    def new_floor(k, h, x):
+        nn, (a, n, bk) = named(k), NEW[k][h]
+        whole(A("Db", nn - 1, slice(a, a + n)), bk, n, x)
 
     def first_end(k):
-        on = OPT.get("e%d" % k, "avva")
-        new_gather(k, 0); new_fwd(k, 0)
-        if k == 1:
-            old_bwd(k, 0); old_bwd(k, 1)
-        else:
-            old_bwd(k, 2)
-        new_gather(k, 1); new_floor(k, 0); new_fwd(k, 1)
-        bwd(k, 0, named(k)); fin(k, 0, on[0])
-        new_floor(k, 1)
-        bwd(k, 1, named(k)); fin(k, 1, on[1])
-        if k == 1:
-            old_bwd(k, 2)
-        bwd(k, 2, named(k)); fin(k, 2, on[2])
-        oc0(k, 3); old_bwd(k, 3); bwd(k, 3, named(k)); fin(k, 3, on[3])
+        step = {"g": lambda h: new_gather(k, h), "c": lambda h: new_fwd(k, h),
+                "f": lambda h: new_floor(k, h, "v"), "M": lambda h: new_floor(k, h, "t"),
+                "O": lambda j: oc0(k, j), "B": lambda j: old_bwd(k, j), "b": lambda j: bwd(k, j, named(k)),
+                "o": lambda j: fin(k, j, "t"), "v": lambda j: fin(k, j, "v")}
+        for x in OPT.get("e%d" % k, END[k]).split():
+            step[x[0]](int(x[1]))
+
+    END = {1: "g0 c0 B0 g1 f0 b0 o0 c1 B1 B2 B3 f1 b1 v1 b2 o2 b3 v3",
+           4: "g0 c0 O3 B3 g1 f0 b0 o0 c1 O2 B2 f1 b1 v1 b2 o2 b3 v3"}
 
     def far(k, c, bk):
-        act(R("cq", c * 512, 512), window(k) + R("oC", c * 32, 32), scale=-1.0, ext=arrived(k))
+        act(R("cq", c * 512, 512), window(k) + R("oC", c * 32, 32), scale=-1.0)
         mm(A(bk), A("Ib"), R("cq", c * 512, 512))
 
-    st = lrow_steps(0, 2)
-    ts(R16("LH", 0, 512), R16("LQ", 0, 512), -1536.0, None, AL.add)
-    for h in range(2):
-        mm(A("PF%d" % h), R16("E", h * 128, 128), R16("LH", 0, 512), True)
+    act(R16("LH", 0, 512), R16("LQ", 0, 512), bias=-1536.0)
+    first_write(0, "v")
+    for b in range(2):
+        for q in range(16):
+            mm(R("PF%d" % b, q, 512 - q, 16), R16("E", q // 8 * 128, 128), R16("LH", q % 8 * 64 + b * 32, 32), q == 0)
+    st = lookup_steps(A("LV"), 0, 2)
+    run(st)
+    first_write(1, "a")
     act(R("Lrow", 0, 512), A("PF0"))
-    run(st[:3])
-    ts(A("pw"), A("pw0"), A("zc"), -113.0, AL.add, AL.add)
-    st[4]()
     cp(R("Lrow", 512, 512), A("PF1"))
-    st[6]()
-    ts(R("AC", 0, 6), R("mub", 0, 6), 0.5, None, AL.mult)
+    act(R("AC", 0, 6), R("mub", 0, 6), scale=0.5)
+    cp(R("oY", 0, 64), A("LV"))
     act(R("crow", 512, 512), A("Lrow") + R("oG", 32, 32))
     cp(R("crow", 0, 512), A("Lrow") + R("oG", 0, 32))
-    tt(R("AC", 6, 2), R("AC", 0, 2), R("AC", 1, 2), AL.mult)
+    first_write(2, "v")
+    iota(R("W", 1024, 1024), [[0, 1024]], 0, 0, True)
     to_list(0, 2, "PR3")
-    cp(A("me"), R("W0", 512, 512))
     for d in (0, 1, 3):
         diag(d)
-    st[3]()
-    st[5]()
+    by_chunk(0)
+    by_chunk(1)
+    ts(R("qq", 96, 32), rows("LV", 0, 1), AWAY + 511, None, AL.bitwise_and)
     cs = cand_steps(0, 2, "PR3")
     cs[0]()
-    ts(R("AC", 9, 3), R("mub", 3, 3), 1.0 / 32, None, AL.mult)
+    for x, a, n in parts("Q0", 1):
+        cp(x, R("X0", 512 + a, n))
     cs[1]()
-    ts(R("qq", 96, 32), rows("LV", 0, 1), AWAY + 511, None, AL.bitwise_and)
-    cs[2]()
-    cs[3]()
-    tt(R("AC", 12, 2), R("AC", 9, 2), R("AC", 4, 2), AL.mult)
-    cs[4]()
-    new_rating(0, "PR2")
-    cp(part("Q", 0, 0), R("W0", 0, 512))
-    cp(part("Q", 0, 1), A("me"))
-    outcomes(1, "PR0")()
-    outcomes(2, "PR1")()
-    mm(A("PF1"), A("Ib"), A("me"), True)
-    open_first(1)
+    for x, a, n in parts("Q0", 0):
+        cp(x, R("X0", a, n))
+    run(cs[2:])
+    later = new_rating(0, "PR2")
+    act(R("W", 0, 1024), A("X0"))
+    mm(A("PF1"), A("Ib"), me(0), True)
     load_first(1, [(0, 512, "PF0")])
-    load_first(2, NEW)
-    prepare(1, "L2 L0")
-    for j in range(NCH):
-        by_chunk(2, j)
+    load_first(2, NEW[1])
+    kf = outcomes(1, "PR0")
     tt(R("s1", 0, 32), R("qq", 0, 32), R("qq", 96, 32), AL.subtract)
-    ts(R("x9", 0, 32), R("vv", 0, 32), 9.0, None, AL.mult)
     tt(R("s2", 0, 32), R("s1", 0, 32), R("vv", 0, 32), AL.mult)
-    ts(R("x9", 32, 32), R("vv", 32, 32), -99.0, 99.0, AL.mult, AL.add)
-    tt(R("BB", 0, 32), R("s2", 0, 32), R("qq", 96, 32), AL.add)
-    tt(R("TH", 0, 32), R("x9", 0, 32), R("x9", 32, 32), AL.add)
-    tt(R("DD", 64, 32), R("qq", 32, 32), R("BB", 0, 32), AL.subtract)
-    tt(R("AC", 8, 1), R("AC", 6, 1), R("AC", 2, 1), AL.mult)
-    tt(R("AC", 14, 1), R("AC", 12, 1), R("AC", 5, 1), AL.mult)
 
+    first_landed(0, "v")
+    later()
+    first_landed(1, "a")
+    first_landed(2, "v")
     far(1, 0, "PF1")
-    tt(R("tc", 512, 512), A("W0") + R("oC", 32, 32), A("me"), AL.subtract, ("arr0",))
+    tt(R("tc", 512, 512), window(1) + R("oC", 32, 32), me(0), AL.subtract)
     act(R("ds", 0, 512), R("tc", 512, 512), AF.Abs)
     act(A("PF1"), A("PF1"), AF.Abs)
-    prepare(1, "L1")
+    kf()
+    outcomes(2, "PR1")()
     for d in (6, 7, 9):
         diag(d)
-    g_named(1, 0); g_named(1, 1); old_fwd(1, 0); old_fwd(1, 1)
+    gather(1, 0, 2); gather(1, 1, 2); old_fwd(1, 0)
+    tt(R("qq", 0, 32), R("s2", 0, 32), R("qq", 96, 32), AL.add)
+    old_fwd(1, 1)
+    tt(R("DD", 64, 32), R("qq", 32, 32), R("qq", 0, 32), AL.subtract)
     tt(R("lt", 0, 512), R("ds", 0, 512), A("PF1"), AL.is_lt)
-    counts(1)
-    g_named(1, 2); g_named(1, 3)
-    tt(R("uu", 0, 32), R("PR3", 0, 32), R("TH", 0, 32), AL.is_ge)
+    counts(1, "PR3")
+    prepare(1, "L2 L0")
+    gather(1, 2, 2); gather(1, 3, 2)
+    ts(R("uu", 0, 32), R("PR3", 0, 32), 99.0, None, AL.is_ge)
     old_fwd(1, 2)
     tt(R("s1", 0, 32), R("uu", 0, 32), R("DD", 64, 32), AL.mult)
     old_fwd(1, 3)
-    tt(R("s2", 0, 32), R("s1", 0, 32), R("BB", 0, 32), AL.add)
-    old_floor(1, 0)
-    prepare(1, "R3 r3")
+    tt(R("s2", 0, 32), R("s1", 0, 32), R("qq", 0, 32), AL.add)
+    whole(A("Db", 0, ALL), "PF0", 512, "t")
+    prepare(1, "L1 L3")
+    ts(R("oY", 64, 32), R("s2", 0, 32), 512.0, None, AL.add)
+    act(R("yob", 0, 32), R("s2", 0, 32), bias=512.0)
+    first_end(1)
+    between(1, lookup_steps(R("yob", 0, 32), 2, 3)
+            + [lambda: by_chunk(2)], OPT.get("p1", "F1 f1 L0 F2 L1 L2 | T1"),
+            [lambda: on(OPT.get("cr", "va")[0])(R("crow", 0, H), A("Lrow") + R("oG", 64, 16)),
+             lambda: on(OPT.get("cr", "va")[1])(R("crow", H, H), A("Lrow") + R("oG", 80, 16)),
+             lambda: to_list(2, 3, "PR3")])
+    cs = cand_steps(2, 3, "PR3")
+    sweep(2, (), cs[:1], [lambda: prepare(2, "L3")])
     for d in (2, 4, 5):
         diag(d)
-    ts(A("oU2"), R("s2", 0, 32), 512.0, None, AL.add)
-    first_end(1)
-    between(1, [lambda: ts(rows("LV", 2, 3), R("s2", 0, 32), 512.0, None, AL.add)] + lrow_steps(2, 3),
-            "R0 r0 F1 f1 L1 F2 L2 O0")
-    cs = cand_steps(2, 3, "PR3")
-    sweep(2, [lambda: act(R("crow", 0, 512), A("Lrow") + R("oG", 64, 32)), lambda: prepare(2, "f2"),
-              lambda: outcomes(3, "PF3")()],
-          [lambda: to_list(2, 3, "PR3"), lambda: prepare(2, "F3 f3")], [cs[0], lambda: prepare(2, "R3 r3")])
-    between(2, cs[1:] + [lambda j=j: by_chunk(3, j) for j in range(NCH)]
-            + [lambda: ts(R("x9", 64, 32), R("vv", 64, 32), -99.0, 99.0, AL.mult, AL.add),
-               lambda: cp(R("BB", 32, 32), R("qq", 32, 32)),
-               lambda: tt(R("DD", 0, 32), R("qq", 64, 32), R("BB", 0, 32), AL.subtract)],
-            "F1 f1 F2 F3 L0 L1 L2 L3")
-    sweep(3, [lambda: prepare(3, "f2 f3")] + [lambda d=d: diag(d) for d in (8, 10, 11)])
+    between(2, cs[1:] + [lambda: tt(R("DD", 0, 32), R("qq", 64, 32), R("qq", 0, 32), AL.subtract),
+                         lambda: tt(R("DD", 32, 32), R("qq", 64, 32), R("qq", 32, 32), AL.subtract)],
+            OPT.get("p2", "F1 f1 F2 L0 L1 L2 | T1"))
+    kf = outcomes(3, "PF3")
+    sweep(3, (), [kf], [lambda d=d: diag(d) for d in (8, 10, 11)])
 
-    open_first(4)
-    act(A("me"), part("Q", 3, 2))
-    for h in range(2):
-        act(A("PF%d" % h), halves("KF", h))
-    new_rating(3, "PR2")
-    mm(A("PR0"), A("Ib"), A("me"), True)
-    mm(A("PR1"), A("Ib"), A("me"), True)
-    load_first(3, NEW)
-    prepare(4, "L2")
-    update(3, [lambda: tt(R("TH", 32, 32), R("x9", 0, 32), R("x9", 64, 32), AL.add),
-               lambda: tt(R("DD", 32, 32), R("qq", 64, 32), R("qq", 32, 32), AL.subtract),
-               lambda: ts(R("TH", 64, 32), R("x9", 64, 32), 9.0, None, AL.add)])
+    banks = list(OLD)
+    old_fill(banks[0])
+    newest(3, "PR0")
+    send(A("Lme"), A("me"), "arrme")
+    old_fill(banks[1])
+    new_rating(3, "PR1")()
+    mm(A("PR2"), A("Ib"), A("me"), True)
+    mm(A("PR3"), A("Ib"), A("me"), True)
+    for bk in banks[2:]:
+        old_fill(bk)
+    load_first(3, NEW[4])
+    update(3, [lambda: [cp(x, R("me", a, n)) for x, a, n in parts("Q3", 2)]])
+    prepare(4, "L0")
     pick = [lambda: tt(A("s1"), R("uu", 32, 64), R("DD", 0, 64), AL.mult),
-            lambda: tt(A("s2"), A("s1"), A("BB"), AL.add),
-            lambda: tt(R("s3", 0, 32), R("s2", 32, 32), R("s2", 0, 32), AL.subtract),
-            lambda: tt(R("s4", 0, 32), R("s3", 0, 32), R("uu", 0, 32), AL.mult),
-            lambda: tt(R("s3", 32, 32), R("s4", 0, 32), R("s2", 0, 32), AL.add)]
-    far(4, 0, "PR0")
-    far(4, 1, "PR1")
+            lambda: ts(R("uu", 0, 32), R("PR2", 0, 32), 99.0, None, AL.is_lt),
+            lambda: tt(A("s2"), A("s1"), R("qq", 0, 64), AL.add),
+            lambda: ts(R("uu", 32, 32), R("PR2", 0, 32), 99.0, None, AL.is_ge),
+            lambda: tt(A("s4"), A("s2"), R("uu", 0, 64), AL.mult),
+            lambda: tt(R("s3", 32, 32), R("s4", 0, 32), R("s4", 32, 32), AL.add)]
+    far(4, 0, "PR2")
+    far(4, 1, "PR3")
+    prepare(4, "L1")
     tt(R("tc", 1024, 512), window(4) + R("oC", 64, 32), A("me"), AL.subtract)
     act(R("ds", 512, 512), R("tc", 1024, 512), AF.Abs)
-    act(A("PR0"), A("PR0"), AF.Abs)
-    act(R("ds", 0, 512), A("PR1"), AF.Abs)
-    act(A("PR1"), R("ds", 0, 512))
-    g_named(4, 0); g_named(4, 1); old_fwd(4, 0); old_fwd(4, 1)
-    old_floor(4, 0)
-    tt(R("lt", 512, 512), R("ds", 512, 512), A("PR0"), AL.is_lt)
-    tt(R("lt", 0, 512), R("ds", 0, 512), A("PR0"), AL.is_lt)
-    prepare(4, "R0 r0")
-    tt(R("lt", 1024, 512), R("ds", 512, 512), A("PR1"), AL.is_lt)
-    counts(3)
-    prepare(4, "R1 r1 O0")
-    old_bwd(4, 0)
-    g_named(4, 2); g_named(4, 3)
-    tt(A("uu"), R("PR3", 0, 96), A("TH"), AL.is_ge)
+    act(A("PR2"), A("PR2"), AF.Abs)
+    act(R("ds", 0, 512), A("PR3"), AF.Abs)
+    act(A("PR3"), R("ds", 0, 512))
+    gather(4, 0, 3); gather(4, 1, 3); old_fwd(4, 0); old_fwd(4, 1)
+    for bk in [] if BYSLOT else banks[:-1]:
+        old_floor(bk)
+    gather(4, 2, 3)
+    tt(R("lt", 512, 512), R("ds", 512, 512), A("PR2"), AL.is_lt)
     old_fwd(4, 2)
-    pick[0]()
+    tt(R("lt", 0, 512), R("ds", 0, 512), A("PR2"), AL.is_lt)
+    tt(R("lt", 1024, 512), R("ds", 512, 512), A("PR3"), AL.is_lt)
+    counts(3, "PR2")
+    act(R("W", AWAY + 1024, 512), A("Lme"), ext=("arrme",))
+    gather(4, 3, 3)
+    act(R("W", 1024, 512), A("me"))
     old_fwd(4, 3)
-    old_floor(4, 1)
-    prepare(4, "R3 r3 O1")
+    for bk in banks if BYSLOT else banks[-1:]:
+        old_floor(bk)
+    prepare(4, "R3 r3")
+    old_bwd(4, 0)
+    ts(R("uu", 32, 64), R("PR2", 32, 64), 99.0, None, AL.is_ge)
     old_bwd(4, 1)
-    run(pick[1:])
-    ts(A("oU3"), R("s3", 32, 32), 1024.0, None, AL.add)
+    run(pick[:4])
+    prepare(4, "R2 r2")
+    run(pick[4:])
+    ts(R("oY", 96, 32), R("s3", 32, 32), 1024.0, None, AL.add)
     first_end(4)
-    plan = "R0 r0 F1 f1 R1 r1 F2 R2 F3 R3 O0 O1"
-    between(4, [lambda: ts(rows("LV", 3, 4), R("s3", 32, 32), 1024.0, None, AL.add)], plan)
-    sweep(5, [lambda: prepare(5, "f2 r2 f3 r3")])
-    between(5, [lambda: cp(A("oY"), A("LV")), lambda: cp(A("yob"), rows("LV", 2, 4)),
-                lambda: dma("s", T.yo[:], A("yob"), "d_yo"),
-                lambda: ts(A("If"), R("Y", 0, 128), 128.0, None, AL.is_equal)], plan)
-    sweep(6, [lambda: prepare(6, "f2 f3")])
+    plan = OPT.get("plan", "F1 f1 L0 F2 L1 L2 | T1 L3")
+    between(4, [lambda: by_chunk(3)], plan)
+    sweep(5)
+    between(5, [], plan)
+    sweep(6, (), [lambda: act(R("yob", 32, 32), R("s3", 32, 32), bias=1024.0), lambda: act(A("If"), A("Ib")),
+                  lambda: dma("s", T.yo[:], A("yob"), "d_yo")])
 
+    E = CP[2]
+    for k in (5, 6):
+        for s in range(3):
+            for x, a, n in parts("Q%d" % k, s, 2, 4):
+                mm(R("PF%d" % s, a - E, n), A("Ib"), x, k == 5 and a == E)
     for s in range(3):
-        mm(A("PF%d" % s), A("Ib"), part("Q", 5, s), True)
-        mm(A("PF%d" % s), A("Ib"), part("Q", 6, s))
-    for s, t in ((0, 1), (2, 0), (1, 2)):
-        act(A("yrb", s, ALL), A("PF%d" % s))
-        cp(R("W", t * 512, 512), A("PF%d" % t))
-
-    def landed(bk, s, a, b, on):
-        n = (b - a) * C
-        mm(R(bk, 0, n), A("Ib"), part("L", 5, s, a, b), True)
-        mm(R(bk, 0, n), A("Ib"), part("L", 6, s, a, b), ext=tuple("arr6%d" % j for j in range(a, b)))
-        on(R("W", AWAY + s * 512 + a * C, n), R(bk, 0, n))
-
+        act(A("yrb", s, slice(E, 512)), R("PF%d" % s, 0, 512 - E))
     for s in range(3):
-        landed("PR%d" % s, s, 0, 2, act if s == 1 else cp)
+        cp(R("W", s * 512 + E, 512 - E), R("PF%d" % s, 0, 512 - E))
     for s in range(3):
-        landed("PF%d" % s, s, 2, 3, act)
+        act(R("W", s * 512, E), A("yrb", s, slice(0, E)))
+    later = newest(6, "PF3")
+    la = OPT.get("la", "aaa vvv vvv").split()
     for s in range(3):
-        if s < 2:
-            tt(R("W", AWAY + s * 512 + 3 * C, C), chunk("L", 5, 3, s, 1), chunk("L", 6, 3, s, 1), AL.add, ("arr63",))
-        else:
-            landed("PR3", s, 3, 4, act)
-    newest(6, "PF3")
+        for k in (5, 6):
+            for x, a, n in parts("L%d" % k, s, 0, 2):
+                mm(R("PR%d" % s, a, n), A("Ib"), x, k == 5 and a == 0, ext=("arr60", "arr61") if k == 6 else ())
+        on(la[0][s])(R("W", AWAY + s * 512, E), R("PR%d" % s, 0, E))
+    later()
+    for j, bk in ((2, "PF0"), (3, "PR3")):
+        mm(R(bk, 0, 3 * CW[j]), A("Ib"), chunk("L", 5, j, 0, 3), True)
+    for j, bk in ((2, "PF0"), (3, "PR3")):
+        mm(R(bk, 0, 3 * CW[j]), A("Ib"), chunk("L", 6, j, 0, 3), ext=("arr6%d" % j,))
+        for s in range(3):
+            on(la[j - 1][s])(R("W", AWAY + s * 512 + CP[j], CW[j]), R(bk, s * CW[j], CW[j]))
     dma("s", T.yr[:], A("yrb"), "d_yr", ext=("arr63",))
 
     def z_of(h, s):
         a = h * H
         tt(R("tc", (4 * h + s) * H, H), window(7) + R("oY", s * 32 + a // 16, H // 16), A("yrb", s, slice(a, a + H)),
            AL.subtract)
-        if s % 2:
+        if h == 0 and s < 2:
+            act(R("PR0", s * H, H), R("tc", s * H, H), AF.Sigmoid, scale=-1.0 / 256)
+        elif s % 2:
             act(A("PR%d" % (2 * h + s // 2)), R("tc", (4 * h + s - 1) * H, 2 * H), AF.Sigmoid, scale=-1.0 / 256)
 
     def weigh(out, h, s):

import numpy as np
from concourse.mybir import AluOpType, ActivationFunctionType

CW = [128, 128, 160, 96]
NCH = len(CW)
CP = [sum(CW[:_j]) for _j in range(NCH + 1)]
CT = []
for _j in range(NCH):
    CT.append((CT[-1][0], CT[-1][1] + 1) if _j and CW[_j] == CW[_j - 1] else ("abcd"[_j], 0))
H = 256
OLD = {"PF0": [0, 1], "PF1": [2, 3]}
NEW = {_k: [(0, CP[1], "PF2"), (CP[1], 512 - CP[1], "PF3")] for _k in (1, 4)}
WRITES = {_k: [(0, 1), (1, 2), (2, 3), (3, 4)] for _k in range(1, 7)}
BYSLOT = False
SG = 1
APART = {}
M = float(3 * 2 ** 22)
DELTA = -127.0 / 256.0
AWAY = 2048
FIRST = [(768, 256), (256, 512), (0, 256)]
OPT = {}

F32, BF, I32, F16, U16 = "float32", "bfloat16", "int32", "float16", "uint16"
SCRATCH = {
    "R0": ("sbuf", [128, 1024], I32), "W": ("sbuf", [128, 3584], F32),
    "X0": ("sbuf", [128, 1024], F16), "L0": ("sbuf", [128, 1024], F16),
    "me": ("sbuf", [128, 512], F16), "Lme": ("sbuf", [128, 512], F16),
    "N": ("sbuf", [128, 4, 512], F16), "cq": ("sbuf", [128, 1536], F16),
    "tb": ("sbuf", [128, 2048], F16), "tn": ("sbuf", [128, 4, 512], F16), "Db": ("sbuf", [128, 3, 512], F16),
    "KF": ("sbuf", [128, 3, 512], F32),
    "ocb": ("sbuf", [128, 2048], BF), "stk": ("sbuf", [128, 4, 512], BF), "mub": ("sbuf", [128, 8], BF),
    "LQ": ("sbuf", [128, 512], I32), "LH": ("sbuf", [128, 512], F16),
    "Lrow": ("sbuf", [128, 1024], F32), "crow": ("sbuf", [128, 1024], F16),
    "tc": ("sbuf", [128, 2048], F32), "ds": ("sbuf", [128, 1024], F32), "lt": ("sbuf", [128, 1536], BF),
    "prod": ("sbuf", [128, 2048], F32), "ysb": ("sbuf", [128, 512], F32), "yrb": ("sbuf", [128, 4, 512], F32),
    "yob": ("sbuf", [128, 64], F32),
    "Y": ("sbuf", [128, 144], I32), "Y2": ("sbuf", [128, 128], I32), "YE": ("sbuf", [128, 256], I32),
    "Ib": ("sbuf", [128, 128], BF), "I16": ("sbuf", [128, 128], BF), "If": ("sbuf", [128, 128], F32),
    "In": ("sbuf", [128, 128], BF), "I9": ("sbuf", [128, 128], BF), "I99": ("sbuf", [128, 128], BF),
    "Sh": ("sbuf", [128, 128], BF), "Z": ("sbuf", [128, 144], BF), "DG": ("sbuf", [128, 1536], BF),
    "E": ("sbuf", [128, 256], BF), "dl": ("sbuf", [128, 512], BF), "Mc": ("sbuf", [128, 512], BF),
    "pmi": ("sbuf", [128, 1], I32), "zc": ("sbuf", [128, 1], F32), "AC": ("sbuf", [128, 8], F32),
    "pw0": ("sbuf", [128, 64], I32), "pw": ("sbuf", [128, 64], I32),
    "LV": ("sbuf", [128, 2, 32], I32), "CV": ("sbuf", [128, 3, 32], I32),
    "hm": ("sbuf", [128, 96], F32), "base": ("sbuf", [128, 96], I32),
    "qq": ("sbuf", [128, 128], I32), "vv": ("sbuf", [128, 128], BF), "uu": ("sbuf", [128, 96], I32),
    "DD": ("sbuf", [128, 96], I32),
    "s1": ("sbuf", [128, 64], I32), "s2": ("sbuf", [128, 64], I32), "s3": ("sbuf", [128, 64], I32),
    "s4": ("sbuf", [128, 64], I32), "s5": ("sbuf", [128, 64], F32),
    "oG": ("sbuf", [128, 96], U16), "oC": ("sbuf", [128, 96], U16),
    "oY": ("sbuf", [128, 128], U16),
}
for _j, (_p, _i) in enumerate(CT):
    SCRATCH["oA" + _p] = ("sbuf", [128, _i + 1, CW[_j] // 4], U16)
    for _k in range(7):
        SCRATCH["Q%d%s" % (_k, _p)] = ("sbuf", [128, _i + 1, (APART.get(_k) or 4) * CW[_j]], F16)
        if _k:
            SCRATCH["L%d%s" % (_k, _p)] = ("sbuf", [128, _i + 1, (2 if _k < 4 else 3) * CW[_j]], F16)
for _k in APART:
    for _f in "QL":
        SCRATCH["%s%de" % (_f, _k)] = ("sbuf", [128, APART[_k] * (512 - CP[2])], F16)
        for _p in {CT[2][0], CT[3][0]}:
            del SCRATCH["%s%d%s" % (_f, _k, _p)]
for _j in range(NCH):
    SCRATCH["PR%d" % _j] = ("psum", [128, 512], F32)
    SCRATCH["PF%d" % _j] = ("psum", [128, 512], F32)

ENG = {"v": "sv", "a": "sa", "p": "sp", "g": "sg"}
DSEM = ["d_r0%d" % _i for _i in range(len(FIRST))] + ["d_opp", "d_lq", "d_mu", "d_oc", "d_stk", "d_yr", "d_yo", "d_y0", "d_y1"]
ARR = ["arr0%d" % _i for _i in range(len(FIRST))] + ["arrme"] + ["arr%d%d" % (_k, _j) for _k in range(1, 7) for _j, _ in WRITES[_k]]
SEMAPHORES = list(ENG.values()) + DSEM + ARR + ["sent"]

AL = AluOpType
AF = ActivationFunctionType


def _cols(name, idx):
    shape = SCRATCH[name][1][1:]
    n = int(np.prod(shape))
    return np.arange(n).reshape(shape)[idx[1:]].reshape(-1)


def _emit(g, T, ops, totals):
    queue = {"v": g.vector, "a": g.scalar, "p": g.tensor, "g": g, "s": g.sync}
    wr, rd, bank = {}, {}, {}
    order, know, clock, waits, need = {}, {q: {} for q in queue}, [], [], set()
    for i, o in enumerate(ops):
        q, key = o["q"], o["sem"] or o["q"]
        deps = set()
        touched = [(a, False) for a in o["r"]] + [(a, True) for a in o["w"]]
        for (name, idx), write in touched:
            if name not in wr:
                n = int(np.prod(SCRATCH[name][1][1:]))
                wr[name], rd[name], bank[name] = np.full(n, -1), {}, {}
            cols = _cols(name, idx)
            deps.update(int(d) for d in np.unique(wr[name][cols]))
            if write:
                for a in rd[name].values():
                    deps.update(int(d) for d in np.unique(a[cols]))
            if SCRATCH[name][0] == "psum":
                deps.update(d for e, d in bank[name].items() if e != q)
        for (name, idx), write in touched:
            cols = _cols(name, idx)
            if write:
                wr[name][cols] = i
                for a in rd[name].values():
                    a[cols] = -1
            else:
                rd[name].setdefault(key, np.full(len(wr[name]), -1))[cols] = i
            bank[name][q] = i
        deps.discard(-1)
        deps.discard(i)
        mine = []
        for s in o["ext"]:
            if know[q].get(s, 0) < 1:
                mine.append(("x", s))
                know[q][s] = 1
        best = {}
        for d in deps:
            dk = ops[d]["sem"] or ops[d]["q"]
            if ops[d]["sem"] == "sent" or (dk == key and (q == "p" or o["sem"])):
                continue
            if dk not in best or d > best[dk]:
                best[dk] = d
        for dk, d in sorted(best.items(), key=lambda e: -e[1]):
            if know[q].get(dk, 0) >= clock[d][dk]:
                continue
            mine.append(("o", d))
            need.add(d)
            for k2, v2 in clock[d].items():
                if know[q].get(k2, 0) < v2:
                    know[q][k2] = v2
        order[key] = order.get(key, 0) + 1
        ck = dict(know[q])
        ck[key] = 1 if o["sem"] else order[key]
        clock.append(ck)
        waits.append(mine)
    count, at = {}, {}
    for i, o in enumerate(ops):
        if o["sem"] in DSEM:
            count[o["sem"]] = count.get(o["sem"], 0) + 16
        elif not o["sem"] and i in need:
            s = ENG[o["q"]]
            count[s] = count.get(s, 0) + 1
            at[i] = count[s]
    for i, o in enumerate(ops):
        e = queue[o["q"]]
        for kind, d in waits[i]:
            if kind == "x":
                e.wait_ge(T.sem[d], totals[d])
            elif ops[d]["sem"]:
                e.wait_ge(T.sem[ops[d]["sem"]], count[ops[d]["sem"]])
            else:
                e.wait_ge(T.sem[ENG[ops[d]["q"]]], at[d])
        ins = o["fn"](e)
        if o["sem"] in DSEM:
            ins.then_inc(T.sem[o["sem"]], 16)
        elif i in at:
            ins.then_inc(T.sem[ENG[o["q"]]], 1)
    for s, n in list(totals.items()) + list(count.items()):
        g.wait_ge(T.sem[s], n)


def rank_program(g, core, T, topo):
    rank = T.rank_of(core)
    if rank is None:
        return
    nr = len(T.cores)
    dst, src = T.cores[(rank - 1) % nr], T.cores[(rank + 1) % nr]
    rid, pid, _ = topo.addr(dst)
    mask_out = topo.mask(core, dst)
    n_out, n_in = len(topo.engines(core, dst)), len(topo.engines(src, core))
    totals = {s: n_in for s in ARR}
    totals["sent"] = 0
    ops, last = [], {}
    ALL = slice(None)

    def A(name, *idx):
        return (name, (ALL,) + (idx if idx else (ALL,) * (len(SCRATCH[name][1]) - 1)))

    def R(name, a, n, step=None):
        return (name, (ALL, slice(a, a + n, step)))

    def R16(name, a, n):
        return (name, (slice(0, 16), slice(a, a + n)))

    def ap(a):
        if isinstance(a, tuple):
            return T[a[0]][a[1]] if len(a) == 2 else T[a[0]][a[1]].indirect(T[a[2]][a[3]])
        return a

    def rds(*xs):
        out = []
        for a in xs:
            if isinstance(a, tuple):
                out.append(a[:2])
                if len(a) == 4:
                    out.append(a[2:])
        return out

    def op(q, fn, r, w, sem=None, ext=()):
        ops.append({"q": q, "fn": fn, "r": rds(*r), "w": rds(*w), "sem": sem, "ext": ext})
        for a in rds(*r):
            last.pop(a[0], None)

    def ts(out, a, s1, s2, o0, o1=None):
        if o1 is None:
            op("v", lambda e: e.tensor_scalar(ap(out), ap(a), ap(s1), None, o0), [a, s1], [out])
        else:
            op("v", lambda e: e.tensor_scalar(ap(out), ap(a), ap(s1), ap(s2), o0, o1), [a, s1, s2], [out])

    def tt(out, a, b, o, ext=()):
        op("v", lambda e: e.tensor_tensor(ap(out), ap(a), ap(b), o), [a, b], [out], ext=ext)

    def cp(out, a, ext=()):
        op("v", lambda e: e.tensor_copy(ap(out), ap(a)), [a], [out], ext=ext)

    def ms(out, c):
        op("v", lambda e: e.memset(ap(out), c), [], [out])

    def act(out, a, f=AF.Identity, bias=0.0, scale=1.0, ext=()):
        op("a", lambda e: e.activation(ap(out), ap(a), f, bias=ap(bias), scale=ap(scale)), [a, bias, scale], [out],
           ext=ext)

    def mm(out, l, r, start=False, ext=()):
        if start:
            last.pop(out[0], None)
        if out[0] in last:
            last[out[0]][0] = False
        flag = [True]
        last[out[0]] = flag
        op("p", lambda e: e.matmul(ap(out), ap(l), ap(r), start, flag[0]), [l, r], [out], ext=ext)

    def opened(b, n):
        mm(R(b, 0, n), A("Ib"), R("dl", 0, n), True)

    def rounded(b, n):
        mm(R(b, 0, n), A("Ib"), R("Mc", 0, n))

    def dma(q, out, a, sem, ext=()):
        op(q, lambda e: e.dma_start(ap(out), ap(a)), [a], [out], sem=sem, ext=ext)

    def send(out, a, sem):
        totals["sent"] += n_out
        op("g", lambda e: e.remote_dma(ap(out), ap(a), T.sem[sem], T.sem.sent, pid, rid, mask_out), [a], [], sem="sent")

    def iota(out, pattern, base, step, flag=False):
        if flag:
            op("g", lambda e: e.iota(ap(out), pattern, base, step, allow_small_or_imprecise_dtypes=True), [], [out])
        else:
            op("g", lambda e: e.iota(ap(out), pattern, base, step), [], [out])

    def dg(d):
        return R("DG", d * 128, 128)

    def chunk(fam, k, j, s, n):
        if k in APART and j >= 2:
            a = APART[k] * (CP[j] - CP[2]) + s * CW[j]
            return R("%s%de" % (fam, k), a, n * CW[j])
        return A("%s%d%s" % (fam, k, CT[j][0]), CT[j][1], slice(s * CW[j], (s + n) * CW[j]))

    def parts(name, s, a=0, b=NCH, unit=1):
        out = []
        for p in sorted({CT[j][0] for j in range(a, b)}):
            js = [j for j in range(a, b) if CT[j][0] == p]
            w = CW[js[0]] // unit
            if name + "e" in SCRATCH and js[0] >= 2:
                out += [(chunk(name[0], int(name[1]), j, s, 1), CP[j], CW[j]) for j in js]
                continue
            out.append((A(name + p, slice(CT[js[0]][1], CT[js[-1]][1] + 1), slice(s * w, (s + 1) * w)),
                        CP[js[0]], CP[js[-1] + 1] - CP[js[0]]))
        return out

    def nat(name, s, n, j):
        return A(name, s if n == 1 else slice(s, s + n), slice(CP[j], CP[j + 1]))

    def rows(name, a, b):
        return A(name, slice(a, b), ALL)

    def pf(j, s, n):
        return R("PF%d" % j, s * CW[j], n * CW[j])

    def pr(j, s, n):
        return R("PR%d" % j, s * CW[j], n * CW[j])

    def run(steps):
        for f in steps:
            f()

    def on(x):
        return cp if x == "v" else act

    ADG = {(1, 0): 0, (2, 1): 1, (3, 2): 2, (2, 0): 3, (3, 1): 4, (3, 0): 5}
    CDG = {(0, 1): 6, (1, 2): 7, (2, 3): 8, (0, 2): 9, (1, 3): 10, (0, 3): 11}

    def diag(d):
        of, by = {0: ("Ib", 0), 1: ("Ib", 1), 2: ("Ib", 2), 3: (0, 1), 4: (1, 2), 5: (3, 2),
                  6: ("I16", 3), 7: ("I16", 4), 8: ("I16", 5), 9: (6, 4), 10: (7, 5), 11: (9, 5)}[d]
        act(dg(d), A(of) if of in ("Ib", "I16") else dg(of), scale=R("AC", by, 1))

    def load(i):
        a, n = FIRST[i]
        dma("s", R("R0", a, n), T.r0[:, a:a + n], "d_r0%d" % i)

    def first_write(i, x):
        if i < len(FIRST):
            a, n = FIRST[i]
            on(x)(R("X0", a, n), R("R0", a, n))
            send(R("L0", a, n), R("X0", a, n), "arr0%d" % i)

    def first_landed(i, x):
        if i < len(FIRST):
            a, n = FIRST[i]
            on(x)(R("W", AWAY + a, n), R("L0", a, n), ext=("arr0%d" % i,))

    load(0)
    dma("a", R16("LQ", 0, 512), T.opp[:], "d_lq")
    dma("a", A("LV"), T.opp[:], "d_opp")
    load(1)
    dma("a", R("mub", 0, 6), T.mu[:], "d_mu")
    for i in range(2, len(FIRST)):
        load(i)
    dma("s", A("ocb"), T.oc[:], "d_oc")
    iota(A("Y"), [[-1, 144]], 128, 1)
    iota(R16("YE", 0, 256), [[1, 2], [2, 8], [0, 16]], 0, -1)
    iota(A("pw0"), [[0, 2], [16, 32]], 0, 0)
    dma("s", A("stk"), T.stake[:], "d_stk", ext=("arr0%d" % (len(FIRST) - 1),))

    ms(A("dl"), DELTA)
    ms(A("Mc"), M)
    ts(A("Ib"), R("Y", 0, 128), 128.0, None, AL.is_equal)
    ts(A("pmi"), R("Y", 0, 1), 15, None, AL.bitwise_and)
    ts(A("Y2"), R("Y", 0, 128), 111, None, AL.bitwise_and)
    ts(R16("E", 0, 256), R16("YE", 0, 256), 0.0, None, AL.is_equal)
    ts(A("zc"), A("pmi"), 113.0, None, AL.add)
    ts(A("Sh"), A("Y2"), 0.0, 0.5, AL.is_equal, AL.mult)
    ts(A("Z"), A("Y"), A("zc"), None, AL.is_equal)
    ts(A("pw"), A("pw0"), A("zc"), -113.0, AL.add, AL.add)
    ms(R("vv", 96, 32), 1.0)
    act(A("I16"), A("Ib"), scale=0.0625)
    act(A("In"), A("Ib"), scale=-1.0)
    act(A("I9"), A("Ib"), scale=-9.0)
    act(A("I99"), A("Ib"), scale=99.0)

    def lookup_steps(v, a, b):
        n = (b - a) * 32
        return [lambda: ts(R("oG", a * 32, n), v, 1023.0, None, AL.min),
                lambda: ts(R("hm", a * 32, n), v, float(AWAY), 0.0625, AL.is_lt, AL.mult),
                lambda: ts(R("base", a * 32, n), v, 1536.0, None, AL.max)]

    def to_list(a, b, bk):
        n = (b - a) * 32
        for i in range(16):
            mm(R(bk, 0, n), R("Z", 15 - i, 128), R("crow", i, 16 * n - i, 16), i == 0)

    def cand_steps(a, b, bk):
        n = (b - a) * 32
        return [lambda: tt(R("s5", 0, n), R(bk, 0, n), R("hm", a * 32, n), AL.mult),
                lambda: tt(rows("CV", a, b), R("s5", 0, n), R("base", a * 32, n), AL.add),
                lambda: cp(R("oC", a * 32, n), rows("CV", a, b)),
                lambda: ts(R("qq", a * 32, n), rows("CV", a, b), AWAY + 511, None, AL.bitwise_and),
                lambda: tt(R("vv", a * 32, n), R("qq", a * 32, n), R("pw", 0, n), AL.not_equal)]

    def by_chunk(s):
        for x, a, n in parts("oA", s, unit=16):
            cp(x, R("oY", s * 32 + a // 16, n // 16))

    def outcomes(s, bk):
        for t in range(s + 1):
            mm(A(bk), A("Ib") if t == s else dg(ADG[(s, t)]), R("ocb", t * 512, 512), t == 0)
        return lambda: act(A("KF", s - 1, ALL), A(bk), bias=DELTA)

    def new_rating(k, bk):
        opened(bk, 512)
        mm(A(bk), A("Sh"), me(k))
        rounded(bk, 512)
        return lambda: act(A("N", k // 3, ALL), A(bk), bias=-M)

    def named(k):
        return 2 if k <= 3 else 3

    def window(k, whole=False):
        return R("W", 0, AWAY + (3 if whole else named(k - 1)) * 512)

    def me(k):
        return R("X0", 512, 512) if k == 0 else A("me")

    def open_f(k, j):
        opened("PF%d" % j, named(k) * CW[j])

    def open_r(k, j):
        opened("PR%d" % j, named(k) * CW[j])

    def fill_f(k, j):
        act(pf(j, 0, named(k)), nat("KF", 0, named(k), j))

    def fill_r(k, j):
        act(pr(j, 0, named(k)), chunk("Q", k - 1, j, 0, named(k)), bias=DELTA)

    def oc0(k, j):
        mm(pr(j, 0, 1), A("I16"), R("ocb", CP[j], CW[j]))

    def load_r(k, j):
        open_r(k, j)
        if k < 6:
            mm(pr(j, 0, named(k)), A("Ib"), chunk("Q", k - 1, j, 0, named(k)))
        oc0(k, j)

    def prepare(k, plan):
        for x in plan.split():
            {"f": fill_f, "r": fill_r, "F": open_f, "R": open_r, "O": oc0, "L": load_r, "T": less}[x[0]](k, int(x[1]))

    def c0(j):
        mm(pr(j, 0, 1), A("I16"), nat("tn", 0, 1, j))

    def tbat(j, n):
        return R("tb", 4 * CP[j], n * CW[j])

    def gather(k, j, n):
        m, w = n - 1 if k - 1 in APART else n, CW[j]
        off = lambda a, b: A("oA" + CT[j][0], CT[j][1], slice(a * w // 16, b * w // 16))
        tt(tbat(j, m), window(k) + off(0, m), chunk("Q", k - 1, j, 0, m), AL.subtract)
        if m < n:
            tt(R("tb", 4 * CP[j] + m * w, w), window(k) + off(m, n), nat("N", 2 + k // 3, 1, j), AL.subtract)

    def spare(k, j):
        return "PR3" if k == 3 else "PF3"

    def less(k, j, n=None, bk=None):
        n, bk = n or named(k) + 1, bk or spare(k, j)
        m = n - 1 if k - 1 in APART else n
        mm(R(bk, 0, m * CW[j]), A("In"), chunk("Q", k - 1, j, 0, m), True)
        if m < n:
            mm(R(bk, m * CW[j], CW[j]), A("In"), nat("N", 2 + k // 3, 1, j))

    def gather_a(k, j, n=None):
        n, w = n or named(k) + 1, CW[j]
        act(R("cq", j % 3 * 512, n * w), window(k) + A("oA" + CT[j][0], CT[j][1], slice(0, n * w // 16)))

    def clip_a(k, j, n=None, bk=None):
        n, bk = n or named(k) + 1, bk or spare(k, j)
        mm(R(bk, 0, n * CW[j]), A("Ib"), R("cq", j % 3 * 512, n * CW[j]))
        ts(nat("tn", 0, n, j), R(bk, 0, n * CW[j]), 256.0, -256.0, AL.min, AL.max)

    def clip(j, n):
        ts(nat("tn", 0, n, j), tbat(j, n), 256.0, -256.0, AL.min, AL.max)

    def fwd(k, j):
        nn = named(k)
        for t in range(nn):
            for s in range(t + 1, nn + 1):
                mm(pf(j, s - 1, 1), dg(ADG[(s, t)]), nat("tn", t, 1, j))
        mm(pf(j, 0, nn), A("Ib"), nat("tn", 1, nn, j))

    def whole(out, a, n, x):
        if x == "v":
            ts(out, R(a, 0, n), M, -M, AL.add, AL.add)
            return
        if x == "t":
            rounded(a, n)
        else:
            act(R(a, 0, n), R(a, 0, n), bias=M)
        act(out, R(a, 0, n), bias=-M)

    def floor_d(k, j, x):
        whole(nat("Db", 0, named(k), j), "PF%d" % j, named(k) * CW[j], x)

    def bwd(k, j, lo=1, hi=None):
        nn = named(k)
        hi = nn + 1 if hi is None else hi
        for t in range(lo, hi):
            for s in range(t):
                mm(pr(j, s, 1), dg(CDG[(s, t)]), nat("Db", t - 1, 1, j))
        b = min(hi, nn)
        if b > lo:
            mm(pr(j, lo, b - lo), A("I16"), nat("Db", lo - 1, b - lo, j))

    def fin(k, j, x):
        nn = named(k)
        whole(chunk("Q", k, j, 0, nn), "PR%d" % j, nn * CW[j], x)
        for a, b in WRITES[k]:
            if b == j + 1 and k in APART and a >= 2:
                x, n = nn * (CP[a] - CP[2]), nn * (CP[b] - CP[a])
                send(R("L%de" % k, x, n), R("Q%de" % k, x, n), "arr%d%d" % (k, a))
            elif b == j + 1:
                (p, i), at = CT[j], slice(CT[a][1], CT[j][1] + 1)
                send(A("L%d%s" % (k, p), at, ALL), A("Q%d%s" % (k, p), at, slice(0, nn * CW[j])), "arr%d%d" % (k, a))

    def newest(k, bk):
        nn = named(k)
        opened(bk, 512)
        was = {1: A("N", 0, ALL), 4: A("N", 1, ALL)}
        now = {3: A("me"), 6: A("yrb", 3, ALL)}
        for x in APART:
            now[x] = was[x + 1] = A("N", 2 + x // 3, ALL)
        for x, a, n in [(was[k], 0, 512)] if k in was else parts("Q%d" % (k - 1), nn):
            mm(R(bk, a, n), A("Ib"), x)
        mm(A(bk), A("I16"), A("Db", nn - 1, ALL))
        rounded(bk, 512)
        if k == 6:
            return lambda: act(now[k], A(bk), bias=-M)
        if k in now:
            act(now[k], A(bk), bias=-M)
            return None
        (x, a, n), rest = parts("Q%d" % k, nn)[0], parts("Q%d" % k, nn)[1:]
        act(x, R(bk, a, n), bias=-M)
        if OPT.get("nw", "a") == "a":
            for x, a, n in rest:
                act(x, R(bk, a, n), bias=-M)
            return None
        return lambda: [ts(x, R(bk, a, n), -M, None, AL.add) for x, a, n in rest]

    def home(k, a, b, by):
        for s in range(named(k)):
            if by[s] != "-":
                for x, p, n in parts("Q%d" % k, s, a, b):
                    on(by[s])(R("W", s * 512 + p, n), x)

    def away(k, a, b, by):
        for s in range(named(k)):
            for x, p, n in parts("L%d" % k, s, a, b):
                on(by[s])(R("W", AWAY + s * 512 + p, n), x,
                          ext=tuple("arr%d%d" % (k, u) for u, v in WRITES[k] if u < b and v > a))

    def sweep(k, ahead=(), mid=(), more=()):
        nn = named(k)
        step = {"g": lambda j: gather(k, j, nn + 1), "c": lambda j: (clip(j, nn + 1), fwd(k, j), c0(j)),
                "f": lambda j: floor_d(k, j, "v"), "F": lambda j: floor_d(k, j, "s"), "M": lambda j: floor_d(k, j, "t"),
                "b": lambda j: bwd(k, j), "o": lambda j: fin(k, j, "t"), "v": lambda j: fin(k, j, "v"),
                "G": lambda j: gather_a(k, j), "C": lambda j: clip_a(k, j), "w": lambda j: (fwd(k, j), c0(j)),
                "d": lambda j: clip(j, nn + 1), "T": lambda j: less(k, j), "L": lambda j: load_r(k, j),
                "X": lambda j: prepare(k, "F%d f%d" % (j, j)), "x": lambda j: fill_f(k, j),
                "s": lambda j: fin(k, j, "s"), "m": lambda j: run(mid), "p": lambda j: run(more),
                "q": lambda s: [tt(A("yrb", s, slice(a, a + n)), x, y, AL.add)
                                for (x, a, n), (y, _, _) in zip(parts("Q5", s, 0, 2), parts("Q6", s, 0, 2))]}
        run(ahead)
        for x in OPT.get("s%d" % k, ORDER[k]).split():
            step[x[0]](int(x[1]))

    ORDER = {2: "G1 x2 g0 m0 d0 C1 w0 M0 w1 X3 M1 b0 o0 p0 g2 c2 b1 o1 g3 c3 f2 f3 b2 v2 b3 v3",
             3: "G1 m0 x2 g0 d0 C1 w0 M0 w1 X3 M1 b0 o0 L3 g2 c2 b1 o1 p0 g3 c3 f2 f3 b2 v2 b3 v3",
             5: "G1 x2 g0 d0 C1 w0 M0 w1 M1 b0 o0 X3 g2 c2 b1 g3 c3 f2 v1 b2 f3 b3 v2 v3"}
    ORDER[6] = ORDER[5].replace("g0", "m0 g0") + " q0 q1 q2"

    def between(k, first, plan, second=()):
        prepare(k + 1, "F0 f0")
        rest = newest(k, "PF3")
        early, late = plan.split("|")
        prepare(k + 1, early)
        update(k, list(first) + [rest or (lambda: None), lambda: prepare(k + 1, late)], second)

    UPDATE = {k: "h02vv- * h24vvv h02--a a02vvv a23vav a34vav" for k in range(1, 6)}
    for k in APART:
        UPDATE[k] = "h02vv- * h24vv- h04--a a02vvv a24vav"
    UPDATE[3] = "h04vv- a02vvv * a23vvv a34vav"

    UPDATE[1] = "h02vv- * h24vvv a02vvv + a23vav a34vav"

    def update(k, first, second=()):
        for x in OPT.get("h%d" % k, UPDATE[k]).split():
            if x in "*+":
                run(first if x == "*" else second)
            else:
                (home if x[0] == "h" else away)(k, int(x[1]), int(x[2]), x[3:])

    def counts(m, bk):
        for i, (best, later) in enumerate([(0, 1), (0, 2), (3, 2)][:m]):
            mm(R(bk, 32 * i, 32), A("I9"), R("vv", 32 * best, 32), i == 0)
            mm(R(bk, 32 * i, 32), A("I99"), R("vv", 32 * later, 32))
        for i in range(16):
            mm(R(bk, 0, 32 * m), R("Z", 15 - i, 128), R("lt", i, 512 * m - i, 16))

    def old_at(j, s):
        if BYSLOT:
            return R("PF%d" % s, CP[j], CW[j])
        bk = [b for b in OLD if j in OLD[b]][0]
        return R(bk, s * old_n(bk) + CP[j] - CP[OLD[bk][0]], CW[j])

    def old_n(bk):
        return H if BYSLOT else sum(CW[j] for j in OLD[bk])

    def old_of(name, bk):
        if BYSLOT:
            return A(name, int(bk[2]), ALL)
        return A(name, slice(0, 2), slice(CP[OLD[bk][0]], CP[OLD[bk][-1] + 1]))

    def old_fill(bk):
        opened(bk, 2 * old_n(bk))
        act(R(bk, 0, 2 * old_n(bk)), old_of("KF", bk))

    def old_fwd(k, j):
        nn = named(k)
        a, n, bk = [x for x in NEW[k] if x[0] <= CP[j] < x[0] + x[1]][0]
        clip(j, nn)
        for s in range(1, nn):
            to = R("PF0", CP[j], CW[j]) if k == 1 else old_at(j, s - 1)
            for t in range(s + 1):
                mm(to, A("Ib") if t == s else dg(ADG[(s, t)]), nat("tn", t, 1, j))
        for t in range(nn):
            mm(R(bk, CP[j] - a, CW[j]), dg(ADG[(nn, t)]), nat("tn", t, 1, j))

    def load_first(s, pieces):
        for a, n, bk in pieces:
            opened(bk, n)
            for t in range(s + 1):
                mm(R(bk, 0, n), A("Ib") if t == s else dg(ADG[(s, t)]), R("ocb", t * 512 + a, n))

    def old_floor(bk):
        whole(old_of("Db", bk), bk, 2 * old_n(bk), "t")

    def old_bwd(k, j):
        c0(j)
        bwd(k, j, 1, named(k))

    def new_gather(k, h):
        nn, (a, n, bk) = named(k), NEW[k][h]
        tt(R("tb", 1536 + a, n), window(k, k == 4) + R("oY", nn * 32 + a // 16, n // 16),
           A("N", k // 3, slice(a, a + n)), AL.subtract)

    def new_fwd(k, h):
        nn, (a, n, bk) = named(k), NEW[k][h]
        ts(A("tn", nn, slice(a, a + n)), R("tb", 1536 + a, n), 256.0, -256.0, AL.min, AL.max)
        mm(R(bk, 0, n), A("Ib"), A("tn", nn, slice(a, a + n)))

    def new_floor(k, h, x):
        nn, (a, n, bk) = named(k), NEW[k][h]
        whole(A("Db", nn - 1, slice(a, a + n)), bk, n, x)

    def first_end(k):
        step = {"g": lambda h: new_gather(k, h), "c": lambda h: new_fwd(k, h),
                "f": lambda h: new_floor(k, h, "v"), "M": lambda h: new_floor(k, h, "t"),
                "O": lambda j: oc0(k, j), "B": lambda j: old_bwd(k, j), "b": lambda j: bwd(k, j, named(k)),
                "o": lambda j: fin(k, j, "t"), "v": lambda j: fin(k, j, "v")}
        for x in OPT.get("e%d" % k, END[k]).split():
            step[x[0]](int(x[1]))

    END = {1: "g0 c0 B0 g1 f0 b0 o0 c1 B1 B2 B3 f1 b1 v1 b2 o2 b3 v3",
           4: "g0 c0 O3 B3 g1 f0 b0 o0 c1 O2 B2 f1 b1 v1 b2 o2 b3 v3"}

    def far(k, c, bk):
        act(R("cq", c * 512, 512), window(k) + R("oC", c * 32, 32), scale=-1.0)
        mm(A(bk), A("Ib"), R("cq", c * 512, 512))

    act(R16("LH", 0, 512), R16("LQ", 0, 512), bias=-1536.0)
    first_write(0, "v")
    for b in range(2):
        for q in range(16):
            mm(R("PF%d" % b, q, 512 - q, 16), R16("E", q // 8 * 128, 128), R16("LH", q % 8 * 64 + b * 32, 32), q == 0)
    st = lookup_steps(A("LV"), 0, 2)
    run(st)
    first_write(1, "a")
    act(R("Lrow", 0, 512), A("PF0"))
    cp(R("Lrow", 512, 512), A("PF1"))
    act(R("AC", 0, 6), R("mub", 0, 6), scale=0.5)
    cp(R("oY", 0, 64), A("LV"))
    act(R("crow", 512, 512), A("Lrow") + R("oG", 32, 32))
    cp(R("crow", 0, 512), A("Lrow") + R("oG", 0, 32))
    first_write(2, "v")
    iota(R("W", 1024, 1024), [[0, 1024]], 0, 0, True)
    to_list(0, 2, "PR3")
    for d in (0, 1, 3):
        diag(d)
    by_chunk(0)
    by_chunk(1)
    ts(R("qq", 96, 32), rows("LV", 0, 1), AWAY + 511, None, AL.bitwise_and)
    cs = cand_steps(0, 2, "PR3")
    cs[0]()
    for x, a, n in parts("Q0", 1):
        cp(x, R("X0", 512 + a, n))
    cs[1]()
    for x, a, n in parts("Q0", 0):
        cp(x, R("X0", a, n))
    run(cs[2:])
    later = new_rating(0, "PR2")
    act(R("W", 0, 1024), A("X0"))
    mm(A("PF1"), A("Ib"), me(0), True)
    load_first(1, [(0, 512, "PF0")])
    load_first(2, NEW[1])
    kf = outcomes(1, "PR0")
    tt(R("s1", 0, 32), R("qq", 0, 32), R("qq", 96, 32), AL.subtract)
    tt(R("s2", 0, 32), R("s1", 0, 32), R("vv", 0, 32), AL.mult)

    first_landed(0, "v")
    later()
    first_landed(1, "a")
    first_landed(2, "v")
    far(1, 0, "PF1")
    tt(R("tc", 512, 512), window(1) + R("oC", 32, 32), me(0), AL.subtract)
    act(R("ds", 0, 512), R("tc", 512, 512), AF.Abs)
    act(A("PF1"), A("PF1"), AF.Abs)
    kf()
    outcomes(2, "PR1")()
    for d in (6, 7, 9):
        diag(d)
    gather(1, 0, 2); gather(1, 1, 2); old_fwd(1, 0)
    tt(R("qq", 0, 32), R("s2", 0, 32), R("qq", 96, 32), AL.add)
    old_fwd(1, 1)
    tt(R("DD", 64, 32), R("qq", 32, 32), R("qq", 0, 32), AL.subtract)
    tt(R("lt", 0, 512), R("ds", 0, 512), A("PF1"), AL.is_lt)
    counts(1, "PR3")
    prepare(1, "L2 L0")
    gather(1, 2, 2); gather(1, 3, 2)
    ts(R("uu", 0, 32), R("PR3", 0, 32), 99.0, None, AL.is_ge)
    old_fwd(1, 2)
    tt(R("s1", 0, 32), R("uu", 0, 32), R("DD", 64, 32), AL.mult)
    old_fwd(1, 3)
    tt(R("s2", 0, 32), R("s1", 0, 32), R("qq", 0, 32), AL.add)
    whole(A("Db", 0, ALL), "PF0", 512, "t")
    prepare(1, "L1 L3")
    ts(R("oY", 64, 32), R("s2", 0, 32), 512.0, None, AL.add)
    act(R("yob", 0, 32), R("s2", 0, 32), bias=512.0)
    first_end(1)
    between(1, lookup_steps(R("yob", 0, 32), 2, 3)
            + [lambda: by_chunk(2)], OPT.get("p1", "F1 f1 L0 F2 L1 L2 | T1"),
            [lambda: on(OPT.get("cr", "va")[0])(R("crow", 0, H), A("Lrow") + R("oG", 64, 16)),
             lambda: on(OPT.get("cr", "va")[1])(R("crow", H, H), A("Lrow") + R("oG", 80, 16)),
             lambda: to_list(2, 3, "PR3")])
    cs = cand_steps(2, 3, "PR3")
    sweep(2, (), cs[:1], [lambda: prepare(2, "L3")])
    for d in (2, 4, 5):
        diag(d)
    between(2, cs[1:] + [lambda: tt(R("DD", 0, 32), R("qq", 64, 32), R("qq", 0, 32), AL.subtract),
                         lambda: tt(R("DD", 32, 32), R("qq", 64, 32), R("qq", 32, 32), AL.subtract)],
            OPT.get("p2", "F1 f1 F2 L0 L1 L2 | T1"))
    kf = outcomes(3, "PF3")
    sweep(3, (), [kf], [lambda d=d: diag(d) for d in (8, 10, 11)])

    banks = list(OLD)
    old_fill(banks[0])
    newest(3, "PR0")
    send(A("Lme"), A("me"), "arrme")
    old_fill(banks[1])
    new_rating(3, "PR1")()
    mm(A("PR2"), A("Ib"), A("me"), True)
    mm(A("PR3"), A("Ib"), A("me"), True)
    for bk in banks[2:]:
        old_fill(bk)
    load_first(3, NEW[4])
    update(3, [lambda: [cp(x, R("me", a, n)) for x, a, n in parts("Q3", 2)]])
    prepare(4, "L0")
    pick = [lambda: tt(A("s1"), R("uu", 32, 64), R("DD", 0, 64), AL.mult),
            lambda: ts(R("uu", 0, 32), R("PR2", 0, 32), 99.0, None, AL.is_lt),
            lambda: tt(A("s2"), A("s1"), R("qq", 0, 64), AL.add),
            lambda: ts(R("uu", 32, 32), R("PR2", 0, 32), 99.0, None, AL.is_ge),
            lambda: tt(A("s4"), A("s2"), R("uu", 0, 64), AL.mult),
            lambda: tt(R("s3", 32, 32), R("s4", 0, 32), R("s4", 32, 32), AL.add)]
    far(4, 0, "PR2")
    far(4, 1, "PR3")
    prepare(4, "L1")
    tt(R("tc", 1024, 512), window(4) + R("oC", 64, 32), A("me"), AL.subtract)
    act(R("ds", 512, 512), R("tc", 1024, 512), AF.Abs)
    act(A("PR2"), A("PR2"), AF.Abs)
    act(R("ds", 0, 512), A("PR3"), AF.Abs)
    act(A("PR3"), R("ds", 0, 512))
    gather(4, 0, 3); gather(4, 1, 3); old_fwd(4, 0); old_fwd(4, 1)
    for bk in [] if BYSLOT else banks[:-1]:
        old_floor(bk)
    gather(4, 2, 3)
    tt(R("lt", 512, 512), R("ds", 512, 512), A("PR2"), AL.is_lt)
    old_fwd(4, 2)
    tt(R("lt", 0, 512), R("ds", 0, 512), A("PR2"), AL.is_lt)
    tt(R("lt", 1024, 512), R("ds", 512, 512), A("PR3"), AL.is_lt)
    counts(3, "PR2")
    act(R("W", AWAY + 1024, 512), A("Lme"), ext=("arrme",))
    gather(4, 3, 3)
    act(R("W", 1024, 512), A("me"))
    old_fwd(4, 3)
    for bk in banks if BYSLOT else banks[-1:]:
        old_floor(bk)
    prepare(4, "R3 r3")
    old_bwd(4, 0)
    ts(R("uu", 32, 64), R("PR2", 32, 64), 99.0, None, AL.is_ge)
    old_bwd(4, 1)
    run(pick[:4])
    prepare(4, "R2 r2")
    run(pick[4:])
    ts(R("oY", 96, 32), R("s3", 32, 32), 1024.0, None, AL.add)
    first_end(4)
    plan = OPT.get("plan", "F1 f1 L0 F2 L1 L2 | T1 L3")
    between(4, [lambda: by_chunk(3)], plan)
    sweep(5)
    between(5, [], plan)
    sweep(6, (), [lambda: act(R("yob", 32, 32), R("s3", 32, 32), bias=1024.0), lambda: act(A("If"), A("Ib")),
                  lambda: dma("s", T.yo[:], A("yob"), "d_yo")])

    E = CP[2]
    for k in (5, 6):
        for s in range(3):
            for x, a, n in parts("Q%d" % k, s, 2, 4):
                mm(R("PF%d" % s, a - E, n), A("Ib"), x, k == 5 and a == E)
    for s in range(3):
        act(A("yrb", s, slice(E, 512)), R("PF%d" % s, 0, 512 - E))
    for s in range(3):
        cp(R("W", s * 512 + E, 512 - E), R("PF%d" % s, 0, 512 - E))
    for s in range(3):
        act(R("W", s * 512, E), A("yrb", s, slice(0, E)))
    later = newest(6, "PF3")
    la = OPT.get("la", "aaa vvv vvv").split()
    for s in range(3):
        for k in (5, 6):
            for x, a, n in parts("L%d" % k, s, 0, 2):
                mm(R("PR%d" % s, a, n), A("Ib"), x, k == 5 and a == 0, ext=("arr60", "arr61") if k == 6 else ())
        on(la[0][s])(R("W", AWAY + s * 512, E), R("PR%d" % s, 0, E))
    later()
    for j, bk in ((2, "PF0"), (3, "PR3")):
        mm(R(bk, 0, 3 * CW[j]), A("Ib"), chunk("L", 5, j, 0, 3), True)
    for j, bk in ((2, "PF0"), (3, "PR3")):
        mm(R(bk, 0, 3 * CW[j]), A("Ib"), chunk("L", 6, j, 0, 3), ext=("arr6%d" % j,))
        for s in range(3):
            on(la[j - 1][s])(R("W", AWAY + s * 512 + CP[j], CW[j]), R(bk, s * CW[j], CW[j]))
    dma("s", T.yr[:], A("yrb"), "d_yr", ext=("arr63",))

    def z_of(h, s):
        a = h * H
        tt(R("tc", (4 * h + s) * H, H), window(7) + R("oY", s * 32 + a // 16, H // 16), A("yrb", s, slice(a, a + H)),
           AL.subtract)
        if h == 0 and s < 2:
            act(R("PR0", s * H, H), R("tc", s * H, H), AF.Sigmoid, scale=-1.0 / 256)
        elif s % 2:
            act(A("PR%d" % (2 * h + s // 2)), R("tc", (4 * h + s - 1) * H, 2 * H), AF.Sigmoid, scale=-1.0 / 256)

    def weigh(out, h, s):
        tt(out, A("PR%d" % (2 * h + s // 2)), A("stk", slice(s, s + 2), slice(h * H, h * H + H)), AL.mult)

    for h in range(2):
        for s in range(4):
            z_of(h, s)
    for s in (0, 2):
        weigh(R("prod", s * H, 2 * H), 0, s)
        mm(R("PF0", 0, H), A("If"), R("prod", s * H, H), s == 0)
        mm(R("PF0", 0, H), A("If"), R("prod", (s + 1) * H, H))
    act(R("ysb", 0, H), R("PF0", 0, H))
    dma("a", T.y[:, 0:H], R("ysb", 0, H), "d_y0")
    weigh(R("prod", 4 * H, 2 * H), 1, 0)
    weigh(A("PR3"), 1, 2)
    tt(R("ds", 0, H), R("PR3", 0, H), R("prod", 4 * H, H), AL.add)
    tt(R("PR3", H, H), R("PR3", H, H), R("prod", 5 * H, H), AL.add)
    tt(R("ysb", H, H), R("PR3", H, H), R("ds", 0, H), AL.add)
    dma("s", T.y[:, H:512], R("ysb", H, H), "d_y1")
    _emit(g, T, ops, totals)
